import numpy as np
import ml_dtypes


def mxq(x, axis, fmt="e4m3"):
    dtype, down = {"e4m3": (ml_dtypes.float8_e4m3fn, 7), "e5m2": (ml_dtypes.float8_e5m2, 14)}[fmt]
    v = np.moveaxis(np.asarray(x, np.float32).astype(ml_dtypes.bfloat16).astype(np.float64), axis, -1)
    blocks = v.reshape(v.shape[:-1] + (-1, 32))
    amax = np.abs(blocks).max(-1, keepdims=True)
    byte = np.maximum(np.where(amax > 0, np.frexp(amax)[1] - 1 + 127, 0) - down, 1)
    scale = np.exp2(byte - 127.0)
    codes = (blocks / scale).astype(np.float32).astype(dtype).astype(np.float64)
    return np.moveaxis((codes * scale).reshape(v.shape), -1, axis)


WIDE = False


def mx_kscale(k):
    if not WIDE:
        return np.ones(k)
    levels = np.array([10, -10, 5, -5, 0])
    if k % 512:
        return np.exp2(np.random.permutation(np.resize(levels, k // 32))).repeat(32)
    a = np.empty((k // 512, 16))
    for p in range(k // 512):
        a[p, :8] = np.random.permutation(np.resize(levels, 8))
        for g in range(8):
            far = levels[np.abs(levels - a[p, g]) >= 10]
            a[p, g + 8] = far[np.random.randint(len(far))]
    return np.exp2(a.ravel()).repeat(32)


def f64(x):
    return np.asarray(x).astype(np.float64)


def striped(idx):
    return np.tile(idx.reshape(-1, 16).T, (8, 1)).astype(np.uint16)


def unstriped(offs):
    return offs[:16].T.reshape(-1).astype(np.int64)


E2M1 = np.array([0.0, 0.5, 1.0, 1.5, 2.0, 3.0, 4.0, 6.0, -0.0, -0.5, -1.0, -1.5, -2.0, -3.0, -4.0, -6.0])


def pack_weight(w, fmt):
    k, n = w.shape
    w = f64(np.asarray(w, np.float32).astype(ml_dtypes.bfloat16)).reshape(k // 32, 32, n)
    amax = np.abs(w).max(1)
    if fmt == "e4m3":
        byte = np.frexp(amax)[1] - 1 + 127 - 7
    else:
        mant, ex = np.frexp(amax / 6.0)
        byte = np.where(mant > 0.5, ex, ex - 1) + 127
    byte = np.clip(np.where(amax > 0, byte, 1), 1, 254)
    scaled = (w * np.exp2(127.0 - byte)[:, None, :]).reshape(k, n).astype(np.float32)
    by_word = np.ascontiguousarray(scaled.reshape(k // 512, 128, 4, n).transpose(0, 1, 3, 2))
    if fmt == "e4m3":
        words = by_word.astype(ml_dtypes.float8_e4m3fn).view(np.uint8)
    else:
        c = by_word.astype(ml_dtypes.float4_e2m1fn).view(np.uint8) & 0xF
        words = (c[..., 0::2] | (c[..., 1::2] << 4)).reshape(k // 512, 128, 2 * n)
    return np.ascontiguousarray(words), np.ascontiguousarray(byte.astype(np.uint8).reshape(k // 512, 16, n))


def unpack_weight(words, scales, fmt):
    g, _, n = scales.shape
    words = np.ascontiguousarray(words).reshape(g, 128, n, -1)
    if fmt == "e4m3":
        vals = words.view(ml_dtypes.float8_e4m3fn).astype(np.float64)
    else:
        nib = np.empty((g, 128, n, 4), np.uint8)
        nib[..., 0::2] = words & 0xF
        nib[..., 1::2] = words >> 4
        vals = E2M1[nib]
    vals = vals * np.repeat(np.exp2(scales.astype(np.float64) - 127.0), 8, axis=1)[..., None]
    return vals.transpose(0, 1, 3, 2).reshape(g * 512, n)


def gelu(v):
    return 0.5 * v * (1.0 + np.tanh(np.sqrt(2.0 / np.pi) * (v + 0.044715 * v**3)))


K, T, S, H, N = 1024, 4096, 1024, 1024, 256

def setup_inputs():
    n = np.random.standard_normal
    s = mx_kscale(K)[:, None]
    u = mx_kscale(H)[:, None]
    tab_words, tab_scales = pack_weight(n((K, T)) * s, "e4m3")
    wc_words, wc_scales = pack_weight(0.6 * n((K, H)) / np.sqrt(K) / s, "e2m1")
    wd_words, wd_scales = pack_weight(0.5 * n((K, N)) / np.sqrt(K) / s, "e4m3")
    return {
        "tab_words": tab_words, "tab_scales": tab_scales,
        "offs": striped(np.random.permutation(T)[:S]),
        "wa": (0.6 * n((K, H)) / np.sqrt(K) / s).astype(np.float32),
        "wc_words": wc_words, "wc_scales": wc_scales,
        "wd_words": wd_words, "wd_scales": wd_scales,
        "i0": (np.exp(0.3 * n(H)) * u[:, 0]).astype(np.float32),
        "w2": (n((H, N)) / np.sqrt(H) / u).astype(np.float32),
        "bo": (0.5 * n(N)).astype(np.float32),
    }

def reference(tab_words, tab_scales, offs, wa, wc_words, wc_scales, wd_words, wd_scales, i0, w2, bo):
    v = unpack_weight(tab_words, tab_scales, "e4m3")[:, unstriped(offs)]
    wc = unpack_weight(wc_words, wc_scales, "e2m1")
    wd = unpack_weight(wd_words, wd_scales, "e4m3")
    qa = mxq(f64(wa), 0, "e4m3")
    q2 = mxq(f64(w2), 0, "e4m3")
    fa = qa.T @ v
    fc = wc.T @ v
    h = f64(i0)[:, None] * (np.exp(fa) - np.exp(fc))
    qh = mxq(h, 0, "e4m3")
    y = q2.T @ qh + wd.T @ v
    return y + f64(bo)[:, None]

@@ -1,0 +1,336 @@
+import math
+from contextlib import ExitStack
+
+import concourse.mybir as mybir
+
+K, T, S, H, N = 1024, 4096, 1024, 1024, 256
+FLOPS = 2 * S * (2 * K * H + H * N + K * N)
+
+F32 = mybir.dt.float32
+BF16 = mybir.dt.bfloat16
+I32 = mybir.dt.int32
+U32 = mybir.dt.uint32
+U16 = mybir.dt.uint16
+U8 = mybir.dt.uint8
+FP8X4 = mybir.dt.float8_e4m3fn_x4
+FP4X4 = mybir.dt.float4_e2m1fn_x4
+ALU = mybir.AluOpType
+ACT = mybir.ActivationFunctionType
+
+P = 128
+W = 512
+HALVES = S // W
+KB = 1024
+
+
+def tile_list_electrode_node_currents_kernel(
+    tc, tab_words, tab_scales, offs, wa, wc_words, wc_scales, wd_words, wd_scales, i0, w2, bo, out
+):
+    nc = tc.nc
+    with ExitStack() as ctx:
+        keep = ctx.enter_context(tc.tile_pool(name="keep", bufs=1))
+        reuse = ctx.enter_context(tc.tile_pool(name="reuse", bufs=1))
+        psum = ctx.enter_context(tc.psum_pool(name="psum", bufs=1))
+        banks = [psum.tile([P, W], F32, name="bank%d" % n) for n in range(8)]
+
+        def held(name, shape, dtype):
+            return keep.tile(shape, dtype, name=name, align_bytes=64)
+
+        def placed(name, shape, dtype, at):
+            return reuse.tile(shape, dtype, name=name, align_bytes=64, offset=at)
+
+        offsets = keep.tile([P, S // 16], U16, name="offsets")
+        nc.sync.dma_start(offsets[:], offs)
+
+        lane = placed("lane", [P, 4], I32, 0)
+        nc.gpsimd.iota(lane[:], [[-1, 4]], base=4, channel_multiplier=1)
+        i0_runs = held("i0_runs", [P, 2, 16], F32)
+        i0_by_m = i0.rearrange("(b m x) -> b m x", b=2, x=16)
+        for b in range(2):
+            nc.gpsimd.dma_start(out=i0_runs[:, b, :], in_=i0_by_m[b].unsqueeze(1).to_broadcast([32, 4, 16]))
+
+        wc_raw = placed("wc_raw", [P, 2, 2 * H], U8, 32 * KB)
+        nc.sync.dma_start(out=wc_raw[:].bitcast(I32), in_=wc_words.rearrange("a p x -> p a x").bitcast(I32))
+
+        table_scales = placed("table_scales", [P, T], U8, 40 * KB)
+        nc.vector.memset(table_scales[:].bitcast(I32), 0)
+        wc_scales_raw = held("wc_scales_raw", [P, 2, H], U8)
+        nc.vector.memset(wc_scales_raw[:].bitcast(I32), 0)
+        lane_mod = placed("lane_mod", [P, 4], I32, 16 * KB)
+        nc.vector.tensor_scalar(lane_mod[:], lane[:], 3, None, ALU.bitwise_and)
+        own = held("own", [P, 4], F32)
+        nc.vector.tensor_scalar(own[:], lane_mod[:], 0.0, None, ALU.is_equal)
+        for q in range(4):
+            nc.sync.dma_start(
+                out=table_scales[32 * q : 32 * q + 8, :].bitcast(I32),
+                in_=tab_scales[:, 4 * q : 4 * q + 4, :].bitcast(I32),
+            )
+
+        def load_scale_rows(queue, plane, src):
+            for q in range(4):
+                queue.dma_start(
+                    out=plane[32 * q : 32 * q + 4, :, :].bitcast(I32),
+                    in_=src[:, 4 * q : 4 * q + 4, :].rearrange("a r n -> r a n").bitcast(I32),
+                )
+
+        table = [placed("table%d" % a, [P, T], I32, 16 * KB * a) for a in range(2)]
+
+        def load_table(a):
+            nc.sync.dma_start(out=table[a][:], in_=tab_words[a].rearrange("p t i -> p (t i)").bitcast(I32))
+
+        load_table(0)
+        load_scale_rows(nc.sync, wc_scales_raw, wc_scales)
+        load_table(1)
+        v_scales1 = held("v_scales1", [P, S], U8)
+        nc.vector.memset(v_scales1[:].bitcast(I32), 0)
+        wd_sc = held("wd_sc", [P, 2, N], U8)
+        nc.vector.memset(wd_sc[:].bitcast(I32), 0)
+        load_scale_rows(nc.gpsimd, wd_sc, wd_scales)
+        bo_sb = held("bo_sb", [P, 2], F32)
+        with nc.allow_non_contiguous_dma(reason="one bias a partition"):
+            nc.gpsimd.dma_start(out=bo_sb[:], in_=bo.rearrange("(c p) -> p c", p=P))
+
+        wc_codes = held("wc_codes", [P, 4, 4, 256], U8)
+        nc.vector.tensor_copy(
+            out=wc_codes[:].bitcast(I32).rearrange("p g t (m e) -> p g t m e", e=2),
+            in_=wc_raw[:].bitcast(I32).rearrange("p a (b m t e) -> p (a b) t m e", b=2, t=4, e=2),
+        )
+
+        v_scales0 = held("v_scales0", [P, S], U8)
+        nc.vector.tensor_copy(v_scales0[:], table_scales[:].indirect(offsets[:]))
+        nc.scalar.dma_start(out=v_scales1[0:100, :].bitcast(I32), in_=v_scales0[4:104, :].bitcast(I32))
+        v_scales = [v_scales0, v_scales1]
+
+        i0_masked = held("i0_masked", [P, 8, 4], F32)
+        nc.vector.tensor_tensor(
+            i0_masked[:],
+            i0_runs[:].rearrange("p b (t u) -> p (b t) u", u=4),
+            own[:].unsqueeze(1).to_broadcast([P, 8, 4]),
+            ALU.mult,
+        )
+        i0_sb = held("i0_sb", [P, 8], F32)
+        nc.vector.tensor_reduce(i0_sb[:], i0_masked[:], mybir.AxisListType.X, ALU.add)
+        bits = i0_sb[:].bitcast(I32)
+        mant = held("mant", [P, 8], I32)
+        nc.vector.tensor_scalar(mant[:], bits, 0x007FFFFF, 0x3F800000, ALU.bitwise_and, ALU.bitwise_or)
+        expo = held("expo", [P, 8], I32)
+        nc.vector.tensor_scalar(expo[:], bits, 23, 0xFF, ALU.logical_shift_right, ALU.bitwise_and)
+        ln_mant = held("ln_mant", [P, 8], F32)
+        nc.scalar.activation(ln_mant[:], mant[:].bitcast(F32), ACT.Ln)
+        sgn = held("sgn", [P, 8], F32)
+        nc.scalar.activation(sgn[:], i0_sb[:], ACT.Sign)
+        warm = held("warm", [P, 8], F32)
+        nc.scalar.activation(warm[:], ln_mant[:], ACT.Exp)
+        ln_pow = held("ln_pow", [P, 8], F32)
+        nc.vector.tensor_scalar(ln_pow[:], expo[:], 127.0, math.log(2.0), ALU.subtract, ALU.mult)
+
+        v_codes = [held("v_codes%d" % a, [P, S], U32) for a in range(2)]
+        nc.vector.tensor_copy(v_codes[0][:], table[0][:].bitcast(U32).indirect(offsets[:]))
+
+        wc_sc = held("wc_sc", [P, 4, 4, 128], U8)
+        nc.vector.tensor_copy(
+            out=wc_sc[:].bitcast(I32),
+            in_=wc_scales_raw[:].bitcast(I32).rearrange("p a (b m t) -> p (a b) t m", b=2, t=4),
+        )
+        ln_i0 = held("ln_i0", [P, 8], F32)
+        nc.vector.tensor_tensor(ln_i0[:], ln_mant[:], ln_pow[:], ALU.add)
+
+        for j in range(HALVES):
+            nc.vector.tensor_copy(
+                v_codes[1][:, j * W : (j + 1) * W],
+                table[1][:].bitcast(U32).indirect(offsets[:, j * W // 16 : (j + 1) * W // 16]),
+            )
+
+        wa_place = {(0, 0): 32 * KB, (1, 0): 40 * KB, (0, 1): 0, (1, 1): 16 * KB}
+        wa_raw = {}
+
+        def load_wa(a, b):
+            raw = placed("wa_raw%d%d" % (a, b), [P, 4, W], F32, wa_place[(a, b)])
+            nc.sync.dma_start(
+                out=raw[:],
+                in_=wa[W * a : W * (a + 1), W * b : W * (b + 1)].rearrange("(p j) c -> p j c", j=4),
+            )
+            wa_raw[(a, b)] = raw
+
+        load_wa(0, 0)
+        load_wa(1, 0)
+        load_wa(0, 1)
+        wd_codes = placed("wd_codes", [P, 2, N], I32, 8 * KB)
+        nc.sync.dma_start(out=wd_codes[:], in_=wd_words.rearrange("a p c i -> p a (c i)").bitcast(I32))
+        load_wa(1, 1)
+        w2_raw = placed("w2_raw", [P, 2, 4, N], F32, 24 * KB)
+        w2_rows = w2.rearrange("(b m t u) n -> b t m u n", b=2, t=4, u=4)
+        for b in range(2):
+            for t in range(4):
+                nc.sync.dma_start(out=w2_raw[:, b, t, :], in_=w2_rows[b, t])
+
+        wa_codes = {}
+        wa_sc = {}
+
+        def quantise_wa(a, b):
+            grouped = held("wa_bf%d%d" % (a, b), [P, W, 4], BF16)
+            nc.vector.tensor_copy(
+                out=grouped[:].rearrange("p (t m u) j -> p t m j u", t=4, u=4),
+                in_=wa_raw[(a, b)][:].rearrange("p j (m t u) -> p t m j u", t=4, u=4),
+            )
+            wa_codes[(a, b)] = held("wa_codes%d%d" % (a, b), [P, W], U32)
+            wa_sc[(a, b)] = held("wa_sc%d%d" % (a, b), [P, W], U8)
+            nc.vector.quantize_mx(
+                out=wa_codes[(a, b)][:].bitcast(FP8X4),
+                scales=wa_sc[(a, b)][:],
+                in_=grouped[:].rearrange("p c j -> p (c j)"),
+            )
+
+        rates = {}
+        for kind in "ac":
+            for b in range(2):
+                for j in range(HALVES):
+                    rates[(kind, b, j)] = held("rate_%s%d%d" % (kind, b, j), [P, 4, W], F32)
+
+        def exponent_pass(bank, kind, b, j, t, a):
+            cols = slice(j * W, (j + 1) * W)
+            if kind == "a":
+                lhs = wa_codes[(a, b)][:, P * t : P * (t + 1)].bitcast(FP8X4)
+                lhs_sc = wa_sc[(a, b)][:, P * t : P * (t + 1)]
+            else:
+                lhs = wc_codes[:, 2 * a + b, t, :].bitcast(FP4X4)
+                lhs_sc = wc_sc[:, 2 * a + b, t, :]
+            nc.tensor.matmul_mx(
+                out=bank[:],
+                lhsT=lhs,
+                lhsT_scale=lhs_sc,
+                rhs=v_codes[a][:, cols].bitcast(FP8X4),
+                rhs_scale=v_scales[a][:, cols],
+                start=(a == 0),
+                stop=(a == 1),
+            )
+
+        def exponential(bank, kind, b, j, t):
+            nc.scalar.activation(
+                rates[(kind, b, j)][:, t, :], bank[:], ACT.Exp, bias=ln_i0[:, 4 * b + t : 4 * b + t + 1]
+            )
+
+        first = [("c", 0, j, t) for j in range(HALVES) for t in range(4)]
+        for n, g in enumerate(first):
+            exponent_pass(banks[n], *g, 0)
+        for n, g in enumerate(first):
+            exponent_pass(banks[n], *g, 1)
+            exponential(banks[n], *g)
+
+        turn = [0]
+
+        def rate_tiles(kind, b, j, slots):
+            for t in slots:
+                bank = banks[turn[0] % 4]
+                turn.append(turn.pop() + 1)
+                exponent_pass(bank, kind, b, j, t, 0)
+                exponent_pass(bank, kind, b, j, t, 1)
+                exponential(bank, kind, b, j, t)
+
+        def y_bank(j, c):
+            return banks[4 + 2 * j + c]
+
+        def leak(j):
+            cols = slice(j * W, (j + 1) * W)
+            for c in range(2):
+                for a in range(2):
+                    nc.tensor.matmul_mx(
+                        out=y_bank(j, c)[:],
+                        lhsT=wd_codes[:, a, P * c : P * (c + 1)].bitcast(FP8X4),
+                        lhsT_scale=wd_sc[:, a, P * c : P * (c + 1)],
+                        rhs=v_codes[a][:, cols].bitcast(FP8X4),
+                        rhs_scale=v_scales[a][:, cols],
+                        start=(a == 0),
+                        stop=False,
+                    )
+
+        h_bf = {}
+        h_codes = {}
+        h_sc = {}
+
+        def net_rate(b, j):
+            h_bf[(b, j)] = held("h_bf%d%d" % (b, j), [P, W, 4], BF16)
+            nc.vector.tensor_tensor(
+                h_bf[(b, j)][:].rearrange("p (c i) t -> p c t i", i=4),
+                rates[("a", b, j)][:].rearrange("p t (c i) -> p c t i", i=4),
+                rates[("c", b, j)][:].rearrange("p t (c i) -> p c t i", i=4),
+                ALU.subtract,
+            )
+
+        def quantise_h(b, j):
+            h_codes[(b, j)] = held("h_codes%d%d" % (b, j), [P, W], U32)
+            h_sc[(b, j)] = held("h_sc%d%d" % (b, j), [P, W], U8)
+            nc.vector.quantize_mx(
+                out=h_codes[(b, j)][:].bitcast(FP8X4),
+                scales=h_sc[(b, j)][:],
+                in_=h_bf[(b, j)][:].rearrange("p c t -> p (c t)"),
+            )
+
+        w2_codes = held("w2_codes", [P, 2, N], U32)
+        w2_sc = held("w2_sc", [P, 2, N], U8)
+
+        def quantise_w2():
+            grouped = held("w2_bf", [P, 2, N, 4], BF16)
+            for b in range(2):
+                nc.vector.tensor_tensor(
+                    grouped[:, b, :, :].rearrange("p (c i) t -> p c t i", i=4),
+                    w2_raw[:, b, :, :].rearrange("p t (c i) -> p c t i", i=4),
+                    sgn[:, 4 * b : 4 * b + 4].unsqueeze(1).unsqueeze(3).to_broadcast([P, N // 4, 4, 4]),
+                    ALU.mult,
+                )
+            nc.vector.quantize_mx(
+                out=w2_codes[:].rearrange("p b n -> p (b n)").bitcast(FP8X4),
+                scales=w2_sc[:].rearrange("p b n -> p (b n)"),
+                in_=grouped[:].rearrange("p b n t -> p (b n t)"),
+            )
+
+        def collect(b, j):
+            for c in range(2):
+                nc.tensor.matmul_mx(
+                    out=y_bank(j, c)[:],
+                    lhsT=w2_codes[:, b, P * c : P * (c + 1)].bitcast(FP8X4),
+                    lhsT_scale=w2_sc[:, b, P * c : P * (c + 1)],
+                    rhs=h_codes[(b, j)][:].bitcast(FP8X4),
+                    rhs_scale=h_sc[(b, j)][:],
+                    start=False,
+                    stop=(b == 1),
+                )
+
+        def finish(j, c, on_vector):
+            result = held("result%d%d" % (j, c), [P, W], F32)
+            if on_vector:
+                nc.vector.tensor_scalar(result[:], y_bank(j, c)[:], bo_sb[:, c : c + 1], None, ALU.add)
+            else:
+                nc.scalar.activation(result[:], y_bank(j, c)[:], ACT.Identity, bias=bo_sb[:, c : c + 1])
+            nc.sync.dma_start(out=out[P * c : P * (c + 1), j * W : (j + 1) * W], in_=result[:])
+
+        rate_tiles("c", 1, 0, [0, 1])
+        quantise_wa(0, 0)
+        quantise_wa(1, 0)
+        rate_tiles("a", 0, 0, range(4))
+        quantise_wa(0, 1)
+        rate_tiles("a", 0, 1, range(4))
+        leak(0)
+        leak(1)
+        net_rate(0, 0)
+        quantise_wa(1, 1)
+        quantise_h(0, 0)
+        rate_tiles("c", 1, 0, [2, 3])
+        rate_tiles("c", 1, 1, range(4))
+        net_rate(0, 1)
+        quantise_w2()
+        quantise_h(0, 1)
+        rate_tiles("a", 1, 0, range(4))
+        collect(0, 0)
+        collect(0, 1)
+        rate_tiles("a", 1, 1, range(4))
+        net_rate(1, 0)
+        quantise_h(1, 0)
+        collect(1, 0)
+        net_rate(1, 1)
+        finish(0, 0, False)
+        finish(0, 1, False)
+        quantise_h(1, 1)
+        collect(1, 1)
+        finish(1, 0, False)
+        finish(1, 1, True)

@@ -44,20 +44,21 @@ def tile_list_electrode_node_currents_kernel(
 
         lane = placed("lane", [P, 4], I32, 0)
         nc.gpsimd.iota(lane[:], [[-1, 4]], base=4, channel_multiplier=1)
-        i0_runs = held("i0_runs", [P, 2, 16], F32)
-        i0_by_m = i0.rearrange("(b m x) -> b m x", b=2, x=16)
-        for b in range(2):
-            nc.gpsimd.dma_start(out=i0_runs[:, b, :], in_=i0_by_m[b].unsqueeze(1).to_broadcast([32, 4, 16]))
-
         wc_raw = placed("wc_raw", [P, 2, 2 * H], U8, 32 * KB)
         nc.sync.dma_start(out=wc_raw[:].bitcast(I32), in_=wc_words.rearrange("a p x -> p a x").bitcast(I32))
 
+
+        i0_runs = held("i0_runs", [P, 2, 16], F32)
+        i0_by_m = i0.rearrange("(b m x) -> b m x", b=2, x=16)
+        for b in range(2):
+            nc.sync.dma_start(out=i0_runs[:, b, :], in_=i0_by_m[b].unsqueeze(1).to_broadcast([32, 4, 16]))
+
         table_scales = placed("table_scales", [P, T], U8, 40 * KB)
         nc.vector.memset(table_scales[:].bitcast(I32), 0)
-        wc_scales_raw = held("wc_scales_raw", [P, 2, H], U8)
-        nc.vector.memset(wc_scales_raw[:].bitcast(I32), 0)
         lane_mod = placed("lane_mod", [P, 4], I32, 16 * KB)
         nc.vector.tensor_scalar(lane_mod[:], lane[:], 3, None, ALU.bitwise_and)
+        wc_scales_raw = held("wc_scales_raw", [P, 2, H], U8)
+        nc.vector.memset(wc_scales_raw[:].bitcast(I32), 0)
         own = held("own", [P, 4], F32)
         nc.vector.tensor_scalar(own[:], lane_mod[:], 0.0, None, ALU.is_equal)
         for q in range(4):
@@ -83,12 +84,6 @@ def tile_list_electrode_node_currents_kernel(
         load_table(1)
         v_scales1 = held("v_scales1", [P, S], U8)
         nc.vector.memset(v_scales1[:].bitcast(I32), 0)
-        wd_sc = held("wd_sc", [P, 2, N], U8)
-        nc.vector.memset(wd_sc[:].bitcast(I32), 0)
-        load_scale_rows(nc.gpsimd, wd_sc, wd_scales)
-        bo_sb = held("bo_sb", [P, 2], F32)
-        with nc.allow_non_contiguous_dma(reason="one bias a partition"):
-            nc.gpsimd.dma_start(out=bo_sb[:], in_=bo.rearrange("(c p) -> p c", p=P))
 
         wc_codes = held("wc_codes", [P, 4, 4, 256], U8)
         nc.vector.tensor_copy(
@@ -117,17 +112,19 @@ def tile_list_electrode_node_currents_kernel(
         nc.vector.tensor_scalar(expo[:], bits, 23, 0xFF, ALU.logical_shift_right, ALU.bitwise_and)
         ln_mant = held("ln_mant", [P, 8], F32)
         nc.scalar.activation(ln_mant[:], mant[:].bitcast(F32), ACT.Ln)
-        sgn = held("sgn", [P, 8], F32)
-        nc.scalar.activation(sgn[:], i0_sb[:], ACT.Sign)
         warm = held("warm", [P, 8], F32)
         nc.scalar.activation(warm[:], ln_mant[:], ACT.Exp)
         ln_pow = held("ln_pow", [P, 8], F32)
         nc.vector.tensor_scalar(ln_pow[:], expo[:], 127.0, math.log(2.0), ALU.subtract, ALU.mult)
 
+        sgn_bits = held("sgn_bits", [P, 8], I32)
+        nc.vector.tensor_scalar(sgn_bits[:], bits, -0x80000000, 0x3F800000, ALU.bitwise_and, ALU.bitwise_or)
+        sgn = sgn_bits[:].bitcast(F32)
+
         v_codes = [held("v_codes%d" % a, [P, S], U32) for a in range(2)]
         nc.vector.tensor_copy(v_codes[0][:], table[0][:].bitcast(U32).indirect(offsets[:]))
 
-        wc_sc = held("wc_sc", [P, 4, 4, 128], U8)
+        wc_sc = placed("wc_sc", [P, 4, 4, 128], U8, 40 * KB + 64)
         nc.vector.tensor_copy(
             out=wc_sc[:].bitcast(I32),
             in_=wc_scales_raw[:].bitcast(I32).rearrange("p a (b m t) -> p (a b) t m", b=2, t=4),
@@ -141,7 +138,7 @@ def tile_list_electrode_node_currents_kernel(
                 table[1][:].bitcast(U32).indirect(offsets[:, j * W // 16 : (j + 1) * W // 16]),
             )
 
-        wa_place = {(0, 0): 32 * KB, (1, 0): 40 * KB, (0, 1): 0, (1, 1): 16 * KB}
+        wa_place = {(0, 0): 32 * KB, (1, 0): 42 * KB + 128, (0, 1): 0, (1, 1): 16 * KB}
         wa_raw = {}
 
         def load_wa(a, b):
@@ -153,10 +150,16 @@ def tile_list_electrode_node_currents_kernel(
             wa_raw[(a, b)] = raw
 
         load_wa(0, 0)
+        bo_sb = placed("bo_sb", [P, 2], F32, 40 * KB)
+        with nc.allow_non_contiguous_dma(reason="one bias a partition"):
+            nc.sync.dma_start(out=bo_sb[:], in_=bo.rearrange("(c p) -> p c", p=P))
         load_wa(1, 0)
         load_wa(0, 1)
         wd_codes = placed("wd_codes", [P, 2, N], I32, 8 * KB)
         nc.sync.dma_start(out=wd_codes[:], in_=wd_words.rearrange("a p c i -> p a (c i)").bitcast(I32))
+        wd_sc = placed("wd_sc", [P, 2, N], U8, 10 * KB)
+        nc.vector.memset(wd_sc[:].bitcast(I32), 0)
+        load_scale_rows(nc.sync, wd_sc, wd_scales)
         load_wa(1, 1)
         w2_raw = placed("w2_raw", [P, 2, 4, N], F32, 24 * KB)
         w2_rows = w2.rearrange("(b m t u) n -> b t m u n", b=2, t=4, u=4)
@@ -167,8 +170,13 @@ def tile_list_electrode_node_currents_kernel(
         wa_codes = {}
         wa_sc = {}
 
+        wa_bf = held("wa_bf", [P, W, 4], BF16)
+
         def quantise_wa(a, b):
-            grouped = held("wa_bf%d%d" % (a, b), [P, W, 4], BF16)
+            if (a, b) == (1, 1):
+                grouped = placed("wa_bf11", [P, W, 4], BF16, 52 * KB)
+            else:
+                grouped = wa_bf
             nc.vector.tensor_copy(
                 out=grouped[:].rearrange("p (t m u) j -> p t m j u", t=4, u=4),
                 in_=wa_raw[(a, b)][:].rearrange("p j (m t u) -> p t m j u", t=4, u=4),
@@ -185,7 +193,11 @@ def tile_list_electrode_node_currents_kernel(
         for kind in "ac":
             for b in range(2):
                 for j in range(HALVES):
-                    rates[(kind, b, j)] = held("rate_%s%d%d" % (kind, b, j), [P, 4, W], F32)
+                    name = "rate_%s%d%d" % (kind, b, j)
+                    if (kind, b) == ("a", 0):
+                        rates[(kind, b, j)] = placed(name, [P, 4, W], F32, (52 + 8 * j) * KB)
+                    else:
+                        rates[(kind, b, j)] = held(name, [P, 4, W], F32)
 
         def exponent_pass(bank, kind, b, j, t, a):
             cols = slice(j * W, (j + 1) * W)
@@ -217,25 +229,22 @@ def tile_list_electrode_node_currents_kernel(
             exponent_pass(banks[n], *g, 1)
             exponential(banks[n], *g)
 
-        turn = [0]
-
-        def rate_tiles(kind, b, j, slots):
-            for t in slots:
-                bank = banks[turn[0] % 4]
-                turn.append(turn.pop() + 1)
+        def rate_tiles(kind, b, j, slots, on):
+            for t, n in zip(slots, on):
+                bank = banks[n]
                 exponent_pass(bank, kind, b, j, t, 0)
                 exponent_pass(bank, kind, b, j, t, 1)
                 exponential(bank, kind, b, j, t)
 
-        def y_bank(j, c):
-            return banks[4 + 2 * j + c]
+        spans = [(0, 512, (4, 5)), (512, 256, (6, 7)), (768, 256, (0, 1))]
 
-        def leak(j):
-            cols = slice(j * W, (j + 1) * W)
+        def leak(s):
+            first_col, width, on = spans[s]
+            cols = slice(first_col, first_col + width)
             for c in range(2):
                 for a in range(2):
                     nc.tensor.matmul_mx(
-                        out=y_bank(j, c)[:],
+                        out=banks[on[c]][:, 0:width],
                         lhsT=wd_codes[:, a, P * c : P * (c + 1)].bitcast(FP8X4),
                         lhsT_scale=wd_sc[:, a, P * c : P * (c + 1)],
                         rhs=v_codes[a][:, cols].bitcast(FP8X4),
@@ -244,33 +253,32 @@ def tile_list_electrode_node_currents_kernel(
                         stop=False,
                     )
 
-        h_bf = {}
-        h_codes = {}
-        h_sc = {}
+        h_bf = [held("h_bf%d" % b, [P, S, 4], BF16) for b in range(2)]
+        h_codes = [held("h_codes%d" % b, [P, S], U32) for b in range(2)]
+        h_sc = [held("h_sc%d" % b, [P, S], U8) for b in range(2)]
 
-        def net_rate(b, j):
-            h_bf[(b, j)] = held("h_bf%d%d" % (b, j), [P, W, 4], BF16)
+        def net_rate(b, first_col, width):
+            j, at = divmod(first_col, W)
             nc.vector.tensor_tensor(
-                h_bf[(b, j)][:].rearrange("p (c i) t -> p c t i", i=4),
-                rates[("a", b, j)][:].rearrange("p t (c i) -> p c t i", i=4),
-                rates[("c", b, j)][:].rearrange("p t (c i) -> p c t i", i=4),
+                h_bf[b][:, first_col : first_col + width, :].rearrange("p (c i) t -> p c t i", i=4),
+                rates[("a", b, j)][:, :, at : at + width].rearrange("p t (c i) -> p c t i", i=4),
+                rates[("c", b, j)][:, :, at : at + width].rearrange("p t (c i) -> p c t i", i=4),
                 ALU.subtract,
             )
 
-        def quantise_h(b, j):
-            h_codes[(b, j)] = held("h_codes%d%d" % (b, j), [P, W], U32)
-            h_sc[(b, j)] = held("h_sc%d%d" % (b, j), [P, W], U8)
+        def quantise_h(b, first_col, width):
+            cols = slice(first_col, first_col + width)
             nc.vector.quantize_mx(
-                out=h_codes[(b, j)][:].bitcast(FP8X4),
-                scales=h_sc[(b, j)][:],
-                in_=h_bf[(b, j)][:].rearrange("p c t -> p (c t)"),
+                out=h_codes[b][:, cols].bitcast(FP8X4),
+                scales=h_sc[b][:, cols],
+                in_=h_bf[b][:, cols, :].rearrange("p c t -> p (c t)"),
             )
 
         w2_codes = held("w2_codes", [P, 2, N], U32)
         w2_sc = held("w2_sc", [P, 2, N], U8)
 
         def quantise_w2():
-            grouped = held("w2_bf", [P, 2, N, 4], BF16)
+            grouped = placed("w2_bf", [P, 2, N, 4], BF16, 60 * KB)
             for b in range(2):
                 nc.vector.tensor_tensor(
                     grouped[:, b, :, :].rearrange("p (c i) t -> p c t i", i=4),
@@ -284,53 +292,64 @@ def tile_list_electrode_node_currents_kernel(
                 in_=grouped[:].rearrange("p b n t -> p (b n t)"),
             )
 
-        def collect(b, j):
+        def collect(b, s):
+            first_col, width, on = spans[s]
+            cols = slice(first_col, first_col + width)
             for c in range(2):
                 nc.tensor.matmul_mx(
-                    out=y_bank(j, c)[:],
+                    out=banks[on[c]][:, 0:width],
                     lhsT=w2_codes[:, b, P * c : P * (c + 1)].bitcast(FP8X4),
                     lhsT_scale=w2_sc[:, b, P * c : P * (c + 1)],
-                    rhs=h_codes[(b, j)][:].bitcast(FP8X4),
-                    rhs_scale=h_sc[(b, j)][:],
+                    rhs=h_codes[b][:, cols].bitcast(FP8X4),
+                    rhs_scale=h_sc[b][:, cols],
                     start=False,
                     stop=(b == 1),
                 )
 
-        def finish(j, c, on_vector):
-            result = held("result%d%d" % (j, c), [P, W], F32)
+        def finish(s, c, on_vector):
+            first_col, width, on = spans[s]
+            result = held("result%d%d" % (s, c), [P, width], F32)
+            total = banks[on[c]][:, 0:width]
             if on_vector:
-                nc.vector.tensor_scalar(result[:], y_bank(j, c)[:], bo_sb[:, c : c + 1], None, ALU.add)
+                nc.vector.tensor_scalar(result[:], total, bo_sb[:, c : c + 1], None, ALU.add)
             else:
-                nc.scalar.activation(result[:], y_bank(j, c)[:], ACT.Identity, bias=bo_sb[:, c : c + 1])
-            nc.sync.dma_start(out=out[P * c : P * (c + 1), j * W : (j + 1) * W], in_=result[:])
+                nc.scalar.activation(result[:], total, ACT.Identity, bias=bo_sb[:, c : c + 1])
+            nc.sync.dma_start(out=out[P * c : P * (c + 1), first_col : first_col + width], in_=result[:])
 
-        rate_tiles("c", 1, 0, [0, 1])
+        rate_tiles("c", 1, 0, [0, 1], [0, 1])
         quantise_wa(0, 0)
         quantise_wa(1, 0)
-        rate_tiles("a", 0, 0, range(4))
+        rate_tiles("a", 0, 0, range(4), [2, 3, 4, 5])
         quantise_wa(0, 1)
-        rate_tiles("a", 0, 1, range(4))
+        rate_tiles("a", 0, 1, range(4), [6, 7, 0, 1])
         leak(0)
         leak(1)
-        net_rate(0, 0)
+        net_rate(0, 0, W)
         quantise_wa(1, 1)
-        quantise_h(0, 0)
-        rate_tiles("c", 1, 0, [2, 3])
-        rate_tiles("c", 1, 1, range(4))
-        net_rate(0, 1)
+        quantise_h(0, 0, W)
+        rate_tiles("c", 1, 0, [2, 3], [2, 3])
+        rate_tiles("c", 1, 1, range(4), range(4))
+        net_rate(0, W, W)
         quantise_w2()
-        quantise_h(0, 1)
-        rate_tiles("a", 1, 0, range(4))
+        quantise_h(0, W, W)
+        rate_tiles("a", 1, 0, range(4), range(4))
         collect(0, 0)
         collect(0, 1)
-        rate_tiles("a", 1, 1, range(4))
-        net_rate(1, 0)
-        quantise_h(1, 0)
+        rate_tiles("a", 1, 1, range(4), range(4))
+        leak(2)
+        collect(0, 2)
+        net_rate(1, 0, W)
+        quantise_h(1, 0, W)
         collect(1, 0)
-        net_rate(1, 1)
         finish(0, 0, False)
         finish(0, 1, False)
-        quantise_h(1, 1)
+        net_rate(1, 512, 256)
+        quantise_h(1, 512, 256)
         collect(1, 1)
         finish(1, 0, False)
-        finish(1, 1, True)
+        finish(1, 1, False)
+        net_rate(1, 768, 256)
+        quantise_h(1, 768, 256)
+        collect(1, 2)
+        finish(2, 0, False)
+        finish(2, 1, True)

@@ -42,7 +42,7 @@ def tile_list_electrode_node_currents_kernel(
         offsets = keep.tile([P, S // 16], U16, name="offsets")
         nc.sync.dma_start(offsets[:], offs)
 
-        lane = placed("lane", [P, 4], I32, 0)
+        lane = held("lane", [P, 4], I32)
         nc.gpsimd.iota(lane[:], [[-1, 4]], base=4, channel_multiplier=1)
         wc_raw = placed("wc_raw", [P, 2, 2 * H], U8, 32 * KB)
         nc.sync.dma_start(out=wc_raw[:].bitcast(I32), in_=wc_words.rearrange("a p x -> p a x").bitcast(I32))
@@ -55,17 +55,15 @@ def tile_list_electrode_node_currents_kernel(
 
         table_scales = placed("table_scales", [P, T], U8, 40 * KB)
         nc.vector.memset(table_scales[:].bitcast(I32), 0)
-        lane_mod = placed("lane_mod", [P, 4], I32, 16 * KB)
+        lane_mod = held("lane_mod", [P, 4], I32)
         nc.vector.tensor_scalar(lane_mod[:], lane[:], 3, None, ALU.bitwise_and)
-        wc_scales_raw = held("wc_scales_raw", [P, 2, H], U8)
+        wc_scales_raw = placed("wc_scales_raw", [P, 2, H], U8, 60 * KB)
         nc.vector.memset(wc_scales_raw[:].bitcast(I32), 0)
         own = held("own", [P, 4], F32)
         nc.vector.tensor_scalar(own[:], lane_mod[:], 0.0, None, ALU.is_equal)
-        for q in range(4):
-            nc.sync.dma_start(
-                out=table_scales[32 * q : 32 * q + 8, :].bitcast(I32),
-                in_=tab_scales[:, 4 * q : 4 * q + 4, :].bitcast(I32),
-            )
+        rows_by_r = tab_scales.rearrange("a (q r) t -> r q a t", r=4).bitcast(I32)
+        for r in range(4):
+            nc.sync.dma_start(out=table_scales[r:P:16, :].bitcast(I32), in_=rows_by_r[r])
 
         def load_scale_rows(queue, plane, src):
             for q in range(4):
@@ -93,7 +91,7 @@ def tile_list_electrode_node_currents_kernel(
 
         v_scales0 = held("v_scales0", [P, S], U8)
         nc.vector.tensor_copy(v_scales0[:], table_scales[:].indirect(offsets[:]))
-        nc.scalar.dma_start(out=v_scales1[0:100, :].bitcast(I32), in_=v_scales0[4:104, :].bitcast(I32))
+        nc.sync.dma_start(out=v_scales1[0:100, :].bitcast(I32), in_=v_scales0[16:116, :].bitcast(I32))
         v_scales = [v_scales0, v_scales1]
 
         i0_masked = held("i0_masked", [P, 8, 4], F32)
@@ -121,10 +119,16 @@ def tile_list_electrode_node_currents_kernel(
         nc.vector.tensor_scalar(sgn_bits[:], bits, -0x80000000, 0x3F800000, ALU.bitwise_and, ALU.bitwise_or)
         sgn = sgn_bits[:].bitcast(F32)
 
-        v_codes = [held("v_codes%d" % a, [P, S], U32) for a in range(2)]
-        nc.vector.tensor_copy(v_codes[0][:], table[0][:].bitcast(U32).indirect(offsets[:]))
+        v_codes = {}
 
-        wc_sc = placed("wc_sc", [P, 4, 4, 128], U8, 40 * KB + 64)
+        def gather_words(a, j, into):
+            nc.vector.tensor_copy(
+                into[:], table[a][:].bitcast(U32).indirect(offsets[:, j * W // 16 : (j + 1) * W // 16])
+            )
+            v_codes[(a, j)] = into
+
+        gather_words(0, 0, held("v_codes00", [P, W], U32))
+        wc_sc = held("wc_sc", [P, 4, 4, 128], U8)
         nc.vector.tensor_copy(
             out=wc_sc[:].bitcast(I32),
             in_=wc_scales_raw[:].bitcast(I32).rearrange("p a (b m t) -> p (a b) t m", b=2, t=4),
@@ -132,13 +136,11 @@ def tile_list_electrode_node_currents_kernel(
         ln_i0 = held("ln_i0", [P, 8], F32)
         nc.vector.tensor_tensor(ln_i0[:], ln_mant[:], ln_pow[:], ALU.add)
 
+        gather_words(0, 1, placed("v_codes01", [P, W], U32, 60 * KB))
         for j in range(HALVES):
-            nc.vector.tensor_copy(
-                v_codes[1][:, j * W : (j + 1) * W],
-                table[1][:].bitcast(U32).indirect(offsets[:, j * W // 16 : (j + 1) * W // 16]),
-            )
+            gather_words(1, j, held("v_codes1%d" % j, [P, W], U32))
 
-        wa_place = {(0, 0): 32 * KB, (1, 0): 42 * KB + 128, (0, 1): 0, (1, 1): 16 * KB}
+        wa_place = {(0, 0): 34 * KB, (1, 0): 42 * KB, (0, 1): 0, (1, 1): 16 * KB}
         wa_raw = {}
 
         def load_wa(a, b):
@@ -150,18 +152,18 @@ def tile_list_electrode_node_currents_kernel(
             wa_raw[(a, b)] = raw
 
         load_wa(0, 0)
-        bo_sb = placed("bo_sb", [P, 2], F32, 40 * KB)
-        with nc.allow_non_contiguous_dma(reason="one bias a partition"):
-            nc.sync.dma_start(out=bo_sb[:], in_=bo.rearrange("(c p) -> p c", p=P))
         load_wa(1, 0)
         load_wa(0, 1)
-        wd_codes = placed("wd_codes", [P, 2, N], I32, 8 * KB)
-        nc.sync.dma_start(out=wd_codes[:], in_=wd_words.rearrange("a p c i -> p a (c i)").bitcast(I32))
-        wd_sc = placed("wd_sc", [P, 2, N], U8, 10 * KB)
+        bo_sb = placed("bo_sb", [P, 2], F32, 8 * KB)
+        with nc.allow_non_contiguous_dma(reason="one bias a partition"):
+            nc.sync.dma_start(out=bo_sb[:], in_=bo.rearrange("(c p) -> p c", p=P))
+        wd_sc = placed("wd_sc", [P, 2, N], U8, 8 * KB + 64)
         nc.vector.memset(wd_sc[:].bitcast(I32), 0)
         load_scale_rows(nc.sync, wd_sc, wd_scales)
         load_wa(1, 1)
-        w2_raw = placed("w2_raw", [P, 2, 4, N], F32, 24 * KB)
+        wd_codes = placed("wd_codes", [P, 2, N], I32, 24 * KB)
+        nc.sync.dma_start(out=wd_codes[:], in_=wd_words.rearrange("a p c i -> p a (c i)").bitcast(I32))
+        w2_raw = placed("w2_raw", [P, 2, 4, N], F32, 34 * KB)
         w2_rows = w2.rearrange("(b m t u) n -> b t m u n", b=2, t=4, u=4)
         for b in range(2):
             for t in range(4):
@@ -172,15 +174,22 @@ def tile_list_electrode_node_currents_kernel(
 
         wa_bf = held("wa_bf", [P, W, 4], BF16)
 
-        def quantise_wa(a, b):
-            if (a, b) == (1, 1):
-                grouped = placed("wa_bf11", [P, W, 4], BF16, 52 * KB)
-            else:
-                grouped = wa_bf
+        def round_wa_on_vector(a, b):
             nc.vector.tensor_copy(
-                out=grouped[:].rearrange("p (t m u) j -> p t m j u", t=4, u=4),
+                out=wa_bf[:].rearrange("p (t m u) j -> p t m j u", t=4, u=4),
                 in_=wa_raw[(a, b)][:].rearrange("p j (m t u) -> p t m j u", t=4, u=4),
             )
+            return wa_bf
+
+        def round_wa_on_scalar(a, b):
+            grouped = placed("wa_bf_last", [P, W, 4], BF16, 52 * KB)
+            by_t_out = grouped[:].rearrange("p (t m u) j -> p t m j u", t=4, u=4)
+            by_t_in = wa_raw[(a, b)][:].rearrange("p j (m t u) -> p t m j u", t=4, u=4)
+            for t in range(4):
+                nc.scalar.copy(by_t_out[:, t], by_t_in[:, t])
+            return grouped
+
+        def quantise_wa(a, b, grouped):
             wa_codes[(a, b)] = held("wa_codes%d%d" % (a, b), [P, W], U32)
             wa_sc[(a, b)] = held("wa_sc%d%d" % (a, b), [P, W], U8)
             nc.vector.quantize_mx(
@@ -194,13 +203,13 @@ def tile_list_electrode_node_currents_kernel(
             for b in range(2):
                 for j in range(HALVES):
                     name = "rate_%s%d%d" % (kind, b, j)
-                    if (kind, b) == ("a", 0):
-                        rates[(kind, b, j)] = placed(name, [P, 4, W], F32, (52 + 8 * j) * KB)
+                    if (kind, b, j) == ("a", 0, 0):
+                        rates[(kind, b, j)] = placed(name, [P, 4, W], F32, 52 * KB)
                     else:
                         rates[(kind, b, j)] = held(name, [P, 4, W], F32)
 
-        def exponent_pass(bank, kind, b, j, t, a):
-            cols = slice(j * W, (j + 1) * W)
+        def exponent_pass(bank, kind, b, j, t, a, part=slice(0, W)):
+            cols = slice(j * W + part.start, j * W + part.stop)
             if kind == "a":
                 lhs = wa_codes[(a, b)][:, P * t : P * (t + 1)].bitcast(FP8X4)
                 lhs_sc = wa_sc[(a, b)][:, P * t : P * (t + 1)]
@@ -208,18 +217,18 @@ def tile_list_electrode_node_currents_kernel(
                 lhs = wc_codes[:, 2 * a + b, t, :].bitcast(FP4X4)
                 lhs_sc = wc_sc[:, 2 * a + b, t, :]
             nc.tensor.matmul_mx(
-                out=bank[:],
+                out=bank[:, part],
                 lhsT=lhs,
                 lhsT_scale=lhs_sc,
-                rhs=v_codes[a][:, cols].bitcast(FP8X4),
+                rhs=v_codes[(a, j)][:, part].bitcast(FP8X4),
                 rhs_scale=v_scales[a][:, cols],
                 start=(a == 0),
                 stop=(a == 1),
             )
 
-        def exponential(bank, kind, b, j, t):
+        def exponential(bank, kind, b, j, t, part=slice(0, W)):
             nc.scalar.activation(
-                rates[(kind, b, j)][:, t, :], bank[:], ACT.Exp, bias=ln_i0[:, 4 * b + t : 4 * b + t + 1]
+                rates[(kind, b, j)][:, t, part], bank[:, part], ACT.Exp, bias=ln_i0[:, 4 * b + t : 4 * b + t + 1]
             )
 
         first = [("c", 0, j, t) for j in range(HALVES) for t in range(4)]
@@ -229,31 +238,32 @@ def tile_list_electrode_node_currents_kernel(
             exponent_pass(banks[n], *g, 1)
             exponential(banks[n], *g)
 
-        def rate_tiles(kind, b, j, slots, on):
+        def rate_tiles(kind, b, j, slots, on, part=slice(0, W)):
             for t, n in zip(slots, on):
                 bank = banks[n]
-                exponent_pass(bank, kind, b, j, t, 0)
-                exponent_pass(bank, kind, b, j, t, 1)
-                exponential(bank, kind, b, j, t)
+                exponent_pass(bank, kind, b, j, t, 0, part)
+                exponent_pass(bank, kind, b, j, t, 1, part)
+                exponential(bank, kind, b, j, t, part)
 
         spans = [(0, 512, (4, 5)), (512, 256, (6, 7)), (768, 256, (0, 1))]
 
         def leak(s):
             first_col, width, on = spans[s]
             cols = slice(first_col, first_col + width)
+            j, at = divmod(first_col, W)
             for c in range(2):
                 for a in range(2):
                     nc.tensor.matmul_mx(
                         out=banks[on[c]][:, 0:width],
                         lhsT=wd_codes[:, a, P * c : P * (c + 1)].bitcast(FP8X4),
                         lhsT_scale=wd_sc[:, a, P * c : P * (c + 1)],
-                        rhs=v_codes[a][:, cols].bitcast(FP8X4),
+                        rhs=v_codes[(a, j)][:, at : at + width].bitcast(FP8X4),
                         rhs_scale=v_scales[a][:, cols],
                         start=(a == 0),
                         stop=False,
                     )
 
-        h_bf = [held("h_bf%d" % b, [P, S, 4], BF16) for b in range(2)]
+        h_bf = [placed("h_bf0", [P, S, 4], BF16, 0)]
         h_codes = [held("h_codes%d" % b, [P, S], U32) for b in range(2)]
         h_sc = [held("h_sc%d" % b, [P, S], U8) for b in range(2)]
 
@@ -278,7 +288,7 @@ def tile_list_electrode_node_currents_kernel(
         w2_sc = held("w2_sc", [P, 2, N], U8)
 
         def quantise_w2():
-            grouped = placed("w2_bf", [P, 2, N, 4], BF16, 60 * KB)
+            grouped = placed("w2_bf", [P, 2, N, 4], BF16, 52 * KB)
             for b in range(2):
                 nc.vector.tensor_tensor(
                     grouped[:, b, :, :].rearrange("p (c i) t -> p c t i", i=4),
@@ -316,26 +326,29 @@ def tile_list_electrode_node_currents_kernel(
                 nc.scalar.activation(result[:], total, ACT.Identity, bias=bo_sb[:, c : c + 1])
             nc.sync.dma_start(out=out[P * c : P * (c + 1), first_col : first_col + width], in_=result[:])
 
-        rate_tiles("c", 1, 0, [0, 1], [0, 1])
-        quantise_wa(0, 0)
-        quantise_wa(1, 0)
-        rate_tiles("a", 0, 0, range(4), [2, 3, 4, 5])
-        quantise_wa(0, 1)
-        rate_tiles("a", 0, 1, range(4), [6, 7, 0, 1])
+        rate_tiles("c", 1, 0, [0], [0])
+        quantise_wa(0, 0, round_wa_on_vector(0, 0))
+        quantise_wa(1, 0, round_wa_on_vector(1, 0))
+        rate_tiles("a", 0, 0, range(4), [1, 2, 3, 4])
+        quantise_wa(0, 1, round_wa_on_vector(0, 1))
+        rate_tiles("a", 0, 1, range(4), [5, 6, 7, 0])
+        net_rate(0, 0, W)
+        wa_last = round_wa_on_scalar(1, 1)
+        quantise_h(0, 0, W)
+        net_rate(0, W, W)
+        quantise_wa(1, 1, wa_last)
+        quantise_h(0, W, W)
+        rate_tiles("c", 1, 0, [1, 2, 3], [1, 2, 3])
         leak(0)
         leak(1)
-        net_rate(0, 0, W)
-        quantise_wa(1, 1)
-        quantise_h(0, 0, W)
-        rate_tiles("c", 1, 0, [2, 3], [2, 3])
-        rate_tiles("c", 1, 1, range(4), range(4))
-        net_rate(0, W, W)
         quantise_w2()
-        quantise_h(0, W, W)
+        h_bf.append(placed("h_bf1", [P, S, 4], BF16, 52 * KB))
         rate_tiles("a", 1, 0, range(4), range(4))
+        rate_tiles("c", 1, 1, range(4), range(4))
         collect(0, 0)
         collect(0, 1)
-        rate_tiles("a", 1, 1, range(4), range(4))
+        rate_tiles("a", 1, 1, range(4), range(4), slice(0, 256))
+        rate_tiles("a", 1, 1, range(4), range(4), slice(256, 512))
         leak(2)
         collect(0, 2)
         net_rate(1, 0, W)

@@ -22,6 +22,26 @@ W = 512
 HALVES = S // W
 KB = 1024
 
+AT_TABLE = (0, 16 * KB)
+AT_WA = {
+    (0, 0): 34 * KB,
+    (1, 0): 42 * KB,
+    (0, 1): 0,
+    (1, 1): 16 * KB,
+}
+AT_BO = 8 * KB
+AT_WD_SCALES = 8 * KB + 64
+AT_WD_CODES = 24 * KB
+AT_WC_RAW = 32 * KB
+AT_TABLE_SCALES = 40 * KB
+AT_FIRST_ANODIC = 52 * KB
+AT_WC_SCALES_RAW = 60 * KB
+
+PASS_ROW_SHIFT = 16
+LIVE_ROWS = 100
+
+SPANS = ((0, 512, (4, 5)), (512, 256, (6, 7)), (768, 256, (0, 1)))
+
 
 def tile_list_electrode_node_currents_kernel(
     tc, tab_words, tab_scales, offs, wa, wc_words, wc_scales, wd_words, wd_scales, i0, w2, bo, out
@@ -44,41 +64,39 @@ def tile_list_electrode_node_currents_kernel(
 
         lane = held("lane", [P, 4], I32)
         nc.gpsimd.iota(lane[:], [[-1, 4]], base=4, channel_multiplier=1)
-        wc_raw = placed("wc_raw", [P, 2, 2 * H], U8, 32 * KB)
+        wc_raw = placed("wc_raw", [P, 2, 2 * H], U8, AT_WC_RAW)
         nc.sync.dma_start(out=wc_raw[:].bitcast(I32), in_=wc_words.rearrange("a p x -> p a x").bitcast(I32))
-
-
         i0_runs = held("i0_runs", [P, 2, 16], F32)
         i0_by_m = i0.rearrange("(b m x) -> b m x", b=2, x=16)
         for b in range(2):
             nc.sync.dma_start(out=i0_runs[:, b, :], in_=i0_by_m[b].unsqueeze(1).to_broadcast([32, 4, 16]))
 
-        table_scales = placed("table_scales", [P, T], U8, 40 * KB)
+        table_scales = placed("table_scales", [P, T], U8, AT_TABLE_SCALES)
         nc.vector.memset(table_scales[:].bitcast(I32), 0)
         lane_mod = held("lane_mod", [P, 4], I32)
         nc.vector.tensor_scalar(lane_mod[:], lane[:], 3, None, ALU.bitwise_and)
-        wc_scales_raw = placed("wc_scales_raw", [P, 2, H], U8, 60 * KB)
+        wc_scales_raw = placed("wc_scales_raw", [P, 2, H], U8, AT_WC_SCALES_RAW)
         nc.vector.memset(wc_scales_raw[:].bitcast(I32), 0)
         own = held("own", [P, 4], F32)
         nc.vector.tensor_scalar(own[:], lane_mod[:], 0.0, None, ALU.is_equal)
-        rows_by_r = tab_scales.rearrange("a (q r) t -> r q a t", r=4).bitcast(I32)
-        for r in range(4):
-            nc.sync.dma_start(out=table_scales[r:P:16, :].bitcast(I32), in_=rows_by_r[r])
+        rows_by_e = tab_scales.rearrange("a (g e) t -> e g a t", e=4).bitcast(I32)
+        for e in range(4):
+            nc.sync.dma_start(out=table_scales[e:P:PASS_ROW_SHIFT, :].bitcast(I32), in_=rows_by_e[e])
 
-        def load_scale_rows(queue, plane, src):
-            for q in range(4):
-                queue.dma_start(
-                    out=plane[32 * q : 32 * q + 4, :, :].bitcast(I32),
-                    in_=src[:, 4 * q : 4 * q + 4, :].rearrange("a r n -> r a n").bitcast(I32),
+        def load_scale_rows(planes, src):
+            for g in range(4):
+                nc.sync.dma_start(
+                    out=planes[32 * g : 32 * g + 4, :, :].bitcast(I32),
+                    in_=src[:, 4 * g : 4 * g + 4, :].rearrange("a e n -> e a n").bitcast(I32),
                 )
 
-        table = [placed("table%d" % a, [P, T], I32, 16 * KB * a) for a in range(2)]
+        table = [placed("table%d" % a, [P, T], I32, AT_TABLE[a]) for a in range(2)]
 
         def load_table(a):
             nc.sync.dma_start(out=table[a][:], in_=tab_words[a].rearrange("p t i -> p (t i)").bitcast(I32))
 
         load_table(0)
-        load_scale_rows(nc.sync, wc_scales_raw, wc_scales)
+        load_scale_rows(wc_scales_raw, wc_scales)
         load_table(1)
         v_scales1 = held("v_scales1", [P, S], U8)
         nc.vector.memset(v_scales1[:].bitcast(I32), 0)
@@ -91,7 +109,10 @@ def tile_list_electrode_node_currents_kernel(
 
         v_scales0 = held("v_scales0", [P, S], U8)
         nc.vector.tensor_copy(v_scales0[:], table_scales[:].indirect(offsets[:]))
-        nc.sync.dma_start(out=v_scales1[0:100, :].bitcast(I32), in_=v_scales0[16:116, :].bitcast(I32))
+        nc.sync.dma_start(
+            out=v_scales1[0:LIVE_ROWS, :].bitcast(I32),
+            in_=v_scales0[PASS_ROW_SHIFT : PASS_ROW_SHIFT + LIVE_ROWS, :].bitcast(I32),
+        )
         v_scales = [v_scales0, v_scales1]
 
         i0_masked = held("i0_masked", [P, 8, 4], F32)
@@ -104,20 +125,17 @@ def tile_list_electrode_node_currents_kernel(
         i0_sb = held("i0_sb", [P, 8], F32)
         nc.vector.tensor_reduce(i0_sb[:], i0_masked[:], mybir.AxisListType.X, ALU.add)
         bits = i0_sb[:].bitcast(I32)
-        mant = held("mant", [P, 8], I32)
-        nc.vector.tensor_scalar(mant[:], bits, 0x007FFFFF, 0x3F800000, ALU.bitwise_and, ALU.bitwise_or)
-        expo = held("expo", [P, 8], I32)
-        nc.vector.tensor_scalar(expo[:], bits, 23, 0xFF, ALU.logical_shift_right, ALU.bitwise_and)
-        ln_mant = held("ln_mant", [P, 8], F32)
-        nc.scalar.activation(ln_mant[:], mant[:].bitcast(F32), ACT.Ln)
-        warm = held("warm", [P, 8], F32)
-        nc.scalar.activation(warm[:], ln_mant[:], ACT.Exp)
-        ln_pow = held("ln_pow", [P, 8], F32)
-        nc.vector.tensor_scalar(ln_pow[:], expo[:], 127.0, math.log(2.0), ALU.subtract, ALU.mult)
-
-        sgn_bits = held("sgn_bits", [P, 8], I32)
-        nc.vector.tensor_scalar(sgn_bits[:], bits, -0x80000000, 0x3F800000, ALU.bitwise_and, ALU.bitwise_or)
-        sgn = sgn_bits[:].bitcast(F32)
+        mantissa = held("mantissa", [P, 8], I32)
+        nc.vector.tensor_scalar(mantissa[:], bits, 0x007FFFFF, 0x3F800000, ALU.bitwise_and, ALU.bitwise_or)
+        exponent = held("exponent", [P, 8], I32)
+        nc.vector.tensor_scalar(exponent[:], bits, 23, 0xFF, ALU.logical_shift_right, ALU.bitwise_and)
+        ln_mantissa = held("ln_mantissa", [P, 8], F32)
+        nc.scalar.activation(ln_mantissa[:], mantissa[:].bitcast(F32), ACT.Ln)
+        ln_power = held("ln_power", [P, 8], F32)
+        nc.vector.tensor_scalar(ln_power[:], exponent[:], 127.0, math.log(2.0), ALU.subtract, ALU.mult)
+        sign_bits = held("sign_bits", [P, 8], I32)
+        nc.vector.tensor_scalar(sign_bits[:], bits, -0x80000000, 0x3F800000, ALU.bitwise_and, ALU.bitwise_or)
+        i0_sign = sign_bits[:].bitcast(F32)
 
         v_codes = {}
 
@@ -134,68 +152,68 @@ def tile_list_electrode_node_currents_kernel(
             in_=wc_scales_raw[:].bitcast(I32).rearrange("p a (b m t) -> p (a b) t m", b=2, t=4),
         )
         ln_i0 = held("ln_i0", [P, 8], F32)
-        nc.vector.tensor_tensor(ln_i0[:], ln_mant[:], ln_pow[:], ALU.add)
-
-        gather_words(0, 1, placed("v_codes01", [P, W], U32, 60 * KB))
+        nc.vector.tensor_tensor(ln_i0[:], ln_mantissa[:], ln_power[:], ALU.add)
+        gather_words(0, 1, placed("v_codes01", [P, W], U32, AT_WC_SCALES_RAW))
         for j in range(HALVES):
             gather_words(1, j, held("v_codes1%d" % j, [P, W], U32))
 
-        wa_place = {(0, 0): 34 * KB, (1, 0): 42 * KB, (0, 1): 0, (1, 1): 16 * KB}
         wa_raw = {}
 
         def load_wa(a, b):
-            raw = placed("wa_raw%d%d" % (a, b), [P, 4, W], F32, wa_place[(a, b)])
+            wa_raw[(a, b)] = placed("wa_raw%d%d" % (a, b), [P, 4, W], F32, AT_WA[(a, b)])
             nc.sync.dma_start(
-                out=raw[:],
-                in_=wa[W * a : W * (a + 1), W * b : W * (b + 1)].rearrange("(p j) c -> p j c", j=4),
+                out=wa_raw[(a, b)][:],
+                in_=wa[W * a : W * (a + 1), W * b : W * (b + 1)].rearrange("(p i) c -> p i c", i=4),
             )
-            wa_raw[(a, b)] = raw
 
         load_wa(0, 0)
         load_wa(1, 0)
         load_wa(0, 1)
-        bo_sb = placed("bo_sb", [P, 2], F32, 8 * KB)
+        bo_sb = placed("bo_sb", [P, 2], F32, AT_BO)
         with nc.allow_non_contiguous_dma(reason="one bias a partition"):
             nc.sync.dma_start(out=bo_sb[:], in_=bo.rearrange("(c p) -> p c", p=P))
-        wd_sc = placed("wd_sc", [P, 2, N], U8, 8 * KB + 64)
+        wd_sc = placed("wd_sc", [P, 2, N], U8, AT_WD_SCALES)
         nc.vector.memset(wd_sc[:].bitcast(I32), 0)
-        load_scale_rows(nc.sync, wd_sc, wd_scales)
+        load_scale_rows(wd_sc, wd_scales)
         load_wa(1, 1)
-        wd_codes = placed("wd_codes", [P, 2, N], I32, 24 * KB)
+        wd_codes = placed("wd_codes", [P, 2, N], I32, AT_WD_CODES)
         nc.sync.dma_start(out=wd_codes[:], in_=wd_words.rearrange("a p c i -> p a (c i)").bitcast(I32))
-        w2_raw = placed("w2_raw", [P, 2, 4, N], F32, 34 * KB)
+        w2_raw = placed("w2_raw", [P, 2, 4, N], F32, AT_WA[(0, 0)])
         w2_rows = w2.rearrange("(b m t u) n -> b t m u n", b=2, t=4, u=4)
         for b in range(2):
             for t in range(4):
                 nc.sync.dma_start(out=w2_raw[:, b, t, :], in_=w2_rows[b, t])
 
-        wa_codes = {}
-        wa_sc = {}
-
         wa_bf = held("wa_bf", [P, W, 4], BF16)
 
-        def round_wa_on_vector(a, b):
-            nc.vector.tensor_copy(
-                out=wa_bf[:].rearrange("p (t m u) j -> p t m j u", t=4, u=4),
-                in_=wa_raw[(a, b)][:].rearrange("p j (m t u) -> p t m j u", t=4, u=4),
+        def slot_views(a, b, grouped):
+            return (
+                grouped[:].rearrange("p (t m u) i -> p t m i u", t=4, u=4),
+                wa_raw[(a, b)][:].rearrange("p i (m t u) -> p t m i u", t=4, u=4),
             )
-            return wa_bf
 
-        def round_wa_on_scalar(a, b):
-            grouped = placed("wa_bf_last", [P, W, 4], BF16, 52 * KB)
-            by_t_out = grouped[:].rearrange("p (t m u) j -> p t m j u", t=4, u=4)
-            by_t_in = wa_raw[(a, b)][:].rearrange("p j (m t u) -> p t m j u", t=4, u=4)
-            for t in range(4):
-                nc.scalar.copy(by_t_out[:, t], by_t_in[:, t])
-            return grouped
+        def round_wa_on_vector(a, b, grouped, slots):
+            dst, src = slot_views(a, b, grouped)
+            nc.vector.tensor_copy(out=dst[:, slots], in_=src[:, slots])
 
-        def quantise_wa(a, b, grouped):
-            wa_codes[(a, b)] = held("wa_codes%d%d" % (a, b), [P, W], U32)
-            wa_sc[(a, b)] = held("wa_sc%d%d" % (a, b), [P, W], U8)
+        def round_wa_on_scalar(a, b, grouped, slots):
+            dst, src = slot_views(a, b, grouped)
+            for t in range(slots.start, slots.stop):
+                nc.scalar.copy(dst[:, t], src[:, t])
+
+        wa_codes = {}
+        wa_sc = {}
+        for a in range(2):
+            for b in range(2):
+                wa_codes[(a, b)] = held("wa_codes%d%d" % (a, b), [P, W], U32)
+                wa_sc[(a, b)] = held("wa_sc%d%d" % (a, b), [P, W], U8)
+
+        def quantise_wa(a, b, grouped, slots):
+            cols = slice(P * slots.start, P * slots.stop)
             nc.vector.quantize_mx(
-                out=wa_codes[(a, b)][:].bitcast(FP8X4),
-                scales=wa_sc[(a, b)][:],
-                in_=grouped[:].rearrange("p c j -> p (c j)"),
+                out=wa_codes[(a, b)][:, cols].bitcast(FP8X4),
+                scales=wa_sc[(a, b)][:, cols],
+                in_=grouped[:, cols, :].rearrange("p c i -> p (c i)"),
             )
 
         rates = {}
@@ -204,12 +222,13 @@ def tile_list_electrode_node_currents_kernel(
                 for j in range(HALVES):
                     name = "rate_%s%d%d" % (kind, b, j)
                     if (kind, b, j) == ("a", 0, 0):
-                        rates[(kind, b, j)] = placed(name, [P, 4, W], F32, 52 * KB)
+                        rates[(kind, b, j)] = placed(name, [P, 4, W], F32, AT_FIRST_ANODIC)
                     else:
                         rates[(kind, b, j)] = held(name, [P, 4, W], F32)
 
-        def exponent_pass(bank, kind, b, j, t, a, part=slice(0, W)):
-            cols = slice(j * W + part.start, j * W + part.stop)
+        whole = slice(0, W)
+
+        def exponent_pass(bank, kind, b, j, t, a, part):
             if kind == "a":
                 lhs = wa_codes[(a, b)][:, P * t : P * (t + 1)].bitcast(FP8X4)
                 lhs_sc = wa_sc[(a, b)][:, P * t : P * (t + 1)]
@@ -221,35 +240,32 @@ def tile_list_electrode_node_currents_kernel(
                 lhsT=lhs,
                 lhsT_scale=lhs_sc,
                 rhs=v_codes[(a, j)][:, part].bitcast(FP8X4),
-                rhs_scale=v_scales[a][:, cols],
+                rhs_scale=v_scales[a][:, j * W + part.start : j * W + part.stop],
                 start=(a == 0),
                 stop=(a == 1),
             )
 
-        def exponential(bank, kind, b, j, t, part=slice(0, W)):
+        def exponential(bank, kind, b, j, t, part):
             nc.scalar.activation(
                 rates[(kind, b, j)][:, t, part], bank[:, part], ACT.Exp, bias=ln_i0[:, 4 * b + t : 4 * b + t + 1]
             )
 
         first = [("c", 0, j, t) for j in range(HALVES) for t in range(4)]
-        for n, g in enumerate(first):
-            exponent_pass(banks[n], *g, 0)
-        for n, g in enumerate(first):
-            exponent_pass(banks[n], *g, 1)
-            exponential(banks[n], *g)
+        for bank, group in zip(banks, first):
+            exponent_pass(bank, *group, 0, whole)
+        for bank, group in zip(banks, first):
+            exponent_pass(bank, *group, 1, whole)
+            exponential(bank, *group, whole)
 
-        def rate_tiles(kind, b, j, slots, on, part=slice(0, W)):
-            for t, n in zip(slots, on):
-                bank = banks[n]
+        def rate_tiles(kind, b, j, first_bank, part):
+            for t in range(4):
+                bank = banks[first_bank + t]
                 exponent_pass(bank, kind, b, j, t, 0, part)
                 exponent_pass(bank, kind, b, j, t, 1, part)
                 exponential(bank, kind, b, j, t, part)
 
-        spans = [(0, 512, (4, 5)), (512, 256, (6, 7)), (768, 256, (0, 1))]
-
         def leak(s):
-            first_col, width, on = spans[s]
-            cols = slice(first_col, first_col + width)
+            first_col, width, on = SPANS[s]
             j, at = divmod(first_col, W)
             for c in range(2):
                 for a in range(2):
@@ -258,21 +274,21 @@ def tile_list_electrode_node_currents_kernel(
                         lhsT=wd_codes[:, a, P * c : P * (c + 1)].bitcast(FP8X4),
                         lhsT_scale=wd_sc[:, a, P * c : P * (c + 1)],
                         rhs=v_codes[(a, j)][:, at : at + width].bitcast(FP8X4),
-                        rhs_scale=v_scales[a][:, cols],
+                        rhs_scale=v_scales[a][:, first_col : first_col + width],
                         start=(a == 0),
                         stop=False,
                     )
 
-        h_bf = [placed("h_bf0", [P, S, 4], BF16, 0)]
+        h_bf = [placed("h_bf0", [P, S, 4], BF16, AT_WA[(0, 1)])]
         h_codes = [held("h_codes%d" % b, [P, S], U32) for b in range(2)]
         h_sc = [held("h_sc%d" % b, [P, S], U8) for b in range(2)]
 
         def net_rate(b, first_col, width):
             j, at = divmod(first_col, W)
             nc.vector.tensor_tensor(
-                h_bf[b][:, first_col : first_col + width, :].rearrange("p (c i) t -> p c t i", i=4),
-                rates[("a", b, j)][:, :, at : at + width].rearrange("p t (c i) -> p c t i", i=4),
-                rates[("c", b, j)][:, :, at : at + width].rearrange("p t (c i) -> p c t i", i=4),
+                h_bf[b][:, first_col : first_col + width, :].rearrange("p (c x) t -> p c t x", x=4),
+                rates[("a", b, j)][:, :, at : at + width].rearrange("p t (c x) -> p c t x", x=4),
+                rates[("c", b, j)][:, :, at : at + width].rearrange("p t (c x) -> p c t x", x=4),
                 ALU.subtract,
             )
 
@@ -288,22 +304,23 @@ def tile_list_electrode_node_currents_kernel(
         w2_sc = held("w2_sc", [P, 2, N], U8)
 
         def quantise_w2():
-            grouped = placed("w2_bf", [P, 2, N, 4], BF16, 52 * KB)
+            w2_bf = held("w2_bf", [P, 2, N, 4], BF16)
             for b in range(2):
                 nc.vector.tensor_tensor(
-                    grouped[:, b, :, :].rearrange("p (c i) t -> p c t i", i=4),
-                    w2_raw[:, b, :, :].rearrange("p t (c i) -> p c t i", i=4),
-                    sgn[:, 4 * b : 4 * b + 4].unsqueeze(1).unsqueeze(3).to_broadcast([P, N // 4, 4, 4]),
+                    w2_bf[:, b, :, :].rearrange("p (c x) t -> p c t x", x=4),
+                    w2_raw[:, b, :, :].rearrange("p t (c x) -> p c t x", x=4),
+                    i0_sign[:, 4 * b : 4 * b + 4].unsqueeze(1).unsqueeze(3).to_broadcast([P, N // 4, 4, 4]),
                     ALU.mult,
                 )
-            nc.vector.quantize_mx(
-                out=w2_codes[:].rearrange("p b n -> p (b n)").bitcast(FP8X4),
-                scales=w2_sc[:].rearrange("p b n -> p (b n)"),
-                in_=grouped[:].rearrange("p b n t -> p (b n t)"),
-            )
+            for b in range(2):
+                nc.vector.quantize_mx(
+                    out=w2_codes[:, b, :].bitcast(FP8X4),
+                    scales=w2_sc[:, b, :],
+                    in_=w2_bf[:, b, :, :].rearrange("p n t -> p (n t)"),
+                )
 
         def collect(b, s):
-            first_col, width, on = spans[s]
+            first_col, width, on = SPANS[s]
             cols = slice(first_col, first_col + width)
             for c in range(2):
                 nc.tensor.matmul_mx(
@@ -317,7 +334,7 @@ def tile_list_electrode_node_currents_kernel(
                 )
 
         def finish(s, c, on_vector):
-            first_col, width, on = spans[s]
+            first_col, width, on = SPANS[s]
             result = held("result%d%d" % (s, c), [P, width], F32)
             total = banks[on[c]][:, 0:width]
             if on_vector:
@@ -326,43 +343,40 @@ def tile_list_electrode_node_currents_kernel(
                 nc.scalar.activation(result[:], total, ACT.Identity, bias=bo_sb[:, c : c + 1])
             nc.sync.dma_start(out=out[P * c : P * (c + 1), first_col : first_col + width], in_=result[:])
 
-        rate_tiles("c", 1, 0, [0], [0])
-        quantise_wa(0, 0, round_wa_on_vector(0, 0))
-        quantise_wa(1, 0, round_wa_on_vector(1, 0))
-        rate_tiles("a", 0, 0, range(4), [1, 2, 3, 4])
-        quantise_wa(0, 1, round_wa_on_vector(0, 1))
-        rate_tiles("a", 0, 1, range(4), [5, 6, 7, 0])
+        all_slots, low_slots, high_slots = slice(0, 4), slice(0, 2), slice(2, 4)
+        round_wa_on_vector(0, 0, wa_bf, all_slots)
+        quantise_wa(0, 0, wa_bf, all_slots)
+        for slots in (low_slots, high_slots):
+            round_wa_on_vector(1, 0, wa_bf, slots)
+            quantise_wa(1, 0, wa_bf, slots)
+        rate_tiles("a", 0, 0, 0, whole)
+        round_wa_on_vector(0, 1, wa_bf, all_slots)
+        quantise_wa(0, 1, wa_bf, all_slots)
+        rate_tiles("a", 0, 1, 4, whole)
         net_rate(0, 0, W)
-        wa_last = round_wa_on_scalar(1, 1)
+        wa_bf_last = placed("wa_bf_last", [P, W, 4], BF16, AT_FIRST_ANODIC)
+        round_wa_on_scalar(1, 1, wa_bf_last, low_slots)
+        round_wa_on_vector(1, 1, wa_bf_last, high_slots)
         quantise_h(0, 0, W)
         net_rate(0, W, W)
-        quantise_wa(1, 1, wa_last)
+        quantise_wa(1, 1, wa_bf_last, all_slots)
         quantise_h(0, W, W)
-        rate_tiles("c", 1, 0, [1, 2, 3], [1, 2, 3])
+        rate_tiles("c", 1, 0, 0, whole)
         leak(0)
         leak(1)
         quantise_w2()
-        h_bf.append(placed("h_bf1", [P, S, 4], BF16, 52 * KB))
-        rate_tiles("a", 1, 0, range(4), range(4))
-        rate_tiles("c", 1, 1, range(4), range(4))
+        h_bf.append(placed("h_bf1", [P, S, 4], BF16, AT_WA[(0, 0)]))
+        rate_tiles("a", 1, 0, 0, whole)
+        rate_tiles("c", 1, 1, 0, whole)
         collect(0, 0)
         collect(0, 1)
-        rate_tiles("a", 1, 1, range(4), range(4), slice(0, 256))
-        rate_tiles("a", 1, 1, range(4), range(4), slice(256, 512))
+        for first_col, width, on in SPANS[1:]:
+            rate_tiles("a", 1, 1, 0, slice(first_col - W, first_col - W + width))
         leak(2)
         collect(0, 2)
-        net_rate(1, 0, W)
-        quantise_h(1, 0, W)
-        collect(1, 0)
-        finish(0, 0, False)
-        finish(0, 1, False)
-        net_rate(1, 512, 256)
-        quantise_h(1, 512, 256)
-        collect(1, 1)
-        finish(1, 0, False)
-        finish(1, 1, False)
-        net_rate(1, 768, 256)
-        quantise_h(1, 768, 256)
-        collect(1, 2)
-        finish(2, 0, False)
-        finish(2, 1, True)
+        for s, (first_col, width, on) in enumerate(SPANS):
+            net_rate(1, first_col, width)
+            quantise_h(1, first_col, width)
+            collect(1, s)
+            finish(s, 0, False)
+            finish(s, 1, s == len(SPANS) - 1)

@@ -29,18 +29,19 @@ AT_WA = {
     (0, 1): 0,
     (1, 1): 16 * KB,
 }
-AT_BO = 8 * KB
-AT_WD_SCALES = 8 * KB + 64
-AT_WD_CODES = 24 * KB
 AT_WC_RAW = 32 * KB
 AT_TABLE_SCALES = 40 * KB
-AT_FIRST_ANODIC = 52 * KB
 AT_WC_SCALES_RAW = 60 * KB
 
 PASS_ROW_SHIFT = 16
-LIVE_ROWS = 100
 
-SPANS = ((0, 512, (4, 5)), (512, 256, (6, 7)), (768, 256, (0, 1)))
+SPANS = (
+    (0, 256, ((0, 0), (0, 256))),
+    (256, 256, ((1, 0), (1, 256))),
+    (512, 256, ((2, 0), (2, 256))),
+    (768, 128, ((3, 0), (3, 128))),
+    (896, 128, ((4, 0), (5, 0))),
+)
 
 
 def tile_list_electrode_node_currents_kernel(
@@ -100,6 +101,8 @@ def tile_list_electrode_node_currents_kernel(
         load_table(1)
         v_scales1 = held("v_scales1", [P, S], U8)
         nc.vector.memset(v_scales1[:].bitcast(I32), 0)
+        wd_sc = held("wd_sc", [P, 2, N], U8)
+        nc.vector.memset(wd_sc[:].bitcast(I32), 0)
 
         wc_codes = held("wc_codes", [P, 4, 4, 256], U8)
         nc.vector.tensor_copy(
@@ -109,10 +112,11 @@ def tile_list_electrode_node_currents_kernel(
 
         v_scales0 = held("v_scales0", [P, S], U8)
         nc.vector.tensor_copy(v_scales0[:], table_scales[:].indirect(offsets[:]))
-        nc.sync.dma_start(
-            out=v_scales1[0:LIVE_ROWS, :].bitcast(I32),
-            in_=v_scales0[PASS_ROW_SHIFT : PASS_ROW_SHIFT + LIVE_ROWS, :].bitcast(I32),
-        )
+        for e in range(4):
+            nc.sync.dma_start(
+                out=v_scales1[e:P:32, :].bitcast(I32),
+                in_=v_scales0[PASS_ROW_SHIFT + e : P : 32, :].bitcast(I32),
+            )
         v_scales = [v_scales0, v_scales1]
 
         i0_masked = held("i0_masked", [P, 8, 4], F32)
@@ -169,20 +173,18 @@ def tile_list_electrode_node_currents_kernel(
         load_wa(0, 0)
         load_wa(1, 0)
         load_wa(0, 1)
-        bo_sb = placed("bo_sb", [P, 2], F32, AT_BO)
-        with nc.allow_non_contiguous_dma(reason="one bias a partition"):
-            nc.sync.dma_start(out=bo_sb[:], in_=bo.rearrange("(c p) -> p c", p=P))
-        wd_sc = placed("wd_sc", [P, 2, N], U8, AT_WD_SCALES)
-        nc.vector.memset(wd_sc[:].bitcast(I32), 0)
-        load_scale_rows(wd_sc, wd_scales)
         load_wa(1, 1)
-        wd_codes = placed("wd_codes", [P, 2, N], I32, AT_WD_CODES)
-        nc.sync.dma_start(out=wd_codes[:], in_=wd_words.rearrange("a p c i -> p a (c i)").bitcast(I32))
         w2_raw = placed("w2_raw", [P, 2, 4, N], F32, AT_WA[(0, 0)])
         w2_rows = w2.rearrange("(b m t u) n -> b t m u n", b=2, t=4, u=4)
         for b in range(2):
             for t in range(4):
                 nc.sync.dma_start(out=w2_raw[:, b, t, :], in_=w2_rows[b, t])
+        wd_codes = held("wd_codes", [P, 2, N], I32)
+        nc.sync.dma_start(out=wd_codes[:], in_=wd_words.rearrange("a p c i -> p a (c i)").bitcast(I32))
+        load_scale_rows(wd_sc, wd_scales)
+        bo_sb = held("bo_sb", [P, 2], F32)
+        with nc.allow_non_contiguous_dma(reason="one bias a partition"):
+            nc.sync.dma_start(out=bo_sb[:], in_=bo.rearrange("(c p) -> p c", p=P))
 
         wa_bf = held("wa_bf", [P, W, 4], BF16)
 
@@ -221,14 +223,9 @@ def tile_list_electrode_node_currents_kernel(
             for b in range(2):
                 for j in range(HALVES):
                     name = "rate_%s%d%d" % (kind, b, j)
-                    if (kind, b, j) == ("a", 0, 0):
-                        rates[(kind, b, j)] = placed(name, [P, 4, W], F32, AT_FIRST_ANODIC)
-                    else:
-                        rates[(kind, b, j)] = held(name, [P, 4, W], F32)
+                    rates[(kind, b, j)] = held(name, [P, 4, W], F32)
 
-        whole = slice(0, W)
-
-        def exponent_pass(bank, kind, b, j, t, a, part):
+        def exponent_pass(bank, kind, b, j, t, a):
             if kind == "a":
                 lhs = wa_codes[(a, b)][:, P * t : P * (t + 1)].bitcast(FP8X4)
                 lhs_sc = wa_sc[(a, b)][:, P * t : P * (t + 1)]
@@ -236,147 +233,172 @@ def tile_list_electrode_node_currents_kernel(
                 lhs = wc_codes[:, 2 * a + b, t, :].bitcast(FP4X4)
                 lhs_sc = wc_sc[:, 2 * a + b, t, :]
             nc.tensor.matmul_mx(
-                out=bank[:, part],
+                out=bank[:],
                 lhsT=lhs,
                 lhsT_scale=lhs_sc,
-                rhs=v_codes[(a, j)][:, part].bitcast(FP8X4),
-                rhs_scale=v_scales[a][:, j * W + part.start : j * W + part.stop],
+                rhs=v_codes[(a, j)][:].bitcast(FP8X4),
+                rhs_scale=v_scales[a][:, j * W : (j + 1) * W],
                 start=(a == 0),
                 stop=(a == 1),
             )
 
-        def exponential(bank, kind, b, j, t, part):
-            nc.scalar.activation(
-                rates[(kind, b, j)][:, t, part], bank[:, part], ACT.Exp, bias=ln_i0[:, 4 * b + t : 4 * b + t + 1]
-            )
-
-        first = [("c", 0, j, t) for j in range(HALVES) for t in range(4)]
-        for bank, group in zip(banks, first):
-            exponent_pass(bank, *group, 0, whole)
-        for bank, group in zip(banks, first):
-            exponent_pass(bank, *group, 1, whole)
-            exponential(bank, *group, whole)
-
-        def rate_tiles(kind, b, j, first_bank, part):
+        def exponents(kind, b, j, first_bank, passes):
             for t in range(4):
-                bank = banks[first_bank + t]
-                exponent_pass(bank, kind, b, j, t, 0, part)
-                exponent_pass(bank, kind, b, j, t, 1, part)
-                exponential(bank, kind, b, j, t, part)
+                for a in passes:
+                    exponent_pass(banks[first_bank + t], kind, b, j, t, a)
+
+        def exponentials(kind, b, j, first_bank, at, width):
+            for t in range(4):
+                nc.scalar.activation(
+                    rates[(kind, b, j)][:, t, at : at + width],
+                    banks[first_bank + t][:, at : at + width],
+                    ACT.Exp,
+                    bias=ln_i0[:, 4 * b + t : 4 * b + t + 1],
+                )
+
+        def rate_tiles(kind, b, j, first_bank):
+            exponents(kind, b, j, first_bank, (0, 1))
+            exponentials(kind, b, j, first_bank, 0, W)
+
+        def span_sum(s, c):
+            first_col, width, places = SPANS[s]
+            bank, at = places[c]
+            return banks[bank][:, at : at + width]
+
+        def shares_bank(s):
+            places = SPANS[s][2]
+            return places[0][0] == places[1][0]
 
         def leak(s):
-            first_col, width, on = SPANS[s]
+            first_col, width, places = SPANS[s]
             j, at = divmod(first_col, W)
             for c in range(2):
                 for a in range(2):
                     nc.tensor.matmul_mx(
-                        out=banks[on[c]][:, 0:width],
+                        out=span_sum(s, c),
                         lhsT=wd_codes[:, a, P * c : P * (c + 1)].bitcast(FP8X4),
                         lhsT_scale=wd_sc[:, a, P * c : P * (c + 1)],
                         rhs=v_codes[(a, j)][:, at : at + width].bitcast(FP8X4),
                         rhs_scale=v_scales[a][:, first_col : first_col + width],
-                        start=(a == 0),
+                        start=(a == 0 and (c == 0 or not shares_bank(s))),
                         stop=False,
                     )
 
-        h_bf = [placed("h_bf0", [P, S, 4], BF16, AT_WA[(0, 1)])]
         h_codes = [held("h_codes%d" % b, [P, S], U32) for b in range(2)]
         h_sc = [held("h_sc%d" % b, [P, S], U8) for b in range(2)]
+        h_bf = {}
 
         def net_rate(b, first_col, width):
             j, at = divmod(first_col, W)
             nc.vector.tensor_tensor(
-                h_bf[b][:, first_col : first_col + width, :].rearrange("p (c x) t -> p c t x", x=4),
+                h_bf[(b, j)][:, at : at + width, :].rearrange("p (c x) t -> p c t x", x=4),
                 rates[("a", b, j)][:, :, at : at + width].rearrange("p t (c x) -> p c t x", x=4),
                 rates[("c", b, j)][:, :, at : at + width].rearrange("p t (c x) -> p c t x", x=4),
                 ALU.subtract,
             )
 
         def quantise_h(b, first_col, width):
+            j, at = divmod(first_col, W)
             cols = slice(first_col, first_col + width)
             nc.vector.quantize_mx(
                 out=h_codes[b][:, cols].bitcast(FP8X4),
                 scales=h_sc[b][:, cols],
-                in_=h_bf[b][:, cols, :].rearrange("p c t -> p (c t)"),
+                in_=h_bf[(b, j)][:, at : at + width, :].rearrange("p c t -> p (c t)"),
             )
 
-        w2_codes = held("w2_codes", [P, 2, N], U32)
-        w2_sc = held("w2_sc", [P, 2, N], U8)
+        w2_bf = held("w2_bf", [P, 2, N, 4], BF16)
+        w2_codes = held("w2_codes", [P, 2 * N], U32)
+        w2_sc = held("w2_sc", [P, 2 * N], U8)
+
+        def round_w2(b):
+            nc.vector.tensor_tensor(
+                w2_bf[:, b, :, :].rearrange("p (c x) t -> p c t x", x=4),
+                w2_raw[:, b, :, :].rearrange("p t (c x) -> p c t x", x=4),
+                i0_sign[:, 4 * b : 4 * b + 4].unsqueeze(1).unsqueeze(3).to_broadcast([P, N // 4, 4, 4]),
+                ALU.mult,
+            )
 
         def quantise_w2():
-            w2_bf = held("w2_bf", [P, 2, N, 4], BF16)
-            for b in range(2):
-                nc.vector.tensor_tensor(
-                    w2_bf[:, b, :, :].rearrange("p (c x) t -> p c t x", x=4),
-                    w2_raw[:, b, :, :].rearrange("p t (c x) -> p c t x", x=4),
-                    i0_sign[:, 4 * b : 4 * b + 4].unsqueeze(1).unsqueeze(3).to_broadcast([P, N // 4, 4, 4]),
-                    ALU.mult,
-                )
-            for b in range(2):
-                nc.vector.quantize_mx(
-                    out=w2_codes[:, b, :].bitcast(FP8X4),
-                    scales=w2_sc[:, b, :],
-                    in_=w2_bf[:, b, :, :].rearrange("p n t -> p (n t)"),
-                )
+            nc.vector.quantize_mx(
+                out=w2_codes[:].bitcast(FP8X4),
+                scales=w2_sc[:],
+                in_=w2_bf[:].rearrange("p b n t -> p (b n t)"),
+            )
 
         def collect(b, s):
-            first_col, width, on = SPANS[s]
+            first_col, width, places = SPANS[s]
             cols = slice(first_col, first_col + width)
             for c in range(2):
+                rows = slice(N * b + P * c, N * b + P * (c + 1))
                 nc.tensor.matmul_mx(
-                    out=banks[on[c]][:, 0:width],
-                    lhsT=w2_codes[:, b, P * c : P * (c + 1)].bitcast(FP8X4),
-                    lhsT_scale=w2_sc[:, b, P * c : P * (c + 1)],
+                    out=span_sum(s, c),
+                    lhsT=w2_codes[:, rows].bitcast(FP8X4),
+                    lhsT_scale=w2_sc[:, rows],
                     rhs=h_codes[b][:, cols].bitcast(FP8X4),
                     rhs_scale=h_sc[b][:, cols],
                     start=False,
-                    stop=(b == 1),
+                    stop=(b == 1 and (c == 1 or not shares_bank(s))),
                 )
 
-        def finish(s, c, on_vector):
-            first_col, width, on = SPANS[s]
-            result = held("result%d%d" % (s, c), [P, width], F32)
-            total = banks[on[c]][:, 0:width]
-            if on_vector:
-                nc.vector.tensor_scalar(result[:], total, bo_sb[:, c : c + 1], None, ALU.add)
-            else:
-                nc.scalar.activation(result[:], total, ACT.Identity, bias=bo_sb[:, c : c + 1])
-            nc.sync.dma_start(out=out[P * c : P * (c + 1), first_col : first_col + width], in_=result[:])
+        out_by_c = out.rearrange("(c p) j -> p c j", p=P)
 
+        def finish(s):
+            first_col, width, places = SPANS[s]
+            result = held("result%d" % s, [P, 2, width], F32)
+            for c in range(2):
+                if c == 1 and s == len(SPANS) - 1:
+                    nc.vector.tensor_scalar(result[:, c, :], span_sum(s, c), bo_sb[:, c : c + 1], None, ALU.add)
+                else:
+                    nc.scalar.activation(result[:, c, :], span_sum(s, c), ACT.Identity, bias=bo_sb[:, c : c + 1])
+            nc.sync.dma_start(out=out_by_c[:, :, first_col : first_col + width], in_=result[:])
+
+        for a in range(2):
+            for j in range(HALVES):
+                exponents("c", 0, j, 4 * j, (a,))
+        for j in range(HALVES):
+            exponentials("c", 0, j, 4 * j, 0, W)
         all_slots, low_slots, high_slots = slice(0, 4), slice(0, 2), slice(2, 4)
         round_wa_on_vector(0, 0, wa_bf, all_slots)
         quantise_wa(0, 0, wa_bf, all_slots)
         for slots in (low_slots, high_slots):
             round_wa_on_vector(1, 0, wa_bf, slots)
+        for slots in (low_slots, high_slots):
             quantise_wa(1, 0, wa_bf, slots)
-        rate_tiles("a", 0, 0, 0, whole)
+        exponents("a", 0, 0, 0, (0,))
+        exponents("a", 0, 0, 0, (1,))
+        exponentials("a", 0, 0, 0, 0, W)
         round_wa_on_vector(0, 1, wa_bf, all_slots)
         quantise_wa(0, 1, wa_bf, all_slots)
-        rate_tiles("a", 0, 1, 4, whole)
+        rate_tiles("a", 0, 1, 4)
+        h_bf[(0, 0)] = placed("h_bf00", [P, W, 4], BF16, AT_WA[(0, 1)])
+        h_bf[(0, 1)] = held("h_bf01", [P, W, 4], BF16)
         net_rate(0, 0, W)
-        wa_bf_last = placed("wa_bf_last", [P, W, 4], BF16, AT_FIRST_ANODIC)
+        wa_bf_last = held("wa_bf_last", [P, W, 4], BF16)
         round_wa_on_scalar(1, 1, wa_bf_last, low_slots)
         round_wa_on_vector(1, 1, wa_bf_last, high_slots)
         quantise_h(0, 0, W)
         net_rate(0, W, W)
         quantise_wa(1, 1, wa_bf_last, all_slots)
         quantise_h(0, W, W)
-        rate_tiles("c", 1, 0, 0, whole)
-        leak(0)
-        leak(1)
+        rate_tiles("c", 1, 0, 0)
+        rate_tiles("c", 1, 1, 4)
+        for b in range(2):
+            round_w2(b)
+        h_bf[(1, 0)] = placed("h_bf10", [P, W, 4], BF16, AT_WA[(0, 0)])
+        h_bf[(1, 1)] = held("h_bf11", [P, W, 4], BF16)
+        exponents("a", 1, 0, 0, (0, 1))
+        exponents("a", 1, 1, 4, (0, 1))
+        for first_col, width, places in SPANS:
+            j, at = divmod(first_col, W)
+            exponentials("a", 1, j, 4 * j, at, width)
+        net_rate(1, SPANS[0][0], SPANS[0][1])
         quantise_w2()
-        h_bf.append(placed("h_bf1", [P, S, 4], BF16, AT_WA[(0, 0)]))
-        rate_tiles("a", 1, 0, 0, whole)
-        rate_tiles("c", 1, 1, 0, whole)
-        collect(0, 0)
-        collect(0, 1)
-        for first_col, width, on in SPANS[1:]:
-            rate_tiles("a", 1, 1, 0, slice(first_col - W, first_col - W + width))
-        leak(2)
-        collect(0, 2)
-        for s, (first_col, width, on) in enumerate(SPANS):
-            net_rate(1, first_col, width)
+        for s in range(len(SPANS)):
+            leak(s)
+            collect(0, s)
+        for s, (first_col, width, places) in enumerate(SPANS):
+            if s + 1 < len(SPANS):
+                net_rate(1, SPANS[s + 1][0], SPANS[s + 1][1])
             quantise_h(1, first_col, width)
             collect(1, s)
-            finish(s, 0, False)
-            finish(s, 1, s == len(SPANS) - 1)
+            finish(s)

@@ -85,11 +85,9 @@ def tile_list_electrode_node_currents_kernel(
             nc.sync.dma_start(out=table_scales[e:P:PASS_ROW_SHIFT, :].bitcast(I32), in_=rows_by_e[e])
 
         def load_scale_rows(planes, src):
-            for g in range(4):
-                nc.sync.dma_start(
-                    out=planes[32 * g : 32 * g + 4, :, :].bitcast(I32),
-                    in_=src[:, 4 * g : 4 * g + 4, :].rearrange("a e n -> e a n").bitcast(I32),
-                )
+            src_by_e = src.rearrange("a (g e) n -> e g a n", e=4).bitcast(I32)
+            for e in range(4):
+                nc.sync.dma_start(out=planes[e:P:32, :, :].bitcast(I32), in_=src_by_e[e])
 
         table = [placed("table%d" % a, [P, T], I32, AT_TABLE[a]) for a in range(2)]
 
@@ -200,8 +198,7 @@ def tile_list_electrode_node_currents_kernel(
 
         def round_wa_on_scalar(a, b, grouped, slots):
             dst, src = slot_views(a, b, grouped)
-            for t in range(slots.start, slots.stop):
-                nc.scalar.copy(dst[:, t], src[:, t])
+            nc.scalar.copy(dst[:, slots], src[:, slots])
 
         wa_codes = {}
         wa_sc = {}
@@ -223,7 +220,10 @@ def tile_list_electrode_node_currents_kernel(
             for b in range(2):
                 for j in range(HALVES):
                     name = "rate_%s%d%d" % (kind, b, j)
-                    rates[(kind, b, j)] = held(name, [P, 4, W], F32)
+                    if (kind, b, j) == ("c", 1, 0):
+                        rates[(kind, b, j)] = placed(name, [P, 4, W], F32, AT_WA[(1, 1)])
+                    else:
+                        rates[(kind, b, j)] = held(name, [P, 4, W], F32)
 
         def exponent_pass(bank, kind, b, j, t, a):
             if kind == "a":
@@ -366,16 +366,18 @@ def tile_list_electrode_node_currents_kernel(
             quantise_wa(1, 0, wa_bf, slots)
         exponents("a", 0, 0, 0, (0,))
         exponents("a", 0, 0, 0, (1,))
-        exponentials("a", 0, 0, 0, 0, W)
+        for at in (0, W // 2):
+            exponentials("a", 0, 0, 0, at, W // 2)
         round_wa_on_vector(0, 1, wa_bf, all_slots)
         quantise_wa(0, 1, wa_bf, all_slots)
         rate_tiles("a", 0, 1, 4)
         h_bf[(0, 0)] = placed("h_bf00", [P, W, 4], BF16, AT_WA[(0, 1)])
         h_bf[(0, 1)] = held("h_bf01", [P, W, 4], BF16)
-        net_rate(0, 0, W)
+        for at in (0, W // 2):
+            net_rate(0, at, W // 2)
         wa_bf_last = held("wa_bf_last", [P, W, 4], BF16)
-        round_wa_on_scalar(1, 1, wa_bf_last, low_slots)
-        round_wa_on_vector(1, 1, wa_bf_last, high_slots)
+        round_wa_on_scalar(1, 1, wa_bf_last, slice(0, 3))
+        round_wa_on_vector(1, 1, wa_bf_last, slice(3, 4))
         quantise_h(0, 0, W)
         net_rate(0, W, W)
         quantise_wa(1, 1, wa_bf_last, all_slots)

@@ -31,6 +31,8 @@ AT_WA = {
 }
 AT_WC_RAW = 32 * KB
 AT_TABLE_SCALES = 40 * KB
+AT_W2 = 8 * KB
+AT_WA_BF_LAST = 52 * KB
 AT_WC_SCALES_RAW = 60 * KB
 
 PASS_ROW_SHIFT = 16
@@ -170,13 +172,13 @@ def tile_list_electrode_node_currents_kernel(
 
         load_wa(0, 0)
         load_wa(1, 0)
-        load_wa(0, 1)
-        load_wa(1, 1)
-        w2_raw = placed("w2_raw", [P, 2, 4, N], F32, AT_WA[(0, 0)])
+        w2_raw = placed("w2_raw", [P, 2, 4, N], F32, AT_W2)
         w2_rows = w2.rearrange("(b m t u) n -> b t m u n", b=2, t=4, u=4)
         for b in range(2):
             for t in range(4):
                 nc.sync.dma_start(out=w2_raw[:, b, t, :], in_=w2_rows[b, t])
+        load_wa(0, 1)
+        load_wa(1, 1)
         wd_codes = held("wd_codes", [P, 2, N], I32)
         nc.sync.dma_start(out=wd_codes[:], in_=wd_words.rearrange("a p c i -> p a (c i)").bitcast(I32))
         load_scale_rows(wd_sc, wd_scales)
@@ -220,7 +222,7 @@ def tile_list_electrode_node_currents_kernel(
             for b in range(2):
                 for j in range(HALVES):
                     name = "rate_%s%d%d" % (kind, b, j)
-                    if (kind, b, j) == ("c", 1, 0):
+                    if (kind, b, j) == ("c", 1, 1):
                         rates[(kind, b, j)] = placed(name, [P, 4, W], F32, AT_WA[(1, 1)])
                     else:
                         rates[(kind, b, j)] = held(name, [P, 4, W], F32)
@@ -368,25 +370,28 @@ def tile_list_electrode_node_currents_kernel(
         exponents("a", 0, 0, 0, (1,))
         for at in (0, W // 2):
             exponentials("a", 0, 0, 0, at, W // 2)
-        round_wa_on_vector(0, 1, wa_bf, all_slots)
-        quantise_wa(0, 1, wa_bf, all_slots)
-        rate_tiles("a", 0, 1, 4)
-        h_bf[(0, 0)] = placed("h_bf00", [P, W, 4], BF16, AT_WA[(0, 1)])
-        h_bf[(0, 1)] = held("h_bf01", [P, W, 4], BF16)
-        for at in (0, W // 2):
-            net_rate(0, at, W // 2)
-        wa_bf_last = held("wa_bf_last", [P, W, 4], BF16)
-        round_wa_on_scalar(1, 1, wa_bf_last, slice(0, 3))
-        round_wa_on_vector(1, 1, wa_bf_last, slice(3, 4))
-        quantise_h(0, 0, W)
-        net_rate(0, W, W)
-        quantise_wa(1, 1, wa_bf_last, all_slots)
-        quantise_h(0, W, W)
-        rate_tiles("c", 1, 0, 0)
-        rate_tiles("c", 1, 1, 4)
         for b in range(2):
             round_w2(b)
-        h_bf[(1, 0)] = placed("h_bf10", [P, W, 4], BF16, AT_WA[(0, 0)])
+        rate_tiles("a", 0, 1, 4)
+        h_bf[(0, 0)] = placed("h_bf00", [P, W, 4], BF16, AT_W2)
+        for at in (0, W // 2):
+            net_rate(0, at, W // 2)
+        round_wa_on_vector(0, 1, wa_bf, all_slots)
+        quantise_w2()
+        quantise_wa(0, 1, wa_bf, all_slots)
+        wa_bf_high = placed("wa_bf_high", [P, W, 4], BF16, AT_WA_BF_LAST)
+        round_wa_on_vector(1, 1, wa_bf_high, high_slots)
+        quantise_h(0, 0, W)
+        quantise_wa(1, 1, wa_bf_high, high_slots)
+        h_bf[(0, 1)] = placed("h_bf01", [P, W, 4], BF16, AT_WA_BF_LAST)
+        net_rate(0, W, W)
+        rate_tiles("c", 1, 0, 0)
+        wa_bf_low = held("wa_bf_low", [P, W, 4], BF16)
+        round_wa_on_scalar(1, 1, wa_bf_low, low_slots)
+        quantise_wa(1, 1, wa_bf_low, low_slots)
+        quantise_h(0, W, W)
+        rate_tiles("c", 1, 1, 4)
+        h_bf[(1, 0)] = held("h_bf10", [P, W, 4], BF16)
         h_bf[(1, 1)] = held("h_bf11", [P, W, 4], BF16)
         exponents("a", 1, 0, 0, (0, 1))
         exponents("a", 1, 1, 4, (0, 1))
@@ -394,7 +399,6 @@ def tile_list_electrode_node_currents_kernel(
             j, at = divmod(first_col, W)
             exponentials("a", 1, j, 4 * j, at, width)
         net_rate(1, SPANS[0][0], SPANS[0][1])
-        quantise_w2()
         for s in range(len(SPANS)):
             leak(s)
             collect(0, s)

@@ -2,6 +2,7 @@ import math
 from contextlib import ExitStack
 
 import concourse.mybir as mybir
+from concourse.masks import make_identity
 
 K, T, S, H, N = 1024, 4096, 1024, 1024, 256
 FLOPS = 2 * S * (2 * K * H + H * N + K * N)
@@ -24,18 +25,18 @@ KB = 1024
 
 AT_TABLE = (0, 16 * KB)
 AT_WA = {
-    (0, 0): 34 * KB,
-    (1, 0): 42 * KB,
+    (0, 0): 36 * KB,
+    (1, 0): 44 * KB,
     (0, 1): 0,
     (1, 1): 16 * KB,
 }
-AT_WC_RAW = 32 * KB
-AT_TABLE_SCALES = 40 * KB
+AT_WC_CODES = 32 * KB
+AT_WC_RAW = 36 * KB
+AT_TABLE_SCALES = 30 * KB
 AT_W2 = 8 * KB
 AT_WA_BF_LAST = 52 * KB
 AT_WC_SCALES_RAW = 60 * KB
 
-PASS_ROW_SHIFT = 16
 
 SPANS = (
     (0, 256, ((0, 0), (0, 256))),
@@ -65,26 +66,22 @@ def tile_list_electrode_node_currents_kernel(
         offsets = keep.tile([P, S // 16], U16, name="offsets")
         nc.sync.dma_start(offsets[:], offs)
 
-        lane = held("lane", [P, 4], I32)
-        nc.gpsimd.iota(lane[:], [[-1, 4]], base=4, channel_multiplier=1)
+        identity = held("identity", [P, P], F32)
+        make_identity(nc, identity[:])
         wc_raw = placed("wc_raw", [P, 2, 2 * H], U8, AT_WC_RAW)
         nc.sync.dma_start(out=wc_raw[:].bitcast(I32), in_=wc_words.rearrange("a p x -> p a x").bitcast(I32))
-        i0_runs = held("i0_runs", [P, 2, 16], F32)
-        i0_by_m = i0.rearrange("(b m x) -> b m x", b=2, x=16)
-        for b in range(2):
-            nc.sync.dma_start(out=i0_runs[:, b, :], in_=i0_by_m[b].unsqueeze(1).to_broadcast([32, 4, 16]))
+        i0_rows = held("i0_rows", [2, W], F32)
+        nc.sync.dma_start(out=i0_rows[:], in_=i0.rearrange("(b r) -> b r", b=2))
 
         table_scales = placed("table_scales", [P, T], U8, AT_TABLE_SCALES)
         nc.vector.memset(table_scales[:].bitcast(I32), 0)
-        lane_mod = held("lane_mod", [P, 4], I32)
-        nc.vector.tensor_scalar(lane_mod[:], lane[:], 3, None, ALU.bitwise_and)
         wc_scales_raw = placed("wc_scales_raw", [P, 2, H], U8, AT_WC_SCALES_RAW)
         nc.vector.memset(wc_scales_raw[:].bitcast(I32), 0)
-        own = held("own", [P, 4], F32)
-        nc.vector.tensor_scalar(own[:], lane_mod[:], 0.0, None, ALU.is_equal)
-        rows_by_e = tab_scales.rearrange("a (g e) t -> e g a t", e=4).bitcast(I32)
-        for e in range(4):
-            nc.sync.dma_start(out=table_scales[e:P:PASS_ROW_SHIFT, :].bitcast(I32), in_=rows_by_e[e])
+        i0_by_slot = held("i0_by_slot", [P, 4, P], F32)
+        nc.vector.memset(i0_by_slot[:], 0.0)
+        nc.sync.dma_start(
+            out=table_scales[0:P:4, :].bitcast(I32), in_=tab_scales.rearrange("a q t -> (a q) t").bitcast(I32)
+        )
 
         def load_scale_rows(planes, src):
             src_by_e = src.rearrange("a (g e) n -> e g a n", e=4).bitcast(I32)
@@ -96,38 +93,45 @@ def tile_list_electrode_node_currents_kernel(
         def load_table(a):
             nc.sync.dma_start(out=table[a][:], in_=tab_words[a].rearrange("p t i -> p (t i)").bitcast(I32))
 
-        load_table(0)
         load_scale_rows(wc_scales_raw, wc_scales)
-        load_table(1)
-        v_scales1 = held("v_scales1", [P, S], U8)
-        nc.vector.memset(v_scales1[:].bitcast(I32), 0)
+        load_table(0)
+        v_scales = [held("v_scales%d" % a, [P, S], U8) for a in range(2)]
+        for a in range(2):
+            nc.vector.memset(v_scales[a][:].bitcast(I32), 0)
         wd_sc = held("wd_sc", [P, 2, N], U8)
         nc.vector.memset(wd_sc[:].bitcast(I32), 0)
 
-        wc_codes = held("wc_codes", [P, 4, 4, 256], U8)
+        picked_scales = held("picked_scales", [P, S], U8)
+        nc.vector.tensor_copy(picked_scales[:], table_scales[:].indirect(offsets[:]))
+
+        def move_scale_rows(a, queue):
+            for e in range(4):
+                queue.dma_start(
+                    out=v_scales[a][e:P:32, :].bitcast(I32),
+                    in_=picked_scales[64 * a + 4 * e : 64 * (a + 1) : 16, :].bitcast(I32),
+                )
+
+        move_scale_rows(0, nc.sync)
+        load_table(1)
+        move_scale_rows(1, nc.sync)
+
+        wc_codes = placed("wc_codes", [P, 4, 4, 256], U8, AT_WC_CODES)
         nc.vector.tensor_copy(
             out=wc_codes[:].bitcast(I32).rearrange("p g t (m e) -> p g t m e", e=2),
             in_=wc_raw[:].bitcast(I32).rearrange("p a (b m t e) -> p (a b) t m e", b=2, t=4, e=2),
         )
 
-        v_scales0 = held("v_scales0", [P, S], U8)
-        nc.vector.tensor_copy(v_scales0[:], table_scales[:].indirect(offsets[:]))
-        for e in range(4):
-            nc.sync.dma_start(
-                out=v_scales1[e:P:32, :].bitcast(I32),
-                in_=v_scales0[PASS_ROW_SHIFT + e : P : 32, :].bitcast(I32),
-            )
-        v_scales = [v_scales0, v_scales1]
-
-        i0_masked = held("i0_masked", [P, 8, 4], F32)
-        nc.vector.tensor_tensor(
-            i0_masked[:],
-            i0_runs[:].rearrange("p b (t u) -> p (b t) u", u=4),
-            own[:].unsqueeze(1).to_broadcast([P, 8, 4]),
-            ALU.mult,
+        nc.scalar.copy(
+            i0_by_slot[0:2].rearrange("b t (m u) -> b t m u", u=4),
+            i0_rows[:].rearrange("b (m t u) -> b t m u", t=4, u=4),
         )
+        for t in range(4):
+            nc.tensor.transpose(banks[0][:, P * t : P * (t + 1)], i0_by_slot[:, t, :], identity[:])
         i0_sb = held("i0_sb", [P, 8], F32)
-        nc.vector.tensor_reduce(i0_sb[:], i0_masked[:], mybir.AxisListType.X, ALU.add)
+        nc.scalar.copy(
+            i0_sb[:].rearrange("p (b t) -> p b t", b=2),
+            banks[0][:].rearrange("p (t b) -> p b t", t=4)[:, 0:2, :],
+        )
         bits = i0_sb[:].bitcast(I32)
         mantissa = held("mantissa", [P, 8], I32)
         nc.vector.tensor_scalar(mantissa[:], bits, 0x007FFFFF, 0x3F800000, ALU.bitwise_and, ALU.bitwise_or)

@@ -83,9 +83,9 @@ def tile_list_electrode_node_currents_kernel(
             out=table_scales[0:P:4, :].bitcast(I32), in_=tab_scales.rearrange("a q t -> (a q) t").bitcast(I32)
         )
 
-        def load_scale_rows(planes, src):
+        def load_scale_rows(planes, src, rows=range(4)):
             src_by_e = src.rearrange("a (g e) n -> e g a n", e=4).bitcast(I32)
-            for e in range(4):
+            for e in rows:
                 nc.sync.dma_start(out=planes[e:P:32, :, :].bitcast(I32), in_=src_by_e[e])
 
         table = [placed("table%d" % a, [P, T], I32, AT_TABLE[a]) for a in range(2)]
@@ -93,8 +93,9 @@ def tile_list_electrode_node_currents_kernel(
         def load_table(a):
             nc.sync.dma_start(out=table[a][:], in_=tab_words[a].rearrange("p t i -> p (t i)").bitcast(I32))
 
-        load_scale_rows(wc_scales_raw, wc_scales)
+        load_scale_rows(wc_scales_raw, wc_scales, range(3))
         load_table(0)
+        load_scale_rows(wc_scales_raw, wc_scales, range(3, 4))
         v_scales = [held("v_scales%d" % a, [P, S], U8) for a in range(2)]
         for a in range(2):
             nc.vector.memset(v_scales[a][:].bitcast(I32), 0)
@@ -366,10 +367,11 @@ def tile_list_electrode_node_currents_kernel(
         all_slots, low_slots, high_slots = slice(0, 4), slice(0, 2), slice(2, 4)
         round_wa_on_vector(0, 0, wa_bf, all_slots)
         quantise_wa(0, 0, wa_bf, all_slots)
-        for slots in (low_slots, high_slots):
-            round_wa_on_vector(1, 0, wa_bf, slots)
-        for slots in (low_slots, high_slots):
-            quantise_wa(1, 0, wa_bf, slots)
+        for t in range(5):
+            if t < 4:
+                round_wa_on_vector(1, 0, wa_bf, slice(t, t + 1))
+            if t > 0:
+                quantise_wa(1, 0, wa_bf, slice(t - 1, t))
         exponents("a", 0, 0, 0, (0,))
         exponents("a", 0, 0, 0, (1,))
         for at in (0, W // 2):

@@ -30,13 +30,14 @@ AT_WA = {
     (0, 1): 0,
     (1, 1): 16 * KB,
 }
+AT_W2 = 8 * KB
+AT_TABLE_SCALES = 32 * KB
 AT_WC_CODES = 32 * KB
 AT_WC_RAW = 36 * KB
-AT_TABLE_SCALES = 30 * KB
-AT_W2 = 8 * KB
-AT_WA_BF_LAST = 52 * KB
+AT_WA_BF_HIGH = 52 * KB
 AT_WC_SCALES_RAW = 60 * KB
 
+TABLE_LEAD = T // 4
 
 SPANS = (
     (0, 256, ((0, 0), (0, 256))),
@@ -90,11 +91,12 @@ def tile_list_electrode_node_currents_kernel(
 
         table = [placed("table%d" % a, [P, T], I32, AT_TABLE[a]) for a in range(2)]
 
-        def load_table(a):
-            nc.sync.dma_start(out=table[a][:], in_=tab_words[a].rearrange("p t i -> p (t i)").bitcast(I32))
+        def load_table(a, cols):
+            words = tab_words[a].rearrange("p t i -> p (t i)").bitcast(I32)
+            nc.sync.dma_start(out=table[a][:, cols], in_=words[:, cols])
 
         load_scale_rows(wc_scales_raw, wc_scales, range(3))
-        load_table(0)
+        load_table(0, slice(0, T))
         load_scale_rows(wc_scales_raw, wc_scales, range(3, 4))
         v_scales = [held("v_scales%d" % a, [P, S], U8) for a in range(2)]
         for a in range(2):
@@ -105,16 +107,17 @@ def tile_list_electrode_node_currents_kernel(
         picked_scales = held("picked_scales", [P, S], U8)
         nc.vector.tensor_copy(picked_scales[:], table_scales[:].indirect(offsets[:]))
 
-        def move_scale_rows(a, queue):
+        def move_scale_rows(a):
             for e in range(4):
-                queue.dma_start(
+                nc.sync.dma_start(
                     out=v_scales[a][e:P:32, :].bitcast(I32),
                     in_=picked_scales[64 * a + 4 * e : 64 * (a + 1) : 16, :].bitcast(I32),
                 )
 
-        move_scale_rows(0, nc.sync)
-        load_table(1)
-        move_scale_rows(1, nc.sync)
+        load_table(1, slice(0, TABLE_LEAD))
+        move_scale_rows(0)
+        load_table(1, slice(TABLE_LEAD, T))
+        move_scale_rows(1)
 
         wc_codes = placed("wc_codes", [P, 4, 4, 256], U8, AT_WC_CODES)
         nc.vector.tensor_copy(
@@ -122,16 +125,16 @@ def tile_list_electrode_node_currents_kernel(
             in_=wc_raw[:].bitcast(I32).rearrange("p a (b m t e) -> p (a b) t m e", b=2, t=4, e=2),
         )
 
-        nc.scalar.copy(
-            i0_by_slot[0:2].rearrange("b t (m u) -> b t m u", u=4),
-            i0_rows[:].rearrange("b (m t u) -> b t m u", t=4, u=4),
+        nc.vector.tensor_copy(
+            out=i0_by_slot[0:2].rearrange("b t (m u) -> b t m u", u=4),
+            in_=i0_rows[:].rearrange("b (m t u) -> b t m u", t=4, u=4),
         )
         for t in range(4):
             nc.tensor.transpose(banks[0][:, P * t : P * (t + 1)], i0_by_slot[:, t, :], identity[:])
         i0_sb = held("i0_sb", [P, 8], F32)
-        nc.scalar.copy(
-            i0_sb[:].rearrange("p (b t) -> p b t", b=2),
-            banks[0][:].rearrange("p (t b) -> p b t", t=4)[:, 0:2, :],
+        nc.vector.tensor_copy(
+            out=i0_sb[:].rearrange("p (b t) -> p b t", b=2),
+            in_=banks[0][:].rearrange("p (t b) -> p b t", t=4)[:, 0:2, :],
         )
         bits = i0_sb[:].bitcast(I32)
         mantissa = held("mantissa", [P, 8], I32)
@@ -367,11 +370,11 @@ def tile_list_electrode_node_currents_kernel(
         all_slots, low_slots, high_slots = slice(0, 4), slice(0, 2), slice(2, 4)
         round_wa_on_vector(0, 0, wa_bf, all_slots)
         quantise_wa(0, 0, wa_bf, all_slots)
-        for t in range(5):
-            if t < 4:
-                round_wa_on_vector(1, 0, wa_bf, slice(t, t + 1))
-            if t > 0:
-                quantise_wa(1, 0, wa_bf, slice(t - 1, t))
+        round_wa_on_vector(1, 0, wa_bf, slice(0, 1))
+        for t in range(1, 4):
+            round_wa_on_vector(1, 0, wa_bf, slice(t, t + 1))
+            quantise_wa(1, 0, wa_bf, slice(t - 1, t))
+        quantise_wa(1, 0, wa_bf, slice(3, 4))
         exponents("a", 0, 0, 0, (0,))
         exponents("a", 0, 0, 0, (1,))
         for at in (0, W // 2):
@@ -385,11 +388,11 @@ def tile_list_electrode_node_currents_kernel(
         round_wa_on_vector(0, 1, wa_bf, all_slots)
         quantise_w2()
         quantise_wa(0, 1, wa_bf, all_slots)
-        wa_bf_high = placed("wa_bf_high", [P, W, 4], BF16, AT_WA_BF_LAST)
+        wa_bf_high = placed("wa_bf_high", [P, W, 4], BF16, AT_WA_BF_HIGH)
         round_wa_on_vector(1, 1, wa_bf_high, high_slots)
         quantise_h(0, 0, W)
         quantise_wa(1, 1, wa_bf_high, high_slots)
-        h_bf[(0, 1)] = placed("h_bf01", [P, W, 4], BF16, AT_WA_BF_LAST)
+        h_bf[(0, 1)] = placed("h_bf01", [P, W, 4], BF16, AT_WA_BF_HIGH)
         net_rate(0, W, W)
         rate_tiles("c", 1, 0, 0)
         wa_bf_low = held("wa_bf_low", [P, W, 4], BF16)

@@ -32,10 +32,10 @@ AT_WA = {
 }
 AT_W2 = 8 * KB
 AT_TABLE_SCALES = 32 * KB
-AT_WC_CODES = 32 * KB
-AT_WC_RAW = 36 * KB
+AT_PLANES = (32 * KB, 34 * KB)
 AT_WA_BF_HIGH = 52 * KB
-AT_WC_SCALES_RAW = 60 * KB
+AT_WA_BF_LOW = 56 * KB
+AT_STAGED = 60 * KB
 
 TABLE_LEAD = T // 4
 
@@ -59,34 +59,47 @@ def tile_list_electrode_node_currents_kernel(
         banks = [psum.tile([P, W], F32, name="bank%d" % n) for n in range(8)]
 
         def held(name, shape, dtype):
-            return keep.tile(shape, dtype, name=name, align_bytes=64)
+            return keep.tile(shape, dtype, name=name, align_bytes=256)
 
         def placed(name, shape, dtype, at):
-            return reuse.tile(shape, dtype, name=name, align_bytes=64, offset=at)
+            return reuse.tile(shape, dtype, name=name, align_bytes=256, offset=at)
 
         offsets = keep.tile([P, S // 16], U16, name="offsets")
         nc.sync.dma_start(offsets[:], offs)
 
         identity = held("identity", [P, P], F32)
         make_identity(nc, identity[:])
-        wc_raw = placed("wc_raw", [P, 2, 2 * H], U8, AT_WC_RAW)
-        nc.sync.dma_start(out=wc_raw[:].bitcast(I32), in_=wc_words.rearrange("a p x -> p a x").bitcast(I32))
-        i0_rows = held("i0_rows", [2, W], F32)
-        nc.sync.dma_start(out=i0_rows[:], in_=i0.rearrange("(b r) -> b r", b=2))
+        wc_raw = [held("wc_raw%d" % b, [P, 2, 2 * W], U8) for b in range(2)]
+        wc_codes = [held("wc_codes%d" % b, [P, 2, 4, 256], U8) for b in range(2)]
+
+        def load_wc(b):
+            words = wc_words.rearrange("a p x -> p a x")[:, :, 2 * W * b : 2 * W * (b + 1)]
+            nc.sync.dma_start(out=wc_raw[b][:].bitcast(I32), in_=words.bitcast(I32))
+
+        def order_wc(b):
+            nc.vector.tensor_copy(
+                out=wc_codes[b][:].bitcast(I32).rearrange("p a t (m e) -> p a t m e", e=2),
+                in_=wc_raw[b][:].bitcast(I32).rearrange("p a (m t e) -> p a t m e", t=4, e=2),
+            )
+
+        load_wc(0)
 
         table_scales = placed("table_scales", [P, T], U8, AT_TABLE_SCALES)
         nc.vector.memset(table_scales[:].bitcast(I32), 0)
-        wc_scales_raw = placed("wc_scales_raw", [P, 2, H], U8, AT_WC_SCALES_RAW)
-        nc.vector.memset(wc_scales_raw[:].bitcast(I32), 0)
+        wc_rows = held("wc_rows", [P, H], U8)
+        nc.vector.memset(wc_rows[:].bitcast(I32), 0)
         i0_by_slot = held("i0_by_slot", [P, 4, P], F32)
         nc.vector.memset(i0_by_slot[:], 0.0)
-        nc.sync.dma_start(
-            out=table_scales[0:P:4, :].bitcast(I32), in_=tab_scales.rearrange("a q t -> (a q) t").bitcast(I32)
-        )
+        for a in range(2):
+            nc.sync.dma_start(out=table_scales[4 + a : P : 8, :].bitcast(I32), in_=tab_scales[a].bitcast(I32))
+        for a in range(2):
+            nc.sync.dma_start(out=wc_rows[4 + a : P : 8, :].bitcast(I32), in_=wc_scales[a].bitcast(I32))
+        i0_rows = held("i0_rows", [2, W], F32)
+        nc.sync.dma_start(out=i0_rows[:], in_=i0.rearrange("(b r) -> b r", b=2))
 
-        def load_scale_rows(planes, src, rows=range(4)):
+        def load_scale_rows(planes, src):
             src_by_e = src.rearrange("a (g e) n -> e g a n", e=4).bitcast(I32)
-            for e in rows:
+            for e in range(4):
                 nc.sync.dma_start(out=planes[e:P:32, :, :].bitcast(I32), in_=src_by_e[e])
 
         table = [placed("table%d" % a, [P, T], I32, AT_TABLE[a]) for a in range(2)]
@@ -95,35 +108,31 @@ def tile_list_electrode_node_currents_kernel(
             words = tab_words[a].rearrange("p t i -> p (t i)").bitcast(I32)
             nc.sync.dma_start(out=table[a][:, cols], in_=words[:, cols])
 
-        load_scale_rows(wc_scales_raw, wc_scales, range(3))
         load_table(0, slice(0, T))
-        load_scale_rows(wc_scales_raw, wc_scales, range(3, 4))
-        v_scales = [held("v_scales%d" % a, [P, S], U8) for a in range(2)]
-        for a in range(2):
-            nc.vector.memset(v_scales[a][:].bitcast(I32), 0)
         wd_sc = held("wd_sc", [P, 2, N], U8)
         nc.vector.memset(wd_sc[:].bitcast(I32), 0)
 
         picked_scales = held("picked_scales", [P, S], U8)
         nc.vector.tensor_copy(picked_scales[:], table_scales[:].indirect(offsets[:]))
+        staged = placed("staged", [P, S + H], U8, AT_STAGED)
+        nc.vector.tensor_copy(
+            out=staged[:, S:].bitcast(I32).rearrange("p (b t m) -> p b t m", b=2, t=4),
+            in_=wc_rows[:].bitcast(I32).rearrange("p (b m t) -> p b t m", b=2, t=4),
+        )
+        nc.vector.tensor_copy(out=staged[:, 0:S].bitcast(I32), in_=picked_scales[:].bitcast(I32))
+        planes = [placed("planes%d" % a, [P, S + H], U8, AT_PLANES[a]) for a in range(2)]
 
         def move_scale_rows(a):
             for e in range(4):
                 nc.sync.dma_start(
-                    out=v_scales[a][e:P:32, :].bitcast(I32),
-                    in_=picked_scales[64 * a + 4 * e : 64 * (a + 1) : 16, :].bitcast(I32),
+                    out=planes[a][e:P:32, :].bitcast(I32), in_=staged[8 * e + 4 + a : P : 32, :].bitcast(I32)
                 )
 
         load_table(1, slice(0, TABLE_LEAD))
         move_scale_rows(0)
         load_table(1, slice(TABLE_LEAD, T))
         move_scale_rows(1)
-
-        wc_codes = placed("wc_codes", [P, 4, 4, 256], U8, AT_WC_CODES)
-        nc.vector.tensor_copy(
-            out=wc_codes[:].bitcast(I32).rearrange("p g t (m e) -> p g t m e", e=2),
-            in_=wc_raw[:].bitcast(I32).rearrange("p a (b m t e) -> p (a b) t m e", b=2, t=4, e=2),
-        )
+        order_wc(0)
 
         nc.vector.tensor_copy(
             out=i0_by_slot[0:2].rearrange("b t (m u) -> b t m u", u=4),
@@ -158,14 +167,9 @@ def tile_list_electrode_node_currents_kernel(
             v_codes[(a, j)] = into
 
         gather_words(0, 0, held("v_codes00", [P, W], U32))
-        wc_sc = held("wc_sc", [P, 4, 4, 128], U8)
-        nc.vector.tensor_copy(
-            out=wc_sc[:].bitcast(I32),
-            in_=wc_scales_raw[:].bitcast(I32).rearrange("p a (b m t) -> p (a b) t m", b=2, t=4),
-        )
         ln_i0 = held("ln_i0", [P, 8], F32)
         nc.vector.tensor_tensor(ln_i0[:], ln_mantissa[:], ln_power[:], ALU.add)
-        gather_words(0, 1, placed("v_codes01", [P, W], U32, AT_WC_SCALES_RAW))
+        gather_words(0, 1, held("v_codes01", [P, W], U32))
         for j in range(HALVES):
             gather_words(1, j, held("v_codes1%d" % j, [P, W], U32))
 
@@ -185,6 +189,7 @@ def tile_list_electrode_node_currents_kernel(
         for b in range(2):
             for t in range(4):
                 nc.sync.dma_start(out=w2_raw[:, b, t, :], in_=w2_rows[b, t])
+        load_wc(1)
         load_wa(0, 1)
         load_wa(1, 1)
         wd_codes = held("wd_codes", [P, 2, N], I32)
@@ -240,14 +245,14 @@ def tile_list_electrode_node_currents_kernel(
                 lhs = wa_codes[(a, b)][:, P * t : P * (t + 1)].bitcast(FP8X4)
                 lhs_sc = wa_sc[(a, b)][:, P * t : P * (t + 1)]
             else:
-                lhs = wc_codes[:, 2 * a + b, t, :].bitcast(FP4X4)
-                lhs_sc = wc_sc[:, 2 * a + b, t, :]
+                lhs = wc_codes[b][:, a, t, :].bitcast(FP4X4)
+                lhs_sc = planes[a][:, S + W * b + P * t : S + W * b + P * (t + 1)]
             nc.tensor.matmul_mx(
                 out=bank[:],
                 lhsT=lhs,
                 lhsT_scale=lhs_sc,
                 rhs=v_codes[(a, j)][:].bitcast(FP8X4),
-                rhs_scale=v_scales[a][:, j * W : (j + 1) * W],
+                rhs_scale=planes[a][:, j * W : (j + 1) * W],
                 start=(a == 0),
                 stop=(a == 1),
             )
@@ -289,7 +294,7 @@ def tile_list_electrode_node_currents_kernel(
                         lhsT=wd_codes[:, a, P * c : P * (c + 1)].bitcast(FP8X4),
                         lhsT_scale=wd_sc[:, a, P * c : P * (c + 1)],
                         rhs=v_codes[(a, j)][:, at : at + width].bitcast(FP8X4),
-                        rhs_scale=v_scales[a][:, first_col : first_col + width],
+                        rhs_scale=planes[a][:, first_col : first_col + width],
                         start=(a == 0 and (c == 0 or not shares_bank(s))),
                         stop=False,
                     )
@@ -298,22 +303,25 @@ def tile_list_electrode_node_currents_kernel(
         h_sc = [held("h_sc%d" % b, [P, S], U8) for b in range(2)]
         h_bf = {}
 
+        def h_view(b, first_col, width):
+            start = max(c for (bb, c) in h_bf if bb == b and c <= first_col)
+            return h_bf[(b, start)][:, first_col - start : first_col - start + width, :]
+
         def net_rate(b, first_col, width):
             j, at = divmod(first_col, W)
             nc.vector.tensor_tensor(
-                h_bf[(b, j)][:, at : at + width, :].rearrange("p (c x) t -> p c t x", x=4),
+                h_view(b, first_col, width).rearrange("p (c x) t -> p c t x", x=4),
                 rates[("a", b, j)][:, :, at : at + width].rearrange("p t (c x) -> p c t x", x=4),
                 rates[("c", b, j)][:, :, at : at + width].rearrange("p t (c x) -> p c t x", x=4),
                 ALU.subtract,
             )
 
         def quantise_h(b, first_col, width):
-            j, at = divmod(first_col, W)
             cols = slice(first_col, first_col + width)
             nc.vector.quantize_mx(
                 out=h_codes[b][:, cols].bitcast(FP8X4),
                 scales=h_sc[b][:, cols],
-                in_=h_bf[(b, j)][:, at : at + width, :].rearrange("p c t -> p (c t)"),
+                in_=h_view(b, first_col, width).rearrange("p c t -> p (c t)"),
             )
 
         w2_bf = held("w2_bf", [P, 2, N, 4], BF16)
@@ -381,6 +389,7 @@ def tile_list_electrode_node_currents_kernel(
             exponentials("a", 0, 0, 0, at, W // 2)
         for b in range(2):
             round_w2(b)
+        order_wc(1)
         rate_tiles("a", 0, 1, 4)
         h_bf[(0, 0)] = placed("h_bf00", [P, W, 4], BF16, AT_W2)
         for at in (0, W // 2):
@@ -392,16 +401,19 @@ def tile_list_electrode_node_currents_kernel(
         round_wa_on_vector(1, 1, wa_bf_high, high_slots)
         quantise_h(0, 0, W)
         quantise_wa(1, 1, wa_bf_high, high_slots)
-        h_bf[(0, 1)] = placed("h_bf01", [P, W, 4], BF16, AT_WA_BF_HIGH)
-        net_rate(0, W, W)
+        h_bf[(0, W)] = placed("h_bf01", [P, W // 2, 4], BF16, AT_WA_BF_HIGH)
+        net_rate(0, W, W // 2)
         rate_tiles("c", 1, 0, 0)
-        wa_bf_low = held("wa_bf_low", [P, W, 4], BF16)
+        wa_bf_low = placed("wa_bf_low", [P, W, 4], BF16, AT_WA_BF_LOW)
         round_wa_on_scalar(1, 1, wa_bf_low, low_slots)
         quantise_wa(1, 1, wa_bf_low, low_slots)
-        quantise_h(0, W, W)
+        h_bf[(0, W + W // 2)] = placed("h_bf02", [P, W // 2, 4], BF16, AT_WA_BF_LOW)
+        net_rate(0, W + W // 2, W // 2)
+        quantise_h(0, W, W // 2)
+        quantise_h(0, W + W // 2, W // 2)
         rate_tiles("c", 1, 1, 4)
         h_bf[(1, 0)] = held("h_bf10", [P, W, 4], BF16)
-        h_bf[(1, 1)] = held("h_bf11", [P, W, 4], BF16)
+        h_bf[(1, W)] = held("h_bf11", [P, W, 4], BF16)
         exponents("a", 1, 0, 0, (0, 1))
         exponents("a", 1, 1, 4, (0, 1))
         for first_col, width, places in SPANS:

@@ -30,22 +30,32 @@ AT_WA = {
     (0, 1): 0,
     (1, 1): 16 * KB,
 }
-AT_W2 = 8 * KB
+AT_W2 = (8 * KB, 12 * KB)
 AT_TABLE_SCALES = 32 * KB
 AT_PLANES = (32 * KB, 34 * KB)
-AT_WA_BF_HIGH = 52 * KB
-AT_WA_BF_LOW = 56 * KB
+AT_FIRST_RATES = 52 * KB
 AT_STAGED = 60 * KB
+AT_FIRST_H = 62 * KB
 
 TABLE_LEAD = T // 4
 
 SPANS = (
-    (0, 256, ((0, 0), (0, 256))),
-    (256, 256, ((1, 0), (1, 256))),
-    (512, 256, ((2, 0), (2, 256))),
-    (768, 128, ((3, 0), (3, 128))),
-    (896, 128, ((4, 0), (5, 0))),
+    (0, 256, ((6, 0), (6, 256))),
+    (256, 256, ((7, 0), (7, 256))),
+    (512, 256, ((4, 0), (4, 256))),
+    (768, 128, ((5, 0), (5, 128))),
+    (896, 128, ((0, 0), (1, 0))),
 )
+GROUP_BANKS = {
+    ("c", 0, 0): (0, 1, 2, 3),
+    ("c", 0, 1): (4, 5, 6, 7),
+    ("a", 0, 0): (0, 1, 2, 3),
+    ("a", 0, 1): (4, 5, 6, 7),
+    ("c", 1, 0): (0, 1, 2, 3),
+    ("c", 1, 1): (4, 5, 0, 1),
+    ("a", 1, 0): (2, 3, 4, 5),
+    ("a", 1, 1): (0, 1, 2, 3),
+}
 
 
 def tile_list_electrode_node_currents_kernel(
@@ -182,38 +192,46 @@ def tile_list_electrode_node_currents_kernel(
                 in_=wa[W * a : W * (a + 1), W * b : W * (b + 1)].rearrange("(p i) c -> p i c", i=4),
             )
 
+        w2_raw = [placed("w2_raw%d" % b, [P, 4, N], F32, AT_W2[b]) for b in range(2)]
+        w2_rows = w2.rearrange("(b m t u) n -> b t m u n", b=2, t=4, u=4)
+
+        def load_w2(b):
+            for t in range(4):
+                nc.sync.dma_start(out=w2_raw[b][:, t, :], in_=w2_rows[b, t])
+
         load_wa(0, 0)
         load_wa(1, 0)
-        w2_raw = placed("w2_raw", [P, 2, 4, N], F32, AT_W2)
-        w2_rows = w2.rearrange("(b m t u) n -> b t m u n", b=2, t=4, u=4)
-        for b in range(2):
-            for t in range(4):
-                nc.sync.dma_start(out=w2_raw[:, b, t, :], in_=w2_rows[b, t])
         load_wc(1)
+        load_w2(0)
         load_wa(0, 1)
         load_wa(1, 1)
         wd_codes = held("wd_codes", [P, 2, N], I32)
         nc.sync.dma_start(out=wd_codes[:], in_=wd_words.rearrange("a p c i -> p a (c i)").bitcast(I32))
         load_scale_rows(wd_sc, wd_scales)
+        load_w2(1)
         bo_sb = held("bo_sb", [P, 2], F32)
         with nc.allow_non_contiguous_dma(reason="one bias a partition"):
             nc.sync.dma_start(out=bo_sb[:], in_=bo.rearrange("(c p) -> p c", p=P))
 
-        wa_bf = held("wa_bf", [P, W, 4], BF16)
+        wa_bf = {}
 
-        def slot_views(a, b, grouped):
-            return (
-                grouped[:].rearrange("p (t m u) i -> p t m i u", t=4, u=4),
-                wa_raw[(a, b)][:].rearrange("p i (m t u) -> p t m i u", t=4, u=4),
-            )
+        def stage_wa(a, b, slots, tile):
+            for t in slots:
+                wa_bf[(a, b, t)] = (tile, slots.start)
 
-        def round_wa_on_vector(a, b, grouped, slots):
-            dst, src = slot_views(a, b, grouped)
-            nc.vector.tensor_copy(out=dst[:, slots], in_=src[:, slots])
+        def round_views(a, b, slots):
+            tile, first = wa_bf[(a, b, slots.start)]
+            dst = tile[:].rearrange("p (t m u) i -> p t m i u", m=32, u=4)
+            src = wa_raw[(a, b)][:].rearrange("p i (m t u) -> p t m i u", t=4, u=4)
+            return dst[:, slots.start - first : slots.stop - first], src[:, slots.start : slots.stop]
 
-        def round_wa_on_scalar(a, b, grouped, slots):
-            dst, src = slot_views(a, b, grouped)
-            nc.scalar.copy(dst[:, slots], src[:, slots])
+        def round_wa_on_vector(a, b, slots):
+            dst, src = round_views(a, b, slots)
+            nc.vector.tensor_copy(out=dst, in_=src)
+
+        def round_wa_on_scalar(a, b, slots):
+            dst, src = round_views(a, b, slots)
+            nc.scalar.copy(dst, src)
 
         wa_codes = {}
         wa_sc = {}
@@ -222,12 +240,13 @@ def tile_list_electrode_node_currents_kernel(
                 wa_codes[(a, b)] = held("wa_codes%d%d" % (a, b), [P, W], U32)
                 wa_sc[(a, b)] = held("wa_sc%d%d" % (a, b), [P, W], U8)
 
-        def quantise_wa(a, b, grouped, slots):
+        def quantise_wa(a, b, slots):
+            tile, first = wa_bf[(a, b, slots.start)]
             cols = slice(P * slots.start, P * slots.stop)
             nc.vector.quantize_mx(
                 out=wa_codes[(a, b)][:, cols].bitcast(FP8X4),
                 scales=wa_sc[(a, b)][:, cols],
-                in_=grouped[:, cols, :].rearrange("p c i -> p (c i)"),
+                in_=tile[:, P * (slots.start - first) : P * (slots.stop - first), :].rearrange("p c i -> p (c i)"),
             )
 
         rates = {}
@@ -235,12 +254,14 @@ def tile_list_electrode_node_currents_kernel(
             for b in range(2):
                 for j in range(HALVES):
                     name = "rate_%s%d%d" % (kind, b, j)
-                    if (kind, b, j) == ("c", 1, 1):
+                    if (kind, b, j) == ("c", 0, 0):
+                        rates[(kind, b, j)] = placed(name, [P, 4, W], F32, AT_FIRST_RATES)
+                    elif (kind, b, j) == ("c", 1, 1):
                         rates[(kind, b, j)] = placed(name, [P, 4, W], F32, AT_WA[(1, 1)])
                     else:
                         rates[(kind, b, j)] = held(name, [P, 4, W], F32)
 
-        def exponent_pass(bank, kind, b, j, t, a):
+        def exponent_pass(kind, b, j, t, a, opens):
             if kind == "a":
                 lhs = wa_codes[(a, b)][:, P * t : P * (t + 1)].bitcast(FP8X4)
                 lhs_sc = wa_sc[(a, b)][:, P * t : P * (t + 1)]
@@ -248,32 +269,32 @@ def tile_list_electrode_node_currents_kernel(
                 lhs = wc_codes[b][:, a, t, :].bitcast(FP4X4)
                 lhs_sc = planes[a][:, S + W * b + P * t : S + W * b + P * (t + 1)]
             nc.tensor.matmul_mx(
-                out=bank[:],
+                out=banks[GROUP_BANKS[(kind, b, j)][t]][:],
                 lhsT=lhs,
                 lhsT_scale=lhs_sc,
                 rhs=v_codes[(a, j)][:].bitcast(FP8X4),
                 rhs_scale=planes[a][:, j * W : (j + 1) * W],
-                start=(a == 0),
-                stop=(a == 1),
+                start=opens,
+                stop=not opens,
             )
 
-        def exponents(kind, b, j, first_bank, passes):
+        def exponents(kind, b, j, passes, opening=0):
             for t in range(4):
                 for a in passes:
-                    exponent_pass(banks[first_bank + t], kind, b, j, t, a)
+                    exponent_pass(kind, b, j, t, a, a == opening)
 
-        def exponentials(kind, b, j, first_bank, at, width):
-            for t in range(4):
+        def exponentials(kind, b, j, slots, at, width):
+            for t in slots:
                 nc.scalar.activation(
                     rates[(kind, b, j)][:, t, at : at + width],
-                    banks[first_bank + t][:, at : at + width],
+                    banks[GROUP_BANKS[(kind, b, j)][t]][:, at : at + width],
                     ACT.Exp,
                     bias=ln_i0[:, 4 * b + t : 4 * b + t + 1],
                 )
 
-        def rate_tiles(kind, b, j, first_bank):
-            exponents(kind, b, j, first_bank, (0, 1))
-            exponentials(kind, b, j, first_bank, 0, W)
+        def rate_tiles(kind, b, j):
+            exponents(kind, b, j, (0, 1))
+            exponentials(kind, b, j, range(4), 0, W)
 
         def span_sum(s, c):
             first_col, width, places = SPANS[s]
@@ -324,34 +345,34 @@ def tile_list_electrode_node_currents_kernel(
                 in_=h_view(b, first_col, width).rearrange("p c t -> p (c t)"),
             )
 
-        w2_bf = held("w2_bf", [P, 2, N, 4], BF16)
-        w2_codes = held("w2_codes", [P, 2 * N], U32)
-        w2_sc = held("w2_sc", [P, 2 * N], U8)
+        w2_bf = {}
+        w2_codes = [held("w2_codes%d" % b, [P, N], U32) for b in range(2)]
+        w2_sc = [held("w2_sc%d" % b, [P, N], U8) for b in range(2)]
 
         def round_w2(b):
             nc.vector.tensor_tensor(
-                w2_bf[:, b, :, :].rearrange("p (c x) t -> p c t x", x=4),
-                w2_raw[:, b, :, :].rearrange("p t (c x) -> p c t x", x=4),
+                w2_bf[b][:].rearrange("p (c x) t -> p c t x", x=4),
+                w2_raw[b][:].rearrange("p t (c x) -> p c t x", x=4),
                 i0_sign[:, 4 * b : 4 * b + 4].unsqueeze(1).unsqueeze(3).to_broadcast([P, N // 4, 4, 4]),
                 ALU.mult,
             )
 
-        def quantise_w2():
+        def quantise_w2(b):
             nc.vector.quantize_mx(
-                out=w2_codes[:].bitcast(FP8X4),
-                scales=w2_sc[:],
-                in_=w2_bf[:].rearrange("p b n t -> p (b n t)"),
+                out=w2_codes[b][:].bitcast(FP8X4),
+                scales=w2_sc[b][:],
+                in_=w2_bf[b][:].rearrange("p n t -> p (n t)"),
             )
 
         def collect(b, s):
             first_col, width, places = SPANS[s]
             cols = slice(first_col, first_col + width)
             for c in range(2):
-                rows = slice(N * b + P * c, N * b + P * (c + 1))
+                rows = slice(P * c, P * (c + 1))
                 nc.tensor.matmul_mx(
                     out=span_sum(s, c),
-                    lhsT=w2_codes[:, rows].bitcast(FP8X4),
-                    lhsT_scale=w2_sc[:, rows],
+                    lhsT=w2_codes[b][:, rows].bitcast(FP8X4),
+                    lhsT_scale=w2_sc[b][:, rows],
                     rhs=h_codes[b][:, cols].bitcast(FP8X4),
                     rhs_scale=h_sc[b][:, cols],
                     start=False,
@@ -362,68 +383,88 @@ def tile_list_electrode_node_currents_kernel(
 
         def finish(s):
             first_col, width, places = SPANS[s]
+            cols = slice(first_col, first_col + width)
             result = held("result%d" % s, [P, 2, width], F32)
             for c in range(2):
                 if c == 1 and s == len(SPANS) - 1:
                     nc.vector.tensor_scalar(result[:, c, :], span_sum(s, c), bo_sb[:, c : c + 1], None, ALU.add)
                 else:
                     nc.scalar.activation(result[:, c, :], span_sum(s, c), ACT.Identity, bias=bo_sb[:, c : c + 1])
-            nc.sync.dma_start(out=out_by_c[:, :, first_col : first_col + width], in_=result[:])
+                if width > P:
+                    nc.sync.dma_start(out=out_by_c[:, c, cols], in_=result[:, c, :])
+            if width == P:
+                nc.sync.dma_start(out=out_by_c[:, :, cols], in_=result[:])
 
+        quarter = W // 2
         for a in range(2):
             for j in range(HALVES):
-                exponents("c", 0, j, 4 * j, (a,))
+                exponents("c", 0, j, (a,))
         for j in range(HALVES):
-            exponentials("c", 0, j, 4 * j, 0, W)
-        all_slots, low_slots, high_slots = slice(0, 4), slice(0, 2), slice(2, 4)
-        round_wa_on_vector(0, 0, wa_bf, all_slots)
-        quantise_wa(0, 0, wa_bf, all_slots)
-        round_wa_on_vector(1, 0, wa_bf, slice(0, 1))
+            exponentials("c", 0, j, range(4), 0, W)
+        stage_wa(0, 0, range(4), held("wa_bf00", [P, W, 4], BF16))
+        for slots in (range(0, 2), range(2, 4)):
+            round_wa_on_vector(0, 0, slots)
+        for slots in (range(0, 2), range(2, 4)):
+            quantise_wa(0, 0, slots)
+        stage_wa(1, 0, range(4), held("wa_bf10", [P, W, 4], BF16))
+        round_wa_on_vector(1, 0, range(0, 1))
         for t in range(1, 4):
-            round_wa_on_vector(1, 0, wa_bf, slice(t, t + 1))
-            quantise_wa(1, 0, wa_bf, slice(t - 1, t))
-        quantise_wa(1, 0, wa_bf, slice(3, 4))
-        exponents("a", 0, 0, 0, (0,))
-        exponents("a", 0, 0, 0, (1,))
-        for at in (0, W // 2):
-            exponentials("a", 0, 0, 0, at, W // 2)
-        for b in range(2):
-            round_w2(b)
+            round_wa_on_vector(1, 0, range(t, t + 1))
+            quantise_wa(1, 0, range(t - 1, t))
         order_wc(1)
-        rate_tiles("a", 0, 1, 4)
-        h_bf[(0, 0)] = placed("h_bf00", [P, W, 4], BF16, AT_W2)
-        for at in (0, W // 2):
-            net_rate(0, at, W // 2)
-        round_wa_on_vector(0, 1, wa_bf, all_slots)
-        quantise_w2()
-        quantise_wa(0, 1, wa_bf, all_slots)
-        wa_bf_high = placed("wa_bf_high", [P, W, 4], BF16, AT_WA_BF_HIGH)
-        round_wa_on_vector(1, 1, wa_bf_high, high_slots)
-        quantise_h(0, 0, W)
-        quantise_wa(1, 1, wa_bf_high, high_slots)
-        h_bf[(0, W)] = placed("h_bf01", [P, W // 2, 4], BF16, AT_WA_BF_HIGH)
-        net_rate(0, W, W // 2)
-        rate_tiles("c", 1, 0, 0)
-        wa_bf_low = placed("wa_bf_low", [P, W, 4], BF16, AT_WA_BF_LOW)
-        round_wa_on_scalar(1, 1, wa_bf_low, low_slots)
-        quantise_wa(1, 1, wa_bf_low, low_slots)
-        h_bf[(0, W + W // 2)] = placed("h_bf02", [P, W // 2, 4], BF16, AT_WA_BF_LOW)
-        net_rate(0, W + W // 2, W // 2)
-        quantise_h(0, W, W // 2)
-        quantise_h(0, W + W // 2, W // 2)
-        rate_tiles("c", 1, 1, 4)
+        quantise_wa(1, 0, range(3, 4))
+        exponents("a", 0, 0, (0,))
+        exponents("a", 0, 0, (1,))
+        exponentials("a", 0, 0, range(0, 2), 0, W)
+        for at in (0, quarter):
+            exponentials("a", 0, 0, range(2, 4), at, quarter)
+        w2_bf[0] = held("w2_bf0", [P, N, 4], BF16)
+        round_w2(0)
+        exponents("a", 0, 1, (1, 0), opening=1)
+        exponentials("a", 0, 1, range(4), 0, W)
+        h_bf[(0, 0)] = placed("h_bf00", [P, W, 4], BF16, AT_FIRST_H)
+        net_rate(0, 0, quarter)
+        quantise_w2(0)
+        net_rate(0, quarter, quarter)
+        quantise_h(0, 0, quarter)
+        stage_wa(0, 1, range(4), placed("wa_bf01", [P, W, 4], BF16, AT_FIRST_RATES))
+        round_wa_on_vector(0, 1, range(4))
+        quantise_h(0, quarter, quarter)
+        quantise_wa(0, 1, range(4))
+        rate_tiles("c", 1, 0)
+        low_slots, high_slots = range(0, 2), range(2, 4)
+        stage_wa(1, 1, low_slots, placed("wa_bf11_low", [P, quarter, 4], BF16, AT_FIRST_H))
+        stage_wa(1, 1, high_slots, placed("wa_bf11_high", [P, quarter, 4], BF16, AT_FIRST_H + 2 * KB))
+        round_wa_on_vector(1, 1, low_slots)
+        round_wa_on_scalar(1, 1, high_slots)
+        h_bf[(0, W)] = placed("h_bf01", [P, quarter, 4], BF16, AT_FIRST_RATES)
+        net_rate(0, W, quarter)
+        quantise_wa(1, 1, low_slots)
+        h_bf[(0, W + quarter)] = held("h_bf02", [P, quarter, 4], BF16)
+        net_rate(0, W + quarter, quarter)
+        quantise_wa(1, 1, high_slots)
+        quantise_h(0, W, quarter)
+        w2_bf[1] = placed("w2_bf1", [P, N, 4], BF16, AT_FIRST_H + 2 * KB)
+        round_w2(1)
+        quantise_h(0, W + quarter, quarter)
+        quantise_w2(1)
+        rate_tiles("c", 1, 1)
+        for s in range(2):
+            leak(s)
         h_bf[(1, 0)] = held("h_bf10", [P, W, 4], BF16)
         h_bf[(1, W)] = held("h_bf11", [P, W, 4], BF16)
-        exponents("a", 1, 0, 0, (0, 1))
-        exponents("a", 1, 1, 4, (0, 1))
-        for first_col, width, places in SPANS:
-            j, at = divmod(first_col, W)
-            exponentials("a", 1, j, 4 * j, at, width)
-        net_rate(1, SPANS[0][0], SPANS[0][1])
-        for s in range(len(SPANS)):
-            leak(s)
+        for j in range(HALVES):
+            exponents("a", 1, j, (0, 1))
+            for first_col, width, places in SPANS:
+                if first_col // W == j:
+                    exponentials("a", 1, j, range(4), first_col % W, width)
+        for s in range(2):
             collect(0, s)
+        net_rate(1, SPANS[0][0], SPANS[0][1])
         for s, (first_col, width, places) in enumerate(SPANS):
+            if s + 2 < len(SPANS):
+                leak(s + 2)
+                collect(0, s + 2)
             if s + 1 < len(SPANS):
                 net_rate(1, SPANS[s + 1][0], SPANS[s + 1][1])
             quantise_h(1, first_col, width)

@@ -33,11 +33,10 @@ AT_WA = {
 AT_W2 = (8 * KB, 12 * KB)
 AT_TABLE_SCALES = 32 * KB
 AT_PLANES = (32 * KB, 34 * KB)
-AT_FIRST_RATES = 52 * KB
-AT_STAGED = 60 * KB
-AT_FIRST_H = 62 * KB
+AT_STAGED = 52 * KB
 
-TABLE_LEAD = T // 4
+TABLE_HEAD = T // 4
+TABLE_LEAD = T // 2
 
 SPANS = (
     (0, 256, ((6, 0), (6, 256))),
@@ -93,6 +92,15 @@ def tile_list_electrode_node_currents_kernel(
             )
 
         load_wc(0)
+        i0_rows = held("i0_rows", [2, W], F32)
+        nc.sync.dma_start(out=i0_rows[:], in_=i0.rearrange("(b r) -> b r", b=2))
+        table = [placed("table%d" % a, [P, T], I32, AT_TABLE[a]) for a in range(2)]
+
+        def load_table(a, cols):
+            words = tab_words[a].rearrange("p t i -> p (t i)").bitcast(I32)
+            nc.sync.dma_start(out=table[a][:, cols], in_=words[:, cols])
+
+        load_table(0, slice(0, TABLE_HEAD))
 
         table_scales = placed("table_scales", [P, T], U8, AT_TABLE_SCALES)
         nc.vector.memset(table_scales[:].bitcast(I32), 0)
@@ -104,21 +112,13 @@ def tile_list_electrode_node_currents_kernel(
             nc.sync.dma_start(out=table_scales[4 + a : P : 8, :].bitcast(I32), in_=tab_scales[a].bitcast(I32))
         for a in range(2):
             nc.sync.dma_start(out=wc_rows[4 + a : P : 8, :].bitcast(I32), in_=wc_scales[a].bitcast(I32))
-        i0_rows = held("i0_rows", [2, W], F32)
-        nc.sync.dma_start(out=i0_rows[:], in_=i0.rearrange("(b r) -> b r", b=2))
 
         def load_scale_rows(planes, src):
             src_by_e = src.rearrange("a (g e) n -> e g a n", e=4).bitcast(I32)
             for e in range(4):
                 nc.sync.dma_start(out=planes[e:P:32, :, :].bitcast(I32), in_=src_by_e[e])
 
-        table = [placed("table%d" % a, [P, T], I32, AT_TABLE[a]) for a in range(2)]
-
-        def load_table(a, cols):
-            words = tab_words[a].rearrange("p t i -> p (t i)").bitcast(I32)
-            nc.sync.dma_start(out=table[a][:, cols], in_=words[:, cols])
-
-        load_table(0, slice(0, T))
+        load_table(0, slice(TABLE_HEAD, T))
         wd_sc = held("wd_sc", [P, 2, N], U8)
         nc.vector.memset(wd_sc[:].bitcast(I32), 0)
 
@@ -201,14 +201,14 @@ def tile_list_electrode_node_currents_kernel(
 
         load_wa(0, 0)
         load_wa(1, 0)
+        for b in range(2):
+            load_w2(b)
         load_wc(1)
-        load_w2(0)
         load_wa(0, 1)
         load_wa(1, 1)
         wd_codes = held("wd_codes", [P, 2, N], I32)
         nc.sync.dma_start(out=wd_codes[:], in_=wd_words.rearrange("a p c i -> p a (c i)").bitcast(I32))
         load_scale_rows(wd_sc, wd_scales)
-        load_w2(1)
         bo_sb = held("bo_sb", [P, 2], F32)
         with nc.allow_non_contiguous_dma(reason="one bias a partition"):
             nc.sync.dma_start(out=bo_sb[:], in_=bo.rearrange("(c p) -> p c", p=P))
@@ -254,10 +254,8 @@ def tile_list_electrode_node_currents_kernel(
             for b in range(2):
                 for j in range(HALVES):
                     name = "rate_%s%d%d" % (kind, b, j)
-                    if (kind, b, j) == ("c", 0, 0):
-                        rates[(kind, b, j)] = placed(name, [P, 4, W], F32, AT_FIRST_RATES)
-                    elif (kind, b, j) == ("c", 1, 1):
-                        rates[(kind, b, j)] = placed(name, [P, 4, W], F32, AT_WA[(1, 1)])
+                    if (kind, b, j) == ("c", 1, 1):
+                        rates[(kind, b, j)] = placed(name, [P, 4, W], F32, AT_WA[(1, 1)] + 4 * KB)
                     else:
                         rates[(kind, b, j)] = held(name, [P, 4, W], F32)
 
@@ -345,34 +343,34 @@ def tile_list_electrode_node_currents_kernel(
                 in_=h_view(b, first_col, width).rearrange("p c t -> p (c t)"),
             )
 
-        w2_bf = {}
-        w2_codes = [held("w2_codes%d" % b, [P, N], U32) for b in range(2)]
-        w2_sc = [held("w2_sc%d" % b, [P, N], U8) for b in range(2)]
+        w2_bf = held("w2_bf", [P, 2, N, 4], BF16)
+        w2_codes = held("w2_codes", [P, 2 * N], U32)
+        w2_sc = held("w2_sc", [P, 2 * N], U8)
 
         def round_w2(b):
             nc.vector.tensor_tensor(
-                w2_bf[b][:].rearrange("p (c x) t -> p c t x", x=4),
+                w2_bf[:, b, :, :].rearrange("p (c x) t -> p c t x", x=4),
                 w2_raw[b][:].rearrange("p t (c x) -> p c t x", x=4),
                 i0_sign[:, 4 * b : 4 * b + 4].unsqueeze(1).unsqueeze(3).to_broadcast([P, N // 4, 4, 4]),
                 ALU.mult,
             )
 
-        def quantise_w2(b):
+        def quantise_w2():
             nc.vector.quantize_mx(
-                out=w2_codes[b][:].bitcast(FP8X4),
-                scales=w2_sc[b][:],
-                in_=w2_bf[b][:].rearrange("p n t -> p (n t)"),
+                out=w2_codes[:].bitcast(FP8X4),
+                scales=w2_sc[:],
+                in_=w2_bf[:].rearrange("p b n t -> p (b n t)"),
             )
 
         def collect(b, s):
             first_col, width, places = SPANS[s]
             cols = slice(first_col, first_col + width)
             for c in range(2):
-                rows = slice(P * c, P * (c + 1))
+                rows = slice(N * b + P * c, N * b + P * (c + 1))
                 nc.tensor.matmul_mx(
                     out=span_sum(s, c),
-                    lhsT=w2_codes[b][:, rows].bitcast(FP8X4),
-                    lhsT_scale=w2_sc[b][:, rows],
+                    lhsT=w2_codes[:, rows].bitcast(FP8X4),
+                    lhsT_scale=w2_sc[:, rows],
                     rhs=h_codes[b][:, cols].bitcast(FP8X4),
                     rhs_scale=h_sc[b][:, cols],
                     start=False,
@@ -411,43 +409,38 @@ def tile_list_electrode_node_currents_kernel(
         for t in range(1, 4):
             round_wa_on_vector(1, 0, range(t, t + 1))
             quantise_wa(1, 0, range(t - 1, t))
-        order_wc(1)
         quantise_wa(1, 0, range(3, 4))
         exponents("a", 0, 0, (0,))
         exponents("a", 0, 0, (1,))
-        exponentials("a", 0, 0, range(0, 2), 0, W)
         for at in (0, quarter):
-            exponentials("a", 0, 0, range(2, 4), at, quarter)
-        w2_bf[0] = held("w2_bf0", [P, N, 4], BF16)
-        round_w2(0)
+            exponentials("a", 0, 0, range(4), at, quarter)
+        for b in range(2):
+            round_w2(b)
+        order_wc(1)
         exponents("a", 0, 1, (1, 0), opening=1)
         exponentials("a", 0, 1, range(4), 0, W)
-        h_bf[(0, 0)] = placed("h_bf00", [P, W, 4], BF16, AT_FIRST_H)
-        net_rate(0, 0, quarter)
-        quantise_w2(0)
-        net_rate(0, quarter, quarter)
-        quantise_h(0, 0, quarter)
-        stage_wa(0, 1, range(4), placed("wa_bf01", [P, W, 4], BF16, AT_FIRST_RATES))
-        round_wa_on_vector(0, 1, range(4))
-        quantise_h(0, quarter, quarter)
-        quantise_wa(0, 1, range(4))
+        h_bf[(0, 0)] = placed("h_bf00", [P, W, 4], BF16, AT_W2[1])
+        for at in (0, quarter):
+            net_rate(0, at, quarter)
+        stage_wa(0, 1, range(4), held("wa_bf01", [P, W, 4], BF16))
+        for slots in (range(0, 2), range(2, 4)):
+            round_wa_on_vector(0, 1, slots)
+        quantise_h(0, 0, W)
         rate_tiles("c", 1, 0)
         low_slots, high_slots = range(0, 2), range(2, 4)
-        stage_wa(1, 1, low_slots, placed("wa_bf11_low", [P, quarter, 4], BF16, AT_FIRST_H))
-        stage_wa(1, 1, high_slots, placed("wa_bf11_high", [P, quarter, 4], BF16, AT_FIRST_H + 2 * KB))
+        stage_wa(1, 1, range(4), held("wa_bf11", [P, W, 4], BF16))
         round_wa_on_vector(1, 1, low_slots)
         round_wa_on_scalar(1, 1, high_slots)
-        h_bf[(0, W)] = placed("h_bf01", [P, quarter, 4], BF16, AT_FIRST_RATES)
-        net_rate(0, W, quarter)
-        quantise_wa(1, 1, low_slots)
-        h_bf[(0, W + quarter)] = held("h_bf02", [P, quarter, 4], BF16)
-        net_rate(0, W + quarter, quarter)
-        quantise_wa(1, 1, high_slots)
-        quantise_h(0, W, quarter)
-        w2_bf[1] = placed("w2_bf1", [P, N, 4], BF16, AT_FIRST_H + 2 * KB)
-        round_w2(1)
-        quantise_h(0, W + quarter, quarter)
-        quantise_w2(1)
+        for slots in (range(0, 2), range(2, 4)):
+            quantise_wa(0, 1, slots)
+        quantise_w2()
+        for slots in (low_slots, high_slots):
+            quantise_wa(1, 1, slots)
+        h_bf[(0, W)] = placed("h_bf01", [P, W, 4], BF16, AT_WA[(1, 1)])
+        for at in (0, quarter):
+            net_rate(0, W + at, quarter)
+        for at in (0, quarter):
+            quantise_h(0, W + at, quarter)
         rate_tiles("c", 1, 1)
         for s in range(2):
             leak(s)
@@ -458,9 +451,9 @@ def tile_list_electrode_node_currents_kernel(
             for first_col, width, places in SPANS:
                 if first_col // W == j:
                     exponentials("a", 1, j, range(4), first_col % W, width)
+        net_rate(1, SPANS[0][0], SPANS[0][1])
         for s in range(2):
             collect(0, s)
-        net_rate(1, SPANS[0][0], SPANS[0][1])
         for s, (first_col, width, places) in enumerate(SPANS):
             if s + 2 < len(SPANS):
                 leak(s + 2)

@@ -35,15 +35,14 @@ AT_TABLE_SCALES = 32 * KB
 AT_PLANES = (32 * KB, 34 * KB)
 AT_STAGED = 52 * KB
 
-TABLE_HEAD = T // 4
-TABLE_LEAD = T // 2
+TABLE_LEAD = T // 4
 
 SPANS = (
-    (0, 256, ((6, 0), (6, 256))),
-    (256, 256, ((7, 0), (7, 256))),
-    (512, 256, ((4, 0), (4, 256))),
-    (768, 128, ((5, 0), (5, 128))),
-    (896, 128, ((0, 0), (1, 0))),
+    (0, 256, ((2, 0), (2, 256))),
+    (256, 256, ((3, 0), (3, 256))),
+    (512, 256, ((6, 0), (6, 256))),
+    (768, 128, ((7, 0), (0, 0))),
+    (896, 128, ((4, 0), (5, 0))),
 )
 GROUP_BANKS = {
     ("c", 0, 0): (0, 1, 2, 3),
@@ -51,9 +50,9 @@ GROUP_BANKS = {
     ("a", 0, 0): (0, 1, 2, 3),
     ("a", 0, 1): (4, 5, 6, 7),
     ("c", 1, 0): (0, 1, 2, 3),
-    ("c", 1, 1): (4, 5, 0, 1),
-    ("a", 1, 0): (2, 3, 4, 5),
-    ("a", 1, 1): (0, 1, 2, 3),
+    ("c", 1, 1): (4, 5, 6, 7),
+    ("a", 1, 0): (0, 1, 2, 3),
+    ("a", 1, 1): (4, 5, 0, 1),
 }
 
 
@@ -92,15 +91,11 @@ def tile_list_electrode_node_currents_kernel(
             )
 
         load_wc(0)
-        i0_rows = held("i0_rows", [2, W], F32)
-        nc.sync.dma_start(out=i0_rows[:], in_=i0.rearrange("(b r) -> b r", b=2))
         table = [placed("table%d" % a, [P, T], I32, AT_TABLE[a]) for a in range(2)]
 
         def load_table(a, cols):
             words = tab_words[a].rearrange("p t i -> p (t i)").bitcast(I32)
             nc.sync.dma_start(out=table[a][:, cols], in_=words[:, cols])
-
-        load_table(0, slice(0, TABLE_HEAD))
 
         table_scales = placed("table_scales", [P, T], U8, AT_TABLE_SCALES)
         nc.vector.memset(table_scales[:].bitcast(I32), 0)
@@ -112,13 +107,15 @@ def tile_list_electrode_node_currents_kernel(
             nc.sync.dma_start(out=table_scales[4 + a : P : 8, :].bitcast(I32), in_=tab_scales[a].bitcast(I32))
         for a in range(2):
             nc.sync.dma_start(out=wc_rows[4 + a : P : 8, :].bitcast(I32), in_=wc_scales[a].bitcast(I32))
+        i0_rows = held("i0_rows", [2, W], F32)
+        nc.sync.dma_start(out=i0_rows[:], in_=i0.rearrange("(b r) -> b r", b=2))
 
         def load_scale_rows(planes, src):
             src_by_e = src.rearrange("a (g e) n -> e g a n", e=4).bitcast(I32)
             for e in range(4):
                 nc.sync.dma_start(out=planes[e:P:32, :, :].bitcast(I32), in_=src_by_e[e])
 
-        load_table(0, slice(TABLE_HEAD, T))
+        load_table(0, slice(0, T))
         wd_sc = held("wd_sc", [P, 2, N], U8)
         nc.vector.memset(wd_sc[:].bitcast(I32), 0)
 
@@ -170,18 +167,25 @@ def tile_list_electrode_node_currents_kernel(
 
         v_codes = {}
 
-        def gather_words(a, j, into):
-            nc.vector.tensor_copy(
-                into[:], table[a][:].bitcast(U32).indirect(offsets[:, j * W // 16 : (j + 1) * W // 16])
-            )
-            v_codes[(a, j)] = into
+        for a in range(2):
+            for j in range(HALVES):
+                v_codes[(a, j)] = held("v_codes%d%d" % (a, j), [P, W], U32)
+        quarter = W // 2
 
-        gather_words(0, 0, held("v_codes00", [P, W], U32))
+        def gather_words(a, j, at, width):
+            first = j * W + at
+            nc.vector.tensor_copy(
+                v_codes[(a, j)][:, at : at + width],
+                table[a][:].bitcast(U32).indirect(offsets[:, first // 16 : (first + width) // 16]),
+            )
+
+        gather_words(0, 0, 0, W)
         ln_i0 = held("ln_i0", [P, 8], F32)
         nc.vector.tensor_tensor(ln_i0[:], ln_mantissa[:], ln_power[:], ALU.add)
-        gather_words(0, 1, held("v_codes01", [P, W], U32))
-        for j in range(HALVES):
-            gather_words(1, j, held("v_codes1%d" % j, [P, W], U32))
+        gather_words(0, 1, 0, W)
+        for at in (0, quarter):
+            gather_words(1, 0, at, quarter)
+        gather_words(1, 1, 0, W)
 
         wa_raw = {}
 
@@ -259,7 +263,14 @@ def tile_list_electrode_node_currents_kernel(
                     else:
                         rates[(kind, b, j)] = held(name, [P, 4, W], F32)
 
-        def exponent_pass(kind, b, j, t, a, opens):
+        def exponent_sum(kind, b, j, t, at, width):
+            group = GROUP_BANKS[(kind, b, j)]
+            if (kind, b, j) == ("c", 0, 0):
+                bank_at = quarter * (t % 2)
+                return banks[group[2 * (at // quarter) + t // 2]][:, bank_at : bank_at + width]
+            return banks[group[t]][:, at : at + width]
+
+        def exponent_pass(kind, b, j, t, a, at, width, opens, closes):
             if kind == "a":
                 lhs = wa_codes[(a, b)][:, P * t : P * (t + 1)].bitcast(FP8X4)
                 lhs_sc = wa_sc[(a, b)][:, P * t : P * (t + 1)]
@@ -267,25 +278,25 @@ def tile_list_electrode_node_currents_kernel(
                 lhs = wc_codes[b][:, a, t, :].bitcast(FP4X4)
                 lhs_sc = planes[a][:, S + W * b + P * t : S + W * b + P * (t + 1)]
             nc.tensor.matmul_mx(
-                out=banks[GROUP_BANKS[(kind, b, j)][t]][:],
+                out=exponent_sum(kind, b, j, t, at, width),
                 lhsT=lhs,
                 lhsT_scale=lhs_sc,
-                rhs=v_codes[(a, j)][:].bitcast(FP8X4),
-                rhs_scale=planes[a][:, j * W : (j + 1) * W],
+                rhs=v_codes[(a, j)][:, at : at + width].bitcast(FP8X4),
+                rhs_scale=planes[a][:, j * W + at : j * W + at + width],
                 start=opens,
-                stop=not opens,
+                stop=closes,
             )
 
         def exponents(kind, b, j, passes, opening=0):
             for t in range(4):
                 for a in passes:
-                    exponent_pass(kind, b, j, t, a, a == opening)
+                    exponent_pass(kind, b, j, t, a, 0, W, a == opening, a != opening)
 
         def exponentials(kind, b, j, slots, at, width):
             for t in slots:
                 nc.scalar.activation(
                     rates[(kind, b, j)][:, t, at : at + width],
-                    banks[GROUP_BANKS[(kind, b, j)][t]][:, at : at + width],
+                    exponent_sum(kind, b, j, t, at, width),
                     ACT.Exp,
                     bias=ln_i0[:, 4 * b + t : 4 * b + t + 1],
                 )
@@ -381,24 +392,31 @@ def tile_list_electrode_node_currents_kernel(
 
         def finish(s):
             first_col, width, places = SPANS[s]
-            cols = slice(first_col, first_col + width)
             result = held("result%d" % s, [P, 2, width], F32)
             for c in range(2):
-                if c == 1 and s == len(SPANS) - 1:
-                    nc.vector.tensor_scalar(result[:, c, :], span_sum(s, c), bo_sb[:, c : c + 1], None, ALU.add)
-                else:
-                    nc.scalar.activation(result[:, c, :], span_sum(s, c), ACT.Identity, bias=bo_sb[:, c : c + 1])
-                if width > P:
-                    nc.sync.dma_start(out=out_by_c[:, c, cols], in_=result[:, c, :])
-            if width == P:
-                nc.sync.dma_start(out=out_by_c[:, :, cols], in_=result[:])
+                nc.scalar.activation(result[:, c, :], span_sum(s, c), ACT.Identity, bias=bo_sb[:, c : c + 1])
+                nc.sync.dma_start(out=out_by_c[:, c, first_col : first_col + width], in_=result[:, c, :])
 
-        quarter = W // 2
+        def finish_last():
+            first_col = SPANS[3][0]
+            for c in range(2):
+                result = held("last_result%d" % c, [P, 2 * P], F32)
+                for s in (3, 4):
+                    into = result[:, P * (s - 3) : P * (s - 2)]
+                    if c == 0:
+                        nc.scalar.activation(into, span_sum(s, c), ACT.Identity, bias=bo_sb[:, c : c + 1])
+                    else:
+                        nc.vector.tensor_scalar(into, span_sum(s, c), bo_sb[:, c : c + 1], None, ALU.add)
+                nc.sync.dma_start(out=out_by_c[:, c, first_col:S], in_=result[:])
+
         for a in range(2):
-            for j in range(HALVES):
-                exponents("c", 0, j, (a,))
-        for j in range(HALVES):
-            exponentials("c", 0, j, range(4), 0, W)
+            for at in (0, quarter):
+                for t in range(4):
+                    exponent_pass("c", 0, 0, t, a, at, quarter, a == 0 and t % 2 == 0, a == 1 and t % 2 == 1)
+            exponents("c", 0, 1, (a,))
+        for at in (0, quarter):
+            exponentials("c", 0, 0, range(4), at, quarter)
+        exponentials("c", 0, 1, range(4), 0, W)
         stage_wa(0, 0, range(4), held("wa_bf00", [P, W, 4], BF16))
         for slots in (range(0, 2), range(2, 4)):
             round_wa_on_vector(0, 0, slots)
@@ -412,8 +430,9 @@ def tile_list_electrode_node_currents_kernel(
         quantise_wa(1, 0, range(3, 4))
         exponents("a", 0, 0, (0,))
         exponents("a", 0, 0, (1,))
+        exponentials("a", 0, 0, range(0, 2), 0, W)
         for at in (0, quarter):
-            exponentials("a", 0, 0, range(4), at, quarter)
+            exponentials("a", 0, 0, range(2, 4), at, quarter)
         for b in range(2):
             round_w2(b)
         order_wc(1)
@@ -427,7 +446,7 @@ def tile_list_electrode_node_currents_kernel(
             round_wa_on_vector(0, 1, slots)
         quantise_h(0, 0, W)
         rate_tiles("c", 1, 0)
-        low_slots, high_slots = range(0, 2), range(2, 4)
+        low_slots, high_slots = range(0, 1), range(1, 4)
         stage_wa(1, 1, range(4), held("wa_bf11", [P, W, 4], BF16))
         round_wa_on_vector(1, 1, low_slots)
         round_wa_on_scalar(1, 1, high_slots)
@@ -441,25 +460,35 @@ def tile_list_electrode_node_currents_kernel(
             net_rate(0, W + at, quarter)
         for at in (0, quarter):
             quantise_h(0, W + at, quarter)
-        rate_tiles("c", 1, 1)
-        for s in range(2):
-            leak(s)
+        exponents("c", 1, 1, (0, 1))
+        exponentials("c", 1, 1, range(0, 2), 0, W)
+        exponents("a", 1, 0, (0, 1))
+        for at in (0, quarter):
+            exponentials("a", 1, 0, range(4), at, quarter)
+        exponentials("c", 1, 1, range(2, 4), 0, W)
+        exponents("a", 1, 1, (0, 1))
+        for at in range(0, W, P):
+            exponentials("a", 1, 1, range(4), at, P)
         h_bf[(1, 0)] = held("h_bf10", [P, W, 4], BF16)
         h_bf[(1, W)] = held("h_bf11", [P, W, 4], BF16)
-        for j in range(HALVES):
-            exponents("a", 1, j, (0, 1))
-            for first_col, width, places in SPANS:
-                if first_col // W == j:
-                    exponentials("a", 1, j, range(4), first_col % W, width)
-        net_rate(1, SPANS[0][0], SPANS[0][1])
         for s in range(2):
+            leak(s)
             collect(0, s)
-        for s, (first_col, width, places) in enumerate(SPANS):
-            if s + 2 < len(SPANS):
-                leak(s + 2)
-                collect(0, s + 2)
-            if s + 1 < len(SPANS):
-                net_rate(1, SPANS[s + 1][0], SPANS[s + 1][1])
-            quantise_h(1, first_col, width)
+            net_rate(1, s * quarter, quarter)
+        for s in range(2):
+            quantise_h(1, s * quarter, quarter)
             collect(1, s)
+        for s in range(2, len(SPANS)):
+            leak(s)
+            collect(0, s)
+        for at in range(W, W + 3 * P, P):
+            net_rate(1, at, P)
+        quantise_h(1, W, quarter)
+        net_rate(1, W + 3 * P, P)
+        for s in range(3, len(SPANS)):
+            quantise_h(1, SPANS[s][0], P)
+        for s in range(2, len(SPANS)):
+            collect(1, s)
+        for s in range(3):
             finish(s)
+        finish_last()

@@ -27,8 +27,8 @@ AT_TABLE = (0, 16 * KB)
 AT_WA = {
     (0, 0): 36 * KB,
     (1, 0): 44 * KB,
-    (0, 1): 0,
-    (1, 1): 16 * KB,
+    (1, 1): 0,
+    (0, 1): 16 * KB,
 }
 AT_W2 = (8 * KB, 12 * KB)
 AT_TABLE_SCALES = 32 * KB
@@ -40,9 +40,9 @@ TABLE_LEAD = T // 4
 SPANS = (
     (0, 256, ((2, 0), (2, 256))),
     (256, 256, ((3, 0), (3, 256))),
-    (512, 256, ((6, 0), (6, 256))),
-    (768, 128, ((7, 0), (0, 0))),
-    (896, 128, ((4, 0), (5, 0))),
+    (512, 256, ((0, 0), (0, 256))),
+    (768, 128, ((1, 0), (4, 0))),
+    (896, 128, ((5, 0), (6, 0))),
 )
 GROUP_BANKS = {
     ("c", 0, 0): (0, 1, 2, 3),
@@ -50,9 +50,9 @@ GROUP_BANKS = {
     ("a", 0, 0): (0, 1, 2, 3),
     ("a", 0, 1): (4, 5, 6, 7),
     ("c", 1, 0): (0, 1, 2, 3),
-    ("c", 1, 1): (4, 5, 6, 7),
+    ("c", 1, 1): (4, 5, 0, 1),
     ("a", 1, 0): (0, 1, 2, 3),
-    ("a", 1, 1): (4, 5, 0, 1),
+    ("a", 1, 1): (4, 5, 6, 7),
 }
 
 
@@ -208,8 +208,8 @@ def tile_list_electrode_node_currents_kernel(
         for b in range(2):
             load_w2(b)
         load_wc(1)
-        load_wa(0, 1)
         load_wa(1, 1)
+        load_wa(0, 1)
         wd_codes = held("wd_codes", [P, 2, N], I32)
         nc.sync.dma_start(out=wd_codes[:], in_=wd_words.rearrange("a p c i -> p a (c i)").bitcast(I32))
         load_scale_rows(wd_sc, wd_scales)
@@ -258,10 +258,7 @@ def tile_list_electrode_node_currents_kernel(
             for b in range(2):
                 for j in range(HALVES):
                     name = "rate_%s%d%d" % (kind, b, j)
-                    if (kind, b, j) == ("c", 1, 1):
-                        rates[(kind, b, j)] = placed(name, [P, 4, W], F32, AT_WA[(1, 1)] + 4 * KB)
-                    else:
-                        rates[(kind, b, j)] = held(name, [P, 4, W], F32)
+                    rates[(kind, b, j)] = held(name, [P, 4, W], F32)
 
         def exponent_sum(kind, b, j, t, at, width):
             group = GROUP_BANKS[(kind, b, j)]
@@ -287,8 +284,8 @@ def tile_list_electrode_node_currents_kernel(
                 stop=closes,
             )
 
-        def exponents(kind, b, j, passes, opening=0):
-            for t in range(4):
+        def exponents(kind, b, j, passes, opening=0, slots=range(4)):
+            for t in slots:
                 for a in passes:
                     exponent_pass(kind, b, j, t, a, 0, W, a == opening, a != opening)
 
@@ -441,32 +438,33 @@ def tile_list_electrode_node_currents_kernel(
         h_bf[(0, 0)] = placed("h_bf00", [P, W, 4], BF16, AT_W2[1])
         for at in (0, quarter):
             net_rate(0, at, quarter)
-        stage_wa(0, 1, range(4), held("wa_bf01", [P, W, 4], BF16))
-        for slots in (range(0, 2), range(2, 4)):
-            round_wa_on_vector(0, 1, slots)
-        quantise_h(0, 0, W)
-        rate_tiles("c", 1, 0)
-        low_slots, high_slots = range(0, 1), range(1, 4)
+        low_slots, high_slots = range(0, 2), range(2, 4)
         stage_wa(1, 1, range(4), held("wa_bf11", [P, W, 4], BF16))
         round_wa_on_vector(1, 1, low_slots)
         round_wa_on_scalar(1, 1, high_slots)
-        for slots in (range(0, 2), range(2, 4)):
-            quantise_wa(0, 1, slots)
+        quantise_h(0, 0, W)
+        rate_tiles("c", 1, 0)
+        quantise_wa(1, 1, low_slots)
         quantise_w2()
+        quantise_wa(1, 1, high_slots)
+        stage_wa(0, 1, range(4), held("wa_bf01", [P, W, 4], BF16))
         for slots in (low_slots, high_slots):
-            quantise_wa(1, 1, slots)
-        h_bf[(0, W)] = placed("h_bf01", [P, W, 4], BF16, AT_WA[(1, 1)])
+            round_wa_on_vector(0, 1, slots)
+        for slots in (low_slots, high_slots):
+            quantise_wa(0, 1, slots)
+        h_bf[(0, W)] = placed("h_bf01", [P, W, 4], BF16, AT_WA[(0, 1)])
         for at in (0, quarter):
             net_rate(0, W + at, quarter)
         for at in (0, quarter):
             quantise_h(0, W + at, quarter)
-        exponents("c", 1, 1, (0, 1))
+        exponents("c", 1, 1, (0, 1), slots=range(0, 2))
         exponentials("c", 1, 1, range(0, 2), 0, W)
-        exponents("a", 1, 0, (0, 1))
+        exponents("a", 1, 0, (1, 0), opening=1)
         for at in (0, quarter):
             exponentials("a", 1, 0, range(4), at, quarter)
+        exponents("c", 1, 1, (0, 1), slots=range(2, 4))
         exponentials("c", 1, 1, range(2, 4), 0, W)
-        exponents("a", 1, 1, (0, 1))
+        exponents("a", 1, 1, (1, 0), opening=1)
         for at in range(0, W, P):
             exponentials("a", 1, 1, range(4), at, P)
         h_bf[(1, 0)] = held("h_bf10", [P, W, 4], BF16)

@@ -258,7 +258,10 @@ def tile_list_electrode_node_currents_kernel(
             for b in range(2):
                 for j in range(HALVES):
                     name = "rate_%s%d%d" % (kind, b, j)
-                    rates[(kind, b, j)] = held(name, [P, 4, W], F32)
+                    if (kind, b, j) == ("c", 1, 0):
+                        rates[(kind, b, j)] = placed(name, [P, 4, W], F32, AT_WA[(1, 1)])
+                    else:
+                        rates[(kind, b, j)] = held(name, [P, 4, W], F32)
 
         def exponent_sum(kind, b, j, t, at, width):
             group = GROUP_BANKS[(kind, b, j)]
@@ -440,17 +443,17 @@ def tile_list_electrode_node_currents_kernel(
             net_rate(0, at, quarter)
         low_slots, high_slots = range(0, 2), range(2, 4)
         stage_wa(1, 1, range(4), held("wa_bf11", [P, W, 4], BF16))
-        round_wa_on_vector(1, 1, low_slots)
-        round_wa_on_scalar(1, 1, high_slots)
+        for slots in (low_slots, high_slots):
+            round_wa_on_scalar(1, 1, slots)
+        quantise_w2()
         quantise_h(0, 0, W)
         rate_tiles("c", 1, 0)
-        quantise_wa(1, 1, low_slots)
-        quantise_w2()
-        quantise_wa(1, 1, high_slots)
+        for slots in (low_slots, high_slots):
+            quantise_wa(1, 1, slots)
         stage_wa(0, 1, range(4), held("wa_bf01", [P, W, 4], BF16))
-        for slots in (low_slots, high_slots):
+        for slots in (range(0, 2), range(2, 4)):
             round_wa_on_vector(0, 1, slots)
-        for slots in (low_slots, high_slots):
+        for slots in (range(0, 2), range(2, 4)):
             quantise_wa(0, 1, slots)
         h_bf[(0, W)] = placed("h_bf01", [P, W, 4], BF16, AT_WA[(0, 1)])
         for at in (0, quarter):
@@ -460,13 +463,14 @@ def tile_list_electrode_node_currents_kernel(
         exponents("c", 1, 1, (0, 1), slots=range(0, 2))
         exponentials("c", 1, 1, range(0, 2), 0, W)
         exponents("a", 1, 0, (1, 0), opening=1)
+        exponentials("a", 1, 0, range(0, 2), 0, W)
         for at in (0, quarter):
-            exponentials("a", 1, 0, range(4), at, quarter)
+            exponentials("a", 1, 0, range(2, 4), at, quarter)
         exponents("c", 1, 1, (0, 1), slots=range(2, 4))
         exponentials("c", 1, 1, range(2, 4), 0, W)
         exponents("a", 1, 1, (1, 0), opening=1)
-        for at in range(0, W, P):
-            exponentials("a", 1, 1, range(4), at, P)
+        for first_col, width, places in SPANS[2:]:
+            exponentials("a", 1, 1, range(4), first_col - W, width)
         h_bf[(1, 0)] = held("h_bf10", [P, W, 4], BF16)
         h_bf[(1, W)] = held("h_bf11", [P, W, 4], BF16)
         for s in range(2):
@@ -479,8 +483,8 @@ def tile_list_electrode_node_currents_kernel(
         for s in range(2, len(SPANS)):
             leak(s)
             collect(0, s)
-        for at in range(W, W + 3 * P, P):
-            net_rate(1, at, P)
+        for first_col, width, places in SPANS[2:4]:
+            net_rate(1, first_col, width)
         quantise_h(1, W, quarter)
         net_rate(1, W + 3 * P, P)
         for s in range(3, len(SPANS)):

@@ -38,11 +38,11 @@ AT_STAGED = 52 * KB
 TABLE_LEAD = T // 4
 
 SPANS = (
-    (0, 256, ((2, 0), (2, 256))),
-    (256, 256, ((3, 0), (3, 256))),
+    (0, 256, ((6, 0), (6, 256))),
+    (256, 256, ((7, 0), (7, 256))),
     (512, 256, ((0, 0), (0, 256))),
     (768, 128, ((1, 0), (4, 0))),
-    (896, 128, ((5, 0), (6, 0))),
+    (896, 128, ((5, 0), (2, 0))),
 )
 GROUP_BANKS = {
     ("c", 0, 0): (0, 1, 2, 3),
@@ -52,7 +52,7 @@ GROUP_BANKS = {
     ("c", 1, 0): (0, 1, 2, 3),
     ("c", 1, 1): (4, 5, 0, 1),
     ("a", 1, 0): (0, 1, 2, 3),
-    ("a", 1, 1): (4, 5, 6, 7),
+    ("a", 1, 1): (4, 5, 2, 3),
 }
 
 
@@ -325,7 +325,7 @@ def tile_list_electrode_node_currents_kernel(
                         lhsT_scale=wd_sc[:, a, P * c : P * (c + 1)],
                         rhs=v_codes[(a, j)][:, at : at + width].bitcast(FP8X4),
                         rhs_scale=planes[a][:, first_col : first_col + width],
-                        start=(a == 0 and (c == 0 or not shares_bank(s))),
+                        start=False,
                         stop=False,
                     )
 
@@ -384,7 +384,7 @@ def tile_list_electrode_node_currents_kernel(
                     lhsT_scale=w2_sc[:, rows],
                     rhs=h_codes[b][:, cols].bitcast(FP8X4),
                     rhs_scale=h_sc[b][:, cols],
-                    start=False,
+                    start=(b == 0 and (c == 0 or not shares_bank(s))),
                     stop=(b == 1 and (c == 1 or not shares_bank(s))),
                 )
 
@@ -430,9 +430,7 @@ def tile_list_electrode_node_currents_kernel(
         quantise_wa(1, 0, range(3, 4))
         exponents("a", 0, 0, (0,))
         exponents("a", 0, 0, (1,))
-        exponentials("a", 0, 0, range(0, 2), 0, W)
-        for at in (0, quarter):
-            exponentials("a", 0, 0, range(2, 4), at, quarter)
+        exponentials("a", 0, 0, range(4), 0, W)
         for b in range(2):
             round_w2(b)
         order_wc(1)
@@ -458,8 +456,7 @@ def tile_list_electrode_node_currents_kernel(
         h_bf[(0, W)] = placed("h_bf01", [P, W, 4], BF16, AT_WA[(0, 1)])
         for at in (0, quarter):
             net_rate(0, W + at, quarter)
-        for at in (0, quarter):
-            quantise_h(0, W + at, quarter)
+        quantise_h(0, W, quarter)
         exponents("c", 1, 1, (0, 1), slots=range(0, 2))
         exponentials("c", 1, 1, range(0, 2), 0, W)
         exponents("a", 1, 0, (1, 0), opening=1)
@@ -469,20 +466,21 @@ def tile_list_electrode_node_currents_kernel(
         exponents("c", 1, 1, (0, 1), slots=range(2, 4))
         exponentials("c", 1, 1, range(2, 4), 0, W)
         exponents("a", 1, 1, (1, 0), opening=1)
-        for first_col, width, places in SPANS[2:]:
-            exponentials("a", 1, 1, range(4), first_col - W, width)
+        for at in (0, quarter):
+            exponentials("a", 1, 1, range(4), at, quarter)
         h_bf[(1, 0)] = held("h_bf10", [P, W, 4], BF16)
         h_bf[(1, W)] = held("h_bf11", [P, W, 4], BF16)
         for s in range(2):
-            leak(s)
             collect(0, s)
+            leak(s)
             net_rate(1, s * quarter, quarter)
         for s in range(2):
             quantise_h(1, s * quarter, quarter)
             collect(1, s)
+        quantise_h(0, W + quarter, quarter)
         for s in range(2, len(SPANS)):
-            leak(s)
             collect(0, s)
+            leak(s)
         for first_col, width, places in SPANS[2:4]:
             net_rate(1, first_col, width)
         quantise_h(1, W, quarter)

@@ -34,6 +34,7 @@ AT_W2 = (8 * KB, 12 * KB)
 AT_TABLE_SCALES = 32 * KB
 AT_PLANES = (32 * KB, 34 * KB)
 AT_STAGED = 52 * KB
+AT_SIGNS = 54 * KB
 
 TABLE_LEAD = T // 4
 
@@ -84,10 +85,10 @@ def tile_list_electrode_node_currents_kernel(
             words = wc_words.rearrange("a p x -> p a x")[:, :, 2 * W * b : 2 * W * (b + 1)]
             nc.sync.dma_start(out=wc_raw[b][:].bitcast(I32), in_=words.bitcast(I32))
 
-        def order_wc(b):
-            nc.vector.tensor_copy(
-                out=wc_codes[b][:].bitcast(I32).rearrange("p a t (m e) -> p a t m e", e=2),
-                in_=wc_raw[b][:].bitcast(I32).rearrange("p a (m t e) -> p a t m e", t=4, e=2),
+        def order_wc(b, copy):
+            copy(
+                wc_codes[b][:].bitcast(U32).rearrange("p a t (m e) -> p a t m e", e=2),
+                wc_raw[b][:].bitcast(U32).rearrange("p a (m t e) -> p a t m e", t=4, e=2),
             )
 
         load_wc(0)
@@ -139,7 +140,7 @@ def tile_list_electrode_node_currents_kernel(
         move_scale_rows(0)
         load_table(1, slice(TABLE_LEAD, T))
         move_scale_rows(1)
-        order_wc(0)
+        order_wc(0, nc.vector.tensor_copy)
 
         nc.vector.tensor_copy(
             out=i0_by_slot[0:2].rearrange("b t (m u) -> b t m u", u=4),
@@ -161,9 +162,9 @@ def tile_list_electrode_node_currents_kernel(
         nc.scalar.activation(ln_mantissa[:], mantissa[:].bitcast(F32), ACT.Ln)
         ln_power = held("ln_power", [P, 8], F32)
         nc.vector.tensor_scalar(ln_power[:], exponent[:], 127.0, math.log(2.0), ALU.subtract, ALU.mult)
-        sign_bits = held("sign_bits", [P, 8], I32)
-        nc.vector.tensor_scalar(sign_bits[:], bits, -0x80000000, 0x3F800000, ALU.bitwise_and, ALU.bitwise_or)
-        i0_sign = sign_bits[:].bitcast(F32)
+        signs = [placed("signs", [P, 8], I32, AT_SIGNS), held("last_signs", [P, 8], I32)]
+        for tile in signs:
+            nc.vector.tensor_scalar(tile[:], bits, -0x80000000, 0x3F800000, ALU.bitwise_and, ALU.bitwise_or)
 
         v_codes = {}
 
@@ -229,26 +230,35 @@ def tile_list_electrode_node_currents_kernel(
             src = wa_raw[(a, b)][:].rearrange("p i (m t u) -> p t m i u", t=4, u=4)
             return dst[:, slots.start - first : slots.stop - first], src[:, slots.start : slots.stop]
 
-        def round_wa_on_vector(a, b, slots):
+        def round_wa_on_vector(a, b, slots, m=slice(0, 32)):
             dst, src = round_views(a, b, slots)
-            nc.vector.tensor_copy(out=dst, in_=src)
+            nc.vector.tensor_copy(out=dst[:, :, m], in_=src[:, :, m])
 
-        def round_wa_on_scalar(a, b, slots):
+        def round_wa_on_scalar(a, b, slots, m=slice(0, 32)):
             dst, src = round_views(a, b, slots)
-            nc.scalar.copy(dst, src)
+            nc.scalar.copy(dst[:, :, m], src[:, :, m])
 
         wa_codes = {}
         wa_sc = {}
         for a in range(2):
             for b in range(2):
-                wa_codes[(a, b)] = held("wa_codes%d%d" % (a, b), [P, W], U32)
+                for half in range(2):
+                    name = "wa_codes%d%d%d" % (a, b, half)
+                    if (a, b, half) == (1, 1, 1):
+                        wa_codes[(a, b, half)] = placed(name, [P, 2 * P], U32, AT_WA[(0, 1)] + 4 * KB)
+                    else:
+                        wa_codes[(a, b, half)] = held(name, [P, 2 * P], U32)
                 wa_sc[(a, b)] = held("wa_sc%d%d" % (a, b), [P, W], U8)
+
+        def wa_words(a, b, slots):
+            half, first = divmod(slots.start, 2)
+            return wa_codes[(a, b, half)][:, P * first : P * (first + len(slots))].bitcast(FP8X4)
 
         def quantise_wa(a, b, slots):
             tile, first = wa_bf[(a, b, slots.start)]
             cols = slice(P * slots.start, P * slots.stop)
             nc.vector.quantize_mx(
-                out=wa_codes[(a, b)][:, cols].bitcast(FP8X4),
+                out=wa_words(a, b, slots),
                 scales=wa_sc[(a, b)][:, cols],
                 in_=tile[:, P * (slots.start - first) : P * (slots.stop - first), :].rearrange("p c i -> p (c i)"),
             )
@@ -272,7 +282,7 @@ def tile_list_electrode_node_currents_kernel(
 
         def exponent_pass(kind, b, j, t, a, at, width, opens, closes):
             if kind == "a":
-                lhs = wa_codes[(a, b)][:, P * t : P * (t + 1)].bitcast(FP8X4)
+                lhs = wa_words(a, b, range(t, t + 1))
                 lhs_sc = wa_sc[(a, b)][:, P * t : P * (t + 1)]
             else:
                 lhs = wc_codes[b][:, a, t, :].bitcast(FP4X4)
@@ -358,11 +368,15 @@ def tile_list_electrode_node_currents_kernel(
         w2_codes = held("w2_codes", [P, 2 * N], U32)
         w2_sc = held("w2_sc", [P, 2 * N], U8)
 
-        def round_w2(b):
+        def round_w2(b, cols, sign_bits):
             nc.vector.tensor_tensor(
-                w2_bf[:, b, :, :].rearrange("p (c x) t -> p c t x", x=4),
-                w2_raw[b][:].rearrange("p t (c x) -> p c t x", x=4),
-                i0_sign[:, 4 * b : 4 * b + 4].unsqueeze(1).unsqueeze(3).to_broadcast([P, N // 4, 4, 4]),
+                w2_bf[:, b, cols, :].rearrange("p (c x) t -> p c t x", x=4),
+                w2_raw[b][:, :, cols].rearrange("p t (c x) -> p c t x", x=4),
+                sign_bits[:, 4 * b : 4 * b + 4]
+                .bitcast(F32)
+                .unsqueeze(1)
+                .unsqueeze(3)
+                .to_broadcast([P, (cols.stop - cols.start) // 4, 4, 4]),
                 ALU.mult,
             )
 
@@ -403,7 +417,7 @@ def tile_list_electrode_node_currents_kernel(
                 result = held("last_result%d" % c, [P, 2 * P], F32)
                 for s in (3, 4):
                     into = result[:, P * (s - 3) : P * (s - 2)]
-                    if c == 0:
+                    if (s, c) == (4, 0):
                         nc.scalar.activation(into, span_sum(s, c), ACT.Identity, bias=bo_sb[:, c : c + 1])
                     else:
                         nc.vector.tensor_scalar(into, span_sum(s, c), bo_sb[:, c : c + 1], None, ALU.add)
@@ -430,29 +444,33 @@ def tile_list_electrode_node_currents_kernel(
         quantise_wa(1, 0, range(3, 4))
         exponents("a", 0, 0, (0,))
         exponents("a", 0, 0, (1,))
-        exponentials("a", 0, 0, range(4), 0, W)
-        for b in range(2):
-            round_w2(b)
-        order_wc(1)
+        exponentials("a", 0, 0, range(0, 2), 0, W)
+        for at in (0, quarter):
+            exponentials("a", 0, 0, range(2, 4), at, quarter)
+        round_w2(0, slice(0, N), signs[0])
+        for c in range(2):
+            round_w2(1, slice(P * c, P * (c + 1)), signs[c])
+        order_wc(1, nc.vector.tensor_copy)
         exponents("a", 0, 1, (1, 0), opening=1)
         exponentials("a", 0, 1, range(4), 0, W)
-        h_bf[(0, 0)] = placed("h_bf00", [P, W, 4], BF16, AT_W2[1])
+        h_bf[(0, 0)] = placed("h_bf00", [P, W, 4], BF16, AT_SIGNS)
         for at in (0, quarter):
             net_rate(0, at, quarter)
         low_slots, high_slots = range(0, 2), range(2, 4)
         stage_wa(1, 1, range(4), held("wa_bf11", [P, W, 4], BF16))
-        for slots in (low_slots, high_slots):
-            round_wa_on_scalar(1, 1, slots)
+        round_wa_on_scalar(1, 1, low_slots)
+        round_wa_on_scalar(1, 1, high_slots, slice(0, 24))
+        round_wa_on_vector(1, 1, high_slots, slice(24, 32))
         quantise_w2()
         quantise_h(0, 0, W)
         rate_tiles("c", 1, 0)
-        for slots in (low_slots, high_slots):
-            quantise_wa(1, 1, slots)
+        quantise_wa(1, 1, low_slots)
         stage_wa(0, 1, range(4), held("wa_bf01", [P, W, 4], BF16))
         for slots in (range(0, 2), range(2, 4)):
             round_wa_on_vector(0, 1, slots)
-        for slots in (range(0, 2), range(2, 4)):
-            quantise_wa(0, 1, slots)
+        quantise_wa(0, 1, low_slots)
+        quantise_wa(1, 1, high_slots)
+        quantise_wa(0, 1, high_slots)
         h_bf[(0, W)] = placed("h_bf01", [P, W, 4], BF16, AT_WA[(0, 1)])
         for at in (0, quarter):
             net_rate(0, W + at, quarter)

import math
from contextlib import ExitStack

import concourse.mybir as mybir
from concourse.masks import make_identity

K, T, S, H, N = 1024, 4096, 1024, 1024, 256
FLOPS = 2 * S * (2 * K * H + H * N + K * N)

F32 = mybir.dt.float32
BF16 = mybir.dt.bfloat16
I32 = mybir.dt.int32
U32 = mybir.dt.uint32
U16 = mybir.dt.uint16
U8 = mybir.dt.uint8
FP8X4 = mybir.dt.float8_e4m3fn_x4
FP4X4 = mybir.dt.float4_e2m1fn_x4
ALU = mybir.AluOpType
ACT = mybir.ActivationFunctionType

P = 128
W = 512
HALVES = S // W
KB = 1024

AT_TABLE = (0, 16 * KB)
AT_WA = {
    (0, 0): 36 * KB,
    (1, 0): 44 * KB,
    (1, 1): 0,
    (0, 1): 16 * KB,
}
AT_W2 = (8 * KB, 12 * KB)
AT_TABLE_SCALES = 32 * KB
AT_PLANES = (32 * KB, 34 * KB)
AT_STAGED = 52 * KB
AT_SIGNS = 54 * KB

TABLE_LEAD = T // 4

SPANS = (
    (0, 256, ((6, 0), (6, 256))),
    (256, 256, ((7, 0), (7, 256))),
    (512, 256, ((0, 0), (0, 256))),
    (768, 128, ((1, 0), (4, 0))),
    (896, 128, ((5, 0), (2, 0))),
)
GROUP_BANKS = {
    ("c", 0, 0): (0, 1, 2, 3),
    ("c", 0, 1): (4, 5, 6, 7),
    ("a", 0, 0): (0, 1, 2, 3),
    ("a", 0, 1): (4, 5, 6, 7),
    ("c", 1, 0): (0, 1, 2, 3),
    ("c", 1, 1): (4, 5, 0, 1),
    ("a", 1, 0): (0, 1, 2, 3),
    ("a", 1, 1): (4, 5, 2, 3),
}


def tile_list_electrode_node_currents_kernel(
    tc, tab_words, tab_scales, offs, wa, wc_words, wc_scales, wd_words, wd_scales, i0, w2, bo, out
):
    nc = tc.nc
    with ExitStack() as ctx:
        keep = ctx.enter_context(tc.tile_pool(name="keep", bufs=1))
        reuse = ctx.enter_context(tc.tile_pool(name="reuse", bufs=1))
        psum = ctx.enter_context(tc.psum_pool(name="psum", bufs=1))
        banks = [psum.tile([P, W], F32, name="bank%d" % n) for n in range(8)]

        def held(name, shape, dtype):
            return keep.tile(shape, dtype, name=name, align_bytes=256)

        def placed(name, shape, dtype, at):
            return reuse.tile(shape, dtype, name=name, align_bytes=256, offset=at)

        offsets = keep.tile([P, S // 16], U16, name="offsets")
        nc.sync.dma_start(offsets[:], offs)

        identity = held("identity", [P, P], F32)
        make_identity(nc, identity[:])
        wc_raw = [held("wc_raw%d" % b, [P, 2, 2 * W], U8) for b in range(2)]
        wc_codes = [held("wc_codes%d" % b, [P, 2, 4, 256], U8) for b in range(2)]

        def load_wc(b):
            words = wc_words.rearrange("a p x -> p a x")[:, :, 2 * W * b : 2 * W * (b + 1)]
            nc.sync.dma_start(out=wc_raw[b][:].bitcast(I32), in_=words.bitcast(I32))

        def order_wc(b, copy):
            copy(
                wc_codes[b][:].bitcast(U32).rearrange("p a t (m e) -> p a t m e", e=2),
                wc_raw[b][:].bitcast(U32).rearrange("p a (m t e) -> p a t m e", t=4, e=2),
            )

        load_wc(0)
        table = [placed("table%d" % a, [P, T], I32, AT_TABLE[a]) for a in range(2)]

        def load_table(a, cols):
            words = tab_words[a].rearrange("p t i -> p (t i)").bitcast(I32)
            nc.sync.dma_start(out=table[a][:, cols], in_=words[:, cols])

        table_scales = placed("table_scales", [P, T], U8, AT_TABLE_SCALES)
        nc.vector.memset(table_scales[:].bitcast(I32), 0)
        wc_rows = held("wc_rows", [P, H], U8)
        nc.vector.memset(wc_rows[:].bitcast(I32), 0)
        i0_by_slot = held("i0_by_slot", [P, 4, P], F32)
        nc.vector.memset(i0_by_slot[:], 0.0)
        for a in range(2):
            nc.sync.dma_start(out=table_scales[4 + a : P : 8, :].bitcast(I32), in_=tab_scales[a].bitcast(I32))
        for a in range(2):
            nc.sync.dma_start(out=wc_rows[4 + a : P : 8, :].bitcast(I32), in_=wc_scales[a].bitcast(I32))
        i0_rows = held("i0_rows", [2, W], F32)
        nc.sync.dma_start(out=i0_rows[:], in_=i0.rearrange("(b r) -> b r", b=2))

        def load_scale_rows(planes, src):
            src_by_e = src.rearrange("a (g e) n -> e g a n", e=4).bitcast(I32)
            for e in range(4):
                nc.sync.dma_start(out=planes[e:P:32, :, :].bitcast(I32), in_=src_by_e[e])

        load_table(0, slice(0, T))
        wd_sc = held("wd_sc", [P, 2, N], U8)
        nc.vector.memset(wd_sc[:].bitcast(I32), 0)

        picked_scales = held("picked_scales", [P, S], U8)
        nc.vector.tensor_copy(picked_scales[:], table_scales[:].indirect(offsets[:]))
        staged = placed("staged", [P, S + H], U8, AT_STAGED)
        nc.vector.tensor_copy(
            out=staged[:, S:].bitcast(I32).rearrange("p (b t m) -> p b t m", b=2, t=4),
            in_=wc_rows[:].bitcast(I32).rearrange("p (b m t) -> p b t m", b=2, t=4),
        )
        nc.vector.tensor_copy(out=staged[:, 0:S].bitcast(I32), in_=picked_scales[:].bitcast(I32))
        planes = [placed("planes%d" % a, [P, S + H], U8, AT_PLANES[a]) for a in range(2)]

        def move_scale_rows(a):
            for e in range(4):
                nc.sync.dma_start(
                    out=planes[a][e:P:32, :].bitcast(I32), in_=staged[8 * e + 4 + a : P : 32, :].bitcast(I32)
                )

        load_table(1, slice(0, TABLE_LEAD))
        move_scale_rows(0)
        load_table(1, slice(TABLE_LEAD, T))
        move_scale_rows(1)
        order_wc(0, nc.vector.tensor_copy)

        nc.vector.tensor_copy(
            out=i0_by_slot[0:2].rearrange("b t (m u) -> b t m u", u=4),
            in_=i0_rows[:].rearrange("b (m t u) -> b t m u", t=4, u=4),
        )
        for t in range(4):
            nc.tensor.transpose(banks[0][:, P * t : P * (t + 1)], i0_by_slot[:, t, :], identity[:])
        i0_sb = held("i0_sb", [P, 8], F32)
        nc.vector.tensor_copy(
            out=i0_sb[:].rearrange("p (b t) -> p b t", b=2),
            in_=banks[0][:].rearrange("p (t b) -> p b t", t=4)[:, 0:2, :],
        )
        bits = i0_sb[:].bitcast(I32)
        mantissa = held("mantissa", [P, 8], I32)
        nc.vector.tensor_scalar(mantissa[:], bits, 0x007FFFFF, 0x3F800000, ALU.bitwise_and, ALU.bitwise_or)
        exponent = held("exponent", [P, 8], I32)
        nc.vector.tensor_scalar(exponent[:], bits, 23, 0xFF, ALU.logical_shift_right, ALU.bitwise_and)
        ln_mantissa = held("ln_mantissa", [P, 8], F32)
        nc.scalar.activation(ln_mantissa[:], mantissa[:].bitcast(F32), ACT.Ln)
        ln_power = held("ln_power", [P, 8], F32)
        nc.vector.tensor_scalar(ln_power[:], exponent[:], 127.0, math.log(2.0), ALU.subtract, ALU.mult)
        signs = [placed("signs", [P, 8], I32, AT_SIGNS), held("last_signs", [P, 8], I32)]
        for tile in signs:
            nc.vector.tensor_scalar(tile[:], bits, -0x80000000, 0x3F800000, ALU.bitwise_and, ALU.bitwise_or)

        v_codes = {}

        for a in range(2):
            for j in range(HALVES):
                v_codes[(a, j)] = held("v_codes%d%d" % (a, j), [P, W], U32)
        quarter = W // 2

        def gather_words(a, j, at, width):
            first = j * W + at
            nc.vector.tensor_copy(
                v_codes[(a, j)][:, at : at + width],
                table[a][:].bitcast(U32).indirect(offsets[:, first // 16 : (first + width) // 16]),
            )

        gather_words(0, 0, 0, W)
        ln_i0 = held("ln_i0", [P, 8], F32)
        nc.vector.tensor_tensor(ln_i0[:], ln_mantissa[:], ln_power[:], ALU.add)
        gather_words(0, 1, 0, W)
        for at in (0, quarter):
            gather_words(1, 0, at, quarter)
        gather_words(1, 1, 0, W)

        wa_raw = {}

        def load_wa(a, b):
            wa_raw[(a, b)] = placed("wa_raw%d%d" % (a, b), [P, 4, W], F32, AT_WA[(a, b)])
            nc.sync.dma_start(
                out=wa_raw[(a, b)][:],
                in_=wa[W * a : W * (a + 1), W * b : W * (b + 1)].rearrange("(p i) c -> p i c", i=4),
            )

        w2_raw = [placed("w2_raw%d" % b, [P, 4, N], F32, AT_W2[b]) for b in range(2)]
        w2_rows = w2.rearrange("(b m t u) n -> b t m u n", b=2, t=4, u=4)

        def load_w2(b):
            for t in range(4):
                nc.sync.dma_start(out=w2_raw[b][:, t, :], in_=w2_rows[b, t])

        load_wa(0, 0)
        load_wa(1, 0)
        for b in range(2):
            load_w2(b)
        load_wc(1)
        load_wa(1, 1)
        load_wa(0, 1)
        wd_codes = held("wd_codes", [P, 2, N], I32)
        nc.sync.dma_start(out=wd_codes[:], in_=wd_words.rearrange("a p c i -> p a (c i)").bitcast(I32))
        load_scale_rows(wd_sc, wd_scales)
        bo_sb = held("bo_sb", [P, 2], F32)
        with nc.allow_non_contiguous_dma(reason="one bias a partition"):
            nc.sync.dma_start(out=bo_sb[:], in_=bo.rearrange("(c p) -> p c", p=P))

        wa_bf = {}

        def stage_wa(a, b, slots, tile):
            for t in slots:
                wa_bf[(a, b, t)] = (tile, slots.start)

        def round_views(a, b, slots):
            tile, first = wa_bf[(a, b, slots.start)]
            dst = tile[:].rearrange("p (t m u) i -> p t m i u", m=32, u=4)
            src = wa_raw[(a, b)][:].rearrange("p i (m t u) -> p t m i u", t=4, u=4)
            return dst[:, slots.start - first : slots.stop - first], src[:, slots.start : slots.stop]

        def round_wa_on_vector(a, b, slots, m=slice(0, 32)):
            dst, src = round_views(a, b, slots)
            nc.vector.tensor_copy(out=dst[:, :, m], in_=src[:, :, m])

        def round_wa_on_scalar(a, b, slots, m=slice(0, 32)):
            dst, src = round_views(a, b, slots)
            nc.scalar.copy(dst[:, :, m], src[:, :, m])

        wa_codes = {}
        wa_sc = {}
        for a in range(2):
            for b in range(2):
                for half in range(2):
                    name = "wa_codes%d%d%d" % (a, b, half)
                    if (a, b, half) == (1, 1, 1):
                        wa_codes[(a, b, half)] = placed(name, [P, 2 * P], U32, AT_WA[(0, 1)] + 4 * KB)
                    else:
                        wa_codes[(a, b, half)] = held(name, [P, 2 * P], U32)
                wa_sc[(a, b)] = held("wa_sc%d%d" % (a, b), [P, W], U8)

        def wa_words(a, b, slots):
            half, first = divmod(slots.start, 2)
            return wa_codes[(a, b, half)][:, P * first : P * (first + len(slots))].bitcast(FP8X4)

        def quantise_wa(a, b, slots):
            tile, first = wa_bf[(a, b, slots.start)]
            cols = slice(P * slots.start, P * slots.stop)
            nc.vector.quantize_mx(
                out=wa_words(a, b, slots),
                scales=wa_sc[(a, b)][:, cols],
                in_=tile[:, P * (slots.start - first) : P * (slots.stop - first), :].rearrange("p c i -> p (c i)"),
            )

        rates = {}
        for kind in "ac":
            for b in range(2):
                for j in range(HALVES):
                    name = "rate_%s%d%d" % (kind, b, j)
                    if (kind, b, j) == ("c", 1, 0):
                        rates[(kind, b, j)] = placed(name, [P, 4, W], F32, AT_WA[(1, 1)])
                    else:
                        rates[(kind, b, j)] = held(name, [P, 4, W], F32)

        def exponent_sum(kind, b, j, t, at, width):
            group = GROUP_BANKS[(kind, b, j)]
            if (kind, b, j) == ("c", 0, 0):
                bank_at = quarter * (t % 2)
                return banks[group[2 * (at // quarter) + t // 2]][:, bank_at : bank_at + width]
            return banks[group[t]][:, at : at + width]

        def exponent_pass(kind, b, j, t, a, at, width, opens, closes):
            if kind == "a":
                lhs = wa_words(a, b, range(t, t + 1))
                lhs_sc = wa_sc[(a, b)][:, P * t : P * (t + 1)]
            else:
                lhs = wc_codes[b][:, a, t, :].bitcast(FP4X4)
                lhs_sc = planes[a][:, S + W * b + P * t : S + W * b + P * (t + 1)]
            nc.tensor.matmul_mx(
                out=exponent_sum(kind, b, j, t, at, width),
                lhsT=lhs,
                lhsT_scale=lhs_sc,
                rhs=v_codes[(a, j)][:, at : at + width].bitcast(FP8X4),
                rhs_scale=planes[a][:, j * W + at : j * W + at + width],
                start=opens,
                stop=closes,
            )

        def exponents(kind, b, j, passes, opening=0, slots=range(4)):
            for t in slots:
                for a in passes:
                    exponent_pass(kind, b, j, t, a, 0, W, a == opening, a != opening)

        def exponentials(kind, b, j, slots, at, width):
            for t in slots:
                nc.scalar.activation(
                    rates[(kind, b, j)][:, t, at : at + width],
                    exponent_sum(kind, b, j, t, at, width),
                    ACT.Exp,
                    bias=ln_i0[:, 4 * b + t : 4 * b + t + 1],
                )

        def rate_tiles(kind, b, j):
            exponents(kind, b, j, (0, 1))
            exponentials(kind, b, j, range(4), 0, W)

        def span_sum(s, c):
            first_col, width, places = SPANS[s]
            bank, at = places[c]
            return banks[bank][:, at : at + width]

        def shares_bank(s):
            places = SPANS[s][2]
            return places[0][0] == places[1][0]

        def leak(s):
            first_col, width, places = SPANS[s]
            j, at = divmod(first_col, W)
            for c in range(2):
                for a in range(2):
                    nc.tensor.matmul_mx(
                        out=span_sum(s, c),
                        lhsT=wd_codes[:, a, P * c : P * (c + 1)].bitcast(FP8X4),
                        lhsT_scale=wd_sc[:, a, P * c : P * (c + 1)],
                        rhs=v_codes[(a, j)][:, at : at + width].bitcast(FP8X4),
                        rhs_scale=planes[a][:, first_col : first_col + width],
                        start=False,
                        stop=False,
                    )

        h_codes = [held("h_codes%d" % b, [P, S], U32) for b in range(2)]
        h_sc = [held("h_sc%d" % b, [P, S], U8) for b in range(2)]
        h_bf = {}

        def h_view(b, first_col, width):
            start = max(c for (bb, c) in h_bf if bb == b and c <= first_col)
            return h_bf[(b, start)][:, first_col - start : first_col - start + width, :]

        def net_rate(b, first_col, width):
            j, at = divmod(first_col, W)
            nc.vector.tensor_tensor(
                h_view(b, first_col, width).rearrange("p (c x) t -> p c t x", x=4),
                rates[("a", b, j)][:, :, at : at + width].rearrange("p t (c x) -> p c t x", x=4),
                rates[("c", b, j)][:, :, at : at + width].rearrange("p t (c x) -> p c t x", x=4),
                ALU.subtract,
            )

        def quantise_h(b, first_col, width):
            cols = slice(first_col, first_col + width)
            nc.vector.quantize_mx(
                out=h_codes[b][:, cols].bitcast(FP8X4),
                scales=h_sc[b][:, cols],
                in_=h_view(b, first_col, width).rearrange("p c t -> p (c t)"),
            )

        w2_bf = held("w2_bf", [P, 2, N, 4], BF16)
        w2_codes = held("w2_codes", [P, 2 * N], U32)
        w2_sc = held("w2_sc", [P, 2 * N], U8)

        def round_w2(b, cols, sign_bits):
            nc.vector.tensor_tensor(
                w2_bf[:, b, cols, :].rearrange("p (c x) t -> p c t x", x=4),
                w2_raw[b][:, :, cols].rearrange("p t (c x) -> p c t x", x=4),
                sign_bits[:, 4 * b : 4 * b + 4]
                .bitcast(F32)
                .unsqueeze(1)
                .unsqueeze(3)
                .to_broadcast([P, (cols.stop - cols.start) // 4, 4, 4]),
                ALU.mult,
            )

        def quantise_w2():
            nc.vector.quantize_mx(
                out=w2_codes[:].bitcast(FP8X4),
                scales=w2_sc[:],
                in_=w2_bf[:].rearrange("p b n t -> p (b n t)"),
            )

        def collect(b, s):
            first_col, width, places = SPANS[s]
            cols = slice(first_col, first_col + width)
            for c in range(2):
                rows = slice(N * b + P * c, N * b + P * (c + 1))
                nc.tensor.matmul_mx(
                    out=span_sum(s, c),
                    lhsT=w2_codes[:, rows].bitcast(FP8X4),
                    lhsT_scale=w2_sc[:, rows],
                    rhs=h_codes[b][:, cols].bitcast(FP8X4),
                    rhs_scale=h_sc[b][:, cols],
                    start=(b == 0 and (c == 0 or not shares_bank(s))),
                    stop=(b == 1 and (c == 1 or not shares_bank(s))),
                )

        out_by_c = out.rearrange("(c p) j -> p c j", p=P)

        def finish(s):
            first_col, width, places = SPANS[s]
            result = held("result%d" % s, [P, 2, width], F32)
            for c in range(2):
                nc.scalar.activation(result[:, c, :], span_sum(s, c), ACT.Identity, bias=bo_sb[:, c : c + 1])
                nc.sync.dma_start(out=out_by_c[:, c, first_col : first_col + width], in_=result[:, c, :])

        def finish_last():
            first_col = SPANS[3][0]
            for c in range(2):
                result = held("last_result%d" % c, [P, 2 * P], F32)
                for s in (3, 4):
                    into = result[:, P * (s - 3) : P * (s - 2)]
                    if (s, c) == (4, 0):
                        nc.scalar.activation(into, span_sum(s, c), ACT.Identity, bias=bo_sb[:, c : c + 1])
                    else:
                        nc.vector.tensor_scalar(into, span_sum(s, c), bo_sb[:, c : c + 1], None, ALU.add)
                nc.sync.dma_start(out=out_by_c[:, c, first_col:S], in_=result[:])

        for a in range(2):
            for at in (0, quarter):
                for t in range(4):
                    exponent_pass("c", 0, 0, t, a, at, quarter, a == 0 and t % 2 == 0, a == 1 and t % 2 == 1)
            exponents("c", 0, 1, (a,))
        for at in (0, quarter):
            exponentials("c", 0, 0, range(4), at, quarter)
        exponentials("c", 0, 1, range(4), 0, W)
        stage_wa(0, 0, range(4), held("wa_bf00", [P, W, 4], BF16))
        for slots in (range(0, 2), range(2, 4)):
            round_wa_on_vector(0, 0, slots)
        for slots in (range(0, 2), range(2, 4)):
            quantise_wa(0, 0, slots)
        stage_wa(1, 0, range(4), held("wa_bf10", [P, W, 4], BF16))
        round_wa_on_vector(1, 0, range(0, 1))
        for t in range(1, 4):
            round_wa_on_vector(1, 0, range(t, t + 1))
            quantise_wa(1, 0, range(t - 1, t))
        quantise_wa(1, 0, range(3, 4))
        exponents("a", 0, 0, (0,))
        exponents("a", 0, 0, (1,))
        exponentials("a", 0, 0, range(0, 2), 0, W)
        for at in (0, quarter):
            exponentials("a", 0, 0, range(2, 4), at, quarter)
        round_w2(0, slice(0, N), signs[0])
        for c in range(2):
            round_w2(1, slice(P * c, P * (c + 1)), signs[c])
        order_wc(1, nc.vector.tensor_copy)
        exponents("a", 0, 1, (1, 0), opening=1)
        exponentials("a", 0, 1, range(4), 0, W)
        h_bf[(0, 0)] = placed("h_bf00", [P, W, 4], BF16, AT_SIGNS)
        for at in (0, quarter):
            net_rate(0, at, quarter)
        low_slots, high_slots = range(0, 2), range(2, 4)
        stage_wa(1, 1, range(4), held("wa_bf11", [P, W, 4], BF16))
        round_wa_on_scalar(1, 1, low_slots)
        round_wa_on_scalar(1, 1, high_slots, slice(0, 24))
        round_wa_on_vector(1, 1, high_slots, slice(24, 32))
        quantise_w2()
        quantise_h(0, 0, W)
        rate_tiles("c", 1, 0)
        quantise_wa(1, 1, low_slots)
        stage_wa(0, 1, range(4), held("wa_bf01", [P, W, 4], BF16))
        for slots in (range(0, 2), range(2, 4)):
            round_wa_on_vector(0, 1, slots)
        quantise_wa(0, 1, low_slots)
        quantise_wa(1, 1, high_slots)
        quantise_wa(0, 1, high_slots)
        h_bf[(0, W)] = placed("h_bf01", [P, W, 4], BF16, AT_WA[(0, 1)])
        for at in (0, quarter):
            net_rate(0, W + at, quarter)
        quantise_h(0, W, quarter)
        exponents("c", 1, 1, (0, 1), slots=range(0, 2))
        exponentials("c", 1, 1, range(0, 2), 0, W)
        exponents("a", 1, 0, (1, 0), opening=1)
        exponentials("a", 1, 0, range(0, 2), 0, W)
        for at in (0, quarter):
            exponentials("a", 1, 0, range(2, 4), at, quarter)
        exponents("c", 1, 1, (0, 1), slots=range(2, 4))
        exponentials("c", 1, 1, range(2, 4), 0, W)
        exponents("a", 1, 1, (1, 0), opening=1)
        for at in (0, quarter):
            exponentials("a", 1, 1, range(4), at, quarter)
        h_bf[(1, 0)] = held("h_bf10", [P, W, 4], BF16)
        h_bf[(1, W)] = held("h_bf11", [P, W, 4], BF16)
        for s in range(2):
            collect(0, s)
            leak(s)
            net_rate(1, s * quarter, quarter)
        for s in range(2):
            quantise_h(1, s * quarter, quarter)
            collect(1, s)
        quantise_h(0, W + quarter, quarter)
        for s in range(2, len(SPANS)):
            collect(0, s)
            leak(s)
        for first_col, width, places in SPANS[2:4]:
            net_rate(1, first_col, width)
        quantise_h(1, W, quarter)
        net_rate(1, W + 3 * P, P)
        for s in range(3, len(SPANS)):
            quantise_h(1, SPANS[s][0], P)
        for s in range(2, len(SPANS)):
            collect(1, s)
        for s in range(3):
            finish(s)
        finish_last()
